import numpy as np, ml_dtypes
CORES = [16,18,20,22]
N = 4
BF = ml_dtypes.bfloat16
def gentries(a):
    return np.ascontiguousarray(a.reshape(8, 16, -1).transpose(0, 2, 1)).reshape(8, -1)
def gtable(e):
    e = np.asarray(e); return np.ascontiguousarray(e.reshape(8, -1, 16).transpose(0, 2, 1)).reshape(128, -1).astype(np.int32)
SO, RO, CR, CL, CF, TR = 512, 1024, 512, 192, 64, 5
S, R = N * SO, N * RO
TH = 24
EPS = np.float32(0.125); UNDER = np.nextafter(EPS, np.float32(0)); LEAST = np.float32(0.00390625)
def expo(rng, lo, hi, *shape):
    return np.exp2(lo + (hi - lo) * rng.random(shape)).astype(np.float32)
def mark(rng, cnt):
    return np.argsort(rng.random((N, 8, 16, SO)), axis=2) < cnt[:, :, None, :]
def rows(rng, cnt):
    hi = np.maximum(expo(rng, -3, 0, N, 8, 16, SO), EPS); lo = np.minimum(expo(rng, -8, -3.1, N, 8, 16, SO), UNDER)
    return np.where(mark(rng, cnt), hi, lo)
def alive(cnt):
    return 2 * cnt + np.roll(cnt, -1, axis=1) >= TH
def lanes(rng, n):
    v = rng.random((N, 8, SO)); v[1::2, :, SO - 1] = -1.0
    return np.where(np.argsort(np.argsort(v, axis=2), axis=2) < n[:, :, None], 16, 0)
def react(rng, live, n):
    a = rng.integers(0, S, (N, 8, RO)); b = rng.integers(0, S, (N, 8, RO))
    for g in range(8):
        lv = np.flatnonzero(live[:, g]); dd = np.flatnonzero(~live[:, g])
        if lv.size == 0 or dd.size == 0: continue
        for q in range(N):
            v = rng.random(RO)
            if q % 2: v[RO - 1] = -1.0
            s = np.argsort(v)[:int(n[q, g])]; x = rng.choice(dd, (2, RO))
            x[0, s] = rng.choice(lv, len(s)); x[1, s] = rng.integers(0, S, len(s))
            x[1] = np.where(rng.random(RO) < 0.1, x[0], x[1]); sw = rng.random(RO) < 0.5
            a[q, g] = np.where(sw, x[1], x[0]); b[q, g] = np.where(sw, x[0], x[1])
    return a, b
def parts(rng):
    c = expo(rng, -0.5, 0.5, N, 8, 1, SO) * expo(rng, -0.25, 0.25, N, 8, 16, SO)
    share = rng.choice(np.array([0.3, 0.45, 0.6, 0.75]), (N, 8, 1))
    cnt = np.where(rng.random((N, 8, SO)) < share, rng.integers(9, 17, (N, 8, SO)), rng.integers(0, 8, (N, 8, SO)))
    e = rows(rng, cnt)
    goal = (rng.random((N, 8, 1, SO)) < 0.05) & (rng.random((N, 8, 16, SO)) < 0.75)
    tau = np.where(goal, np.float32(1), expo(rng, -8, -4, N, 8, 16, SO))
    hot = ((1.0 + 0.25 * rng.permutation(8)) * 0.0625).reshape(1, 8, 1, 1)
    k = np.where(rng.random((N, 8, 1, RO)) < hot, expo(rng, -0.75, 0.5, N, 8, 1, RO), expo(rng, -5, -3, N, 8, 1, RO)) * expo(rng, -0.5, 0.5, N, 8, 16, RO)
    return [c, e, tau, k, rng.integers(0, S, (N, 8, RO)), rng.integers(0, S, (N, 8, RO)), rng.integers(0, R, (N, 8, SO, 16)), rng.integers(0, S, (N, 8, SO, 16))]
def pack(c, e, tau, k, a, b, rx, ot):
    fl = lambda x, lo, hi: np.ascontiguousarray(np.clip(x.astype(np.float32), np.float32(lo), np.float32(hi)).reshape(N, 128, -1))
    ls = lambda x: np.stack([gtable(v.reshape(8, -1)) for v in x])
    return {"cin": fl(c, 0.125, 8), "ein": fl(e, 0.00390625, 1), "tau": fl(tau, 0.00390625, 1), "kin": fl(k, 0.015625, 2), "ra": ls(a), "rb": ls(b), "rx": ls(rx), "ot": ls(ot)}
def setup_inputs(rng):
    return pack(*parts(rng))
def setup_inputs_spread(rng):
    p = parts(rng)
    p[0] = np.clip(expo(rng, -3, 3, N, 8, 1, SO) * expo(rng, -0.5, 0.5, N, 8, 16, SO), 0.125, 8)
    p[3] = np.clip(expo(rng, -6, -1, N, 8, 1, RO) * expo(rng, -0.5, 0.5, N, 8, 16, RO), 0.015625, 2)
    return pack(*p)
def atend(rng, x, top, share):
    return np.where(rng.random(x.shape) < 0.72, np.where(rng.random(x.shape) < share, top, 0), x)
def setup_inputs_ends(rng):
    c, e, tau, k, a, b, rx, ot = parts(rng); q = N - 1
    n = rng.choice(np.array([CL // 2, CL - 1, CL, CL + 1, SO // 2, SO - CF]), (N, 8)); n[q] = CL - 1
    cnt = lanes(rng, n); mix = rng.random((N, 8, SO)) < 0.2; mix[q] = False
    cnt = np.where(mix, rng.choice(np.array([1, 7, 8, 11, 12, 15]), (N, 8, SO)), cnt)
    cnt[0, 7, :2] = 16; cnt[q, 7, SO - 2:] = 16
    e = np.where(mark(rng, cnt), np.float32(1), LEAST)
    ch = lambda w, share, hi, lo: rng.random((N, 8, 16, w)) < np.where(rng.random((N, 8, 1, w)) < share, hi, lo)
    c = np.where(ch(SO, 0.15, 0.9, 0.05), 8.0, 0.125); k = np.where(ch(RO, 0.25, 0.9, 0.08), 2.0, 0.015625); tau = np.where(ch(SO, 0.06, 0.9, 0.01), np.float32(1), LEAST)
    a = atend(rng, a, S - 1, 0.5); b = atend(rng, b, S - 1, 0.5); ot = atend(rng, ot, S - 1, 0.5)
    rx = atend(rng, rx, R - 1, np.where(rng.random((N, 8, SO, 1)) < 0.3, 0.5, 0.02))
    a[0, :, 0] = 0; b[0, :, 0] = 0; k[0, :, :, 0] = 0.015625; c[0, :, :, 0] = 0.125
    a[q, :, RO - 1] = S - 1; b[q, :, RO - 1] = S - 1; k[q, :, :, RO - 1] = 2.0; c[q, :, :, SO - 1] = 8.0
    rx[q, :, SO - 1, :8] = R - 1; rx[q, :, SO - 1, 8:] = 0; rx[q, :, SO - 2, :8] = 0; rx[q, :, SO - 2, 8:] = R - 1
    rx[0, :, 0, :8] = 0; rx[0, :, 0, 8:] = R - 1; rx[0, :, 1, :8] = R - 1; rx[0, :, 1, 8:] = 0
    c[q, 7, :, SO - 2] = 8.0; c[0, 7, :, 1] = 0.125
    a[q, :, RO - 17:RO - 1] = S - 1; b[q, :, RO - 17:RO - 1] = S - 1; k[q, :, :, RO - 17:RO - 1] = 2.0 - 0.03125 * rng.random((8, 16, 16))
    for g in range(8):
        h = rng.permutation(np.flatnonzero(cnt[q, g, :SO - 2] == 16))[:8]
        c[q, g][:, h] = 4.0; rx[q, g, h] = R - 17 + np.argsort(rng.random((len(h), 16)), axis=1)
    return pack(c, e, tau, k, a, b, rx, ot)
def setup_inputs_corners(rng):
    p = parts(rng); q = N - 1
    menu = np.array([0, 1, CL - 1, CL, CL + 1, SO, SO - CF, SO - CF + 1, SO - CF - 1, SO - 1, SO // 2]); n = rng.choice(menu, (N, 8))
    n[0] = menu[:8]; n[1] = rng.permutation(menu)[:8]; n[q] = np.where(np.arange(8) % 2 == 1, CL, SO - CF)
    m = np.array([0, 1, CR - 1, CR, CR + 1, RO, RO - 1, CR]); rn = rng.choice(m, (N, 8)); rn[0] = rng.permutation(m); rn[q] = m
    cnt = lanes(rng, n); p[1] = rows(rng, cnt); p[4], p[5] = react(rng, alive(cnt), rn)
    own = (np.arange(N)[:, None] * SO + np.arange(SO)[None, :])[:, None, :, None]
    z = rng.random((N, 8, SO, 16)); p[7] = np.where(z < 0.1, own, np.where(z < 0.15, 0, np.where(z < 0.2, S - 1, p[7])))
    z = rng.random((N, 8, SO, 16)); p[6] = np.where(z < 0.05, 0, np.where(z < 0.1, R - 1, p[6]))
    return pack(*p)
def setup_inputs_crowd(rng):
    c, e, tau, k, a, b, rx, ot = parts(rng)
    for g in range(8):
        x, y = int(rng.integers(0, S)), int(rng.integers(0, R))
        if g == 0: x, y = S - 1, R - 1
        if g == 1: x, y = 0, 0
        e[x // SO, g, :, x % SO] = 1.0 if g < 4 else LEAST; tau[x // SO, g, :, x % SO] = 1.0 if g < 4 else LEAST
        if g % 4 == 0: a[:, g] = x; b[:, g] = x; rx[:, g] = y; ot[:, g] = x
        if g % 4 == 1:
            j = int(rng.integers(0, RO)); a[:, g, :j] = x; a[:, g, j + 1:] = x; b[:, g, :j] = x; b[:, g, j + 1:] = x
            rx[:, g, :, :15] = y; ot[:, g, :, :15] = x
        if g % 4 == 2:
            sp = np.array([x, (x + 1) % S, (x + SO) % S]); rc = np.array([y, (y + 1) % R, (y + RO) % R])
            a[:, g] = rng.choice(sp, (N, RO)); b[:, g] = rng.choice(sp, (N, RO)); rx[:, g] = rng.choice(rc, (N, SO, 16)); ot[:, g] = rng.choice(sp, (N, SO, 16))
        if g % 4 == 3: a[:, g] = x; rx[:, g, :, :8] = y
    return pack(c, e, tau, k, a, b, rx, ot)
def setup_inputs_calm(rng):
    p = parts(rng); i = 3 * np.arange(N)[:, None] + np.arange(8)[None, :]; q = N - 1
    n = np.array([0, 1, 2, 3, SO - 1, SO, CL, CL + 1])[i % 8]; n[1, 4:] = CL
    cnt = lanes(rng, n); keep = np.array(cnt[1, 4:])
    cnt[1::2] = rng.choice(np.array([0, 1, 2, 7, 8, 11, 12, 15, 16]), cnt[1::2].shape)
    v = rng.permutation(SO // 4); z, u = int(v[0]), int(v[1]); chain = v[2:7]; lapse = v[7:15]; rise = v[15:23]
    gg = SO // 4 + rng.permutation(CL - SO // 4)[:8]
    cnt[1, 4:] = keep; cnt[1, :2] = 16; cnt[1][:2, chain] = 0; cnt[1, 2] = 0; cnt[1, 3] = 16
    cnt[q][:, gg] = 16; cnt[q][:, z] = 16; cnt[q][:, u] = 0
    half = rng.random((N, 8, 16, SO)) < 0.5
    p[2] = np.where(mark(rng, cnt), np.where(half, EPS, np.float32(1)), np.where(half, UNDER, expo(rng, -8, -6, N, 8, 16, SO))); p[1] = np.array(p[2])
    p[0] = expo(rng, -1, 0.5, N, 8, 1, SO) * expo(rng, -0.25, 0.25, N, 8, 16, SO); p[3] = expo(rng, -6, -5.5, N, 8, 16, RO)
    lv = alive(cnt); p[4], p[5] = react(rng, lv, np.array([0, 1, 2, 3, RO - 1, RO, CR - 1, CR])[(i + 2) % 8])
    c, e, tau, k, a, b, rx, ot = p
    for x in (a, b):
        x[:, 2] = np.where(np.isin(x[:, 2], SO + lapse), q * SO + u, x[:, 2]); x[:, 3] = np.where(np.isin(x[:, 3], SO + rise), q * SO + z, x[:, 3])
        x[1, 2] = SO + rng.choice(lapse, RO)
    e[1, 2][:, lapse] = 1.0; tau[1, 2][:, lapse] = LEAST
    e[1, 3][:, rise] = LEAST
    for g in range(8):
        d = 2.0 ** -int(rng.integers(13, 20)); y, y2 = [int(x) for x in rng.permutation(RO)[:2]]; s = int(rng.integers(0, 16))
        flat = lv[:, g].reshape(-1)
        for j, rate in ((y, 0.5 * (1.0 - d)), (y2, 0.875)):
            x = q * SO + (z if flat[a[q, g, j]] or flat[b[q, g, j]] else u)
            a[q, g, j] = x; b[q, g, j] = x; k[q, g, :, j] = rate
        rx[:, g] = np.where((rx[:, g] == q * RO + y) | (rx[:, g] == q * RO + y2), rx[:, g] - q * RO, rx[:, g])
        c[q, g][:, [z, u]] = 1.0; rx[q, g, z, 8:] = rx[q, g, z, :8]
        e[q, g, :, z] = 0.25 * (1.0 + d); tau[q, g, :, z] = 0.25 * (1.0 + d)
        tau[q, g][:, gg] = LEAST; e[q, g][:, gg] = EPS; rx[q, g, gg, s] = q * RO + y; ot[q, g, gg, s] = q * SO + z
        if g < 2:
            src = q * SO + int(gg[0])
            for x in chain:
                e[1, g, :, x] = LEAST; tau[1, g, :, x] = LEAST; rx[1, g, x] = q * RO + y2; ot[1, g, x] = src; src = SO + int(x)
        if g >= 4:
            ot[1, g] = q * SO + rng.integers(0, SO, (SO, 16)); ot[1, g, SO - 1, 15] = q * SO + z; rx[1, g, SO - 1, 15] = q * RO + y
            tau[1, g, :, SO - 1] = LEAST; e[1, g, :, SO - 1] = EPS; c[1, g, :, SO - 1] = 1.0
    return pack(c, e, tau, k, a, b, rx, ot)
def check_inputs(d):
    bad = []
    for k, lo, hi in (("cin", 0.125, 8), ("ein", 0.00390625, 1), ("tau", 0.00390625, 1), ("kin", 0.015625, 2), ("ra", 0, S - 1), ("rb", 0, S - 1), ("rx", 0, R - 1), ("ot", 0, S - 1)):
        if not (np.min(d[k]) >= lo and np.max(d[k]) <= hi): bad.append("range of " + k)
    return bad
def first(flag, start, cap):
    f = np.roll(flag, -start, axis=2).astype(np.int64); before = np.add.accumulate(f, axis=2) - f
    return np.roll((f == 1) & (before < cap), start, axis=2)
def reference(cin, ein, tau, kin, ra, rb, rx, ot):
    F = np.float32
    glue = lambda x: np.array(x.astype(F).reshape(N, 8, 16, -1).transpose(1, 2, 0, 3), order="C").reshape(8, 16, -1)
    lst = lambda x: np.stack([gentries(v) for v in x]).astype(np.int64).transpose(1, 0, 2).reshape(8, -1)
    C, E, low, k = glue(cin), glue(ein), glue(tau), glue(kin)
    A, B = lst(ra), lst(rb); RX, OT = lst(rx).reshape(8, S, 16), lst(ot).reshape(8, S, 16)
    w = np.stack([(k[g] * C[g][:, A[g]]) * C[g][:, B[g]] for g in range(8)])
    for t in range(TR):
        cnt = np.add.reduce((E >= EPS).astype(np.int64), axis=1)
        live = 2 * cnt + np.roll(cnt, -1, axis=0) >= TH
        act = np.take_along_axis(live, A, 1) | np.take_along_axis(live, B, 1)
        mr = first(act.reshape(8, N, RO), (t * (RO // 4)) % RO, CR).reshape(8, R)
        ml = first(live.reshape(8, N, SO), (t * (SO // 4)) % SO, CL).reshape(8, S)
        mf = first(~live.reshape(8, N, SO), (t * (SO // 4)) % SO, CF).reshape(8, S)
        for g in range(8):
            j = np.flatnonzero(mr[g]); w[g][:, j] = (k[g][:, j] * C[g][:, A[g, j]]) * C[g][:, B[g, j]]
        for sweep in range(2):
            for g in range(8):
                s = np.flatnonzero(ml[g] | mf[g])
                p = E[g][:, OT[g, s].reshape(-1)] * np.minimum(w[g][:, RX[g, s].reshape(-1)], F(1))
                E[g][:, s] = np.maximum(low[g][:, s], np.max(p.reshape(16, len(s), 16), axis=2))
        for g in range(8):
            s = np.flatnonzero(ml[g]); x = w[g][:, RX[g, s].reshape(-1)].reshape(16, len(s), 16)
            for level in range(3): x = x[:, :, 0::2] + x[:, :, 1::2]
            C[g][:, s] = np.minimum(np.maximum(C[g][:, s] + (x[:, :, 0] - x[:, :, 1]) * F(0.125), F(0.125)), F(8))
    back = lambda x: np.ascontiguousarray(x.reshape(8, 16, N, -1).transpose(2, 0, 1, 3)).reshape(N, 128, -1)
    return {"yc": back(C), "ye": back(E), "yw": back(w)}

@@ -1,0 +1,553 @@
+from concourse.bass import DstId, RemoteDMATransfer
+from concourse.mybir import AluOpType as A, ActivationFunctionType as F
+
+N, SO, RO, TR = 4, 512, 1024, 5
+W0, W1 = 0, 5120
+ET = 4096
+C0, CA, F2 = 512, 2560, 1024
+PRE = [(512, 1536, "s"), (1536, 2048, "v"), (2048, 2560, "s")]
+CH1 = [0, 512, 1024, 2048, 2560, 3328, 4096]
+CA0 = 1536
+PRE0 = [(512, 1024, "s"), (1024, 1536, "v")]
+CH10 = [0, 512, 1024, 1536, 2304, 3200, 4096]
+CH2 = [0, 512, 1024, 2048, 3072, 4096]
+
+f32, bf, f16, i32, u16 = "float32", "bfloat16", "float16", "int32", "uint16"
+SCRATCH = {
+    "BIG": ("sbuf", [128, 10240], f32), "EA": ("sbuf", [128, 6144], f32), "EB": ("sbuf", [128, 6144], f32),
+    "WM": ("sbuf", [128, 4096], f32), "MG": ("sbuf", [128, 4096], f32),
+    "CT": ("sbuf", [128, 2048], f32), "LV": ("sbuf", [128, 2048], bf),
+    "XG": ("sbuf", [128, 3072], f32), "EG": ("sbuf", [128, 4096], f32), "RM": ("sbuf", [128, 1024], f32),
+    "KK": ("sbuf", [128, 1024], f32), "TT": ("sbuf", [128, 1024], f32), "CB": ("sbuf", [128, 1024], f32),
+    "TAU": ("sbuf", [128, 528], f32), "TE": ("sbuf", [128, 512], f32),
+    "RAI": ("sbuf", [128, 64], i32), "RBI": ("sbuf", [128, 64], i32),
+    "A16": ("sbuf", [128, 64], u16), "B16": ("sbuf", [128, 64], u16),
+    "RXI": ("sbuf", [128, 512], i32), "OTI": ("sbuf", [128, 512], i32), "PKT": ("sbuf", [128, 512], i32),
+    "PKD": ("sbuf", [128, 512], i32), "PK": ("sbuf", [128, 1216], i32), "O32": ("sbuf", [128, 256], i32),
+    "RX16": ("sbuf", [128, 256], u16), "OT16": ("sbuf", [128, 256], u16),
+    "LA": ("sbuf", [128, 1024], bf), "ACT": ("sbuf", [128, 1024], bf), "SC": ("sbuf", [128, 1024], f16),
+    "TY": ("sbuf", [128, 1024], bf), "SCL": ("sbuf", [128, 512], f16), "CAR": ("sbuf", [128, 8], f32),
+    "FL": ("sbuf", [128, 512], bf), "MX": ("sbuf", [128, 128], bf), "M0": ("sbuf", [128, 144], f32),
+    "M1": ("sbuf", [128, 144], f32), "Z1": ("sbuf", [128, 144], bf), "Z2": ("sbuf", [128, 144], f16),
+    "ONE": ("sbuf", [128, 128], bf), "JB": ("sbuf", [128, 128], bf), "JF": ("sbuf", [128, 128], f32),
+    "I1": ("sbuf", [128, 144], f32), "I2": ("sbuf", [128, 128], f32), "I3": ("sbuf", [128, 64], f32),
+    "PI": ("sbuf", [128, 8], i32), "PJ": ("sbuf", [128, 8], i32), "COL": ("sbuf", [128, 16], f32),
+    "KT": ("sbuf", [128, 64], f32), "YE": ("sbuf", [128, 32], f32), "SM": ("sbuf", [128, 512], f32),
+    "SL16": ("sbuf", [128, 32], u16), "OE16": ("sbuf", [128, 32], u16), "OD16": ("sbuf", [128, 32], u16),
+    "OU16": ("sbuf", [128, 32], u16), "SEL": ("sbuf", [128, 64], u16),
+    "L1": ("sbuf", [128, 768], f32), "L2": ("sbuf", [128, 384], f32), "L3": ("sbuf", [128, 192], f32),
+    "DD": ("sbuf", [128, 200], f32), "CN": ("sbuf", [128, 512], f32),
+    "PS": ("psum", [128, 4096], f32),
+}
+SEMAPHORES = ["sv", "ss", "sp", "sg", "ldc", "lde", "ldl", "ldk", "ldx", "ldt", "so",
+              "ac", "ae", "af", "al", "aw", "ax", "ah", "lc", "le", "lf", "ll", "lw", "lx"]
+
+
+def helpers(T, topo):
+    out = []
+    for c in T.cores:
+        free = [h for h in topo.cores_of(c) if h not in T.cores and h not in out]
+        near = [h for h in free if topo.die(h) == topo.die(c)]
+        out.append((near or free)[0])
+    return out
+
+
+def far_plan(T, topo, hs):
+    used, out = [], []
+    for c in T.cores:
+        h = [x for x in hs if x not in used and topo.die(x) != topo.die(c)][0]
+        used.append(h)
+        out.append((h, [d for d in T.cores if topo.die(d) != topo.die(c)], [d for d in T.cores if d != c and topo.die(d) == topo.die(c)]))
+    return out
+
+
+def dst_id(topo, c):
+    rid, pid, _ = topo.addr(c)
+    return DstId(rid=rid, pnc=pid)
+
+
+def common_engines(topo, src, dsts):
+    e = [x for x in topo.engines(src, dsts[0]) if all(x in topo.engines(src, d) for d in dsts)]
+    n = 1
+    while 2 * n <= len(e):
+        n *= 2
+    return e[:n]
+
+
+def as_mask(engines):
+    return sum(1 << e for e in engines)
+
+
+def half_cols(q, t, base):
+    base = base + q * RO
+    a, b = t % 4, (t + 1) % 4
+    if b == a + 1:
+        return [(base + 256 * a, base + 256 * a + 512)]
+    return [(base + 256 * a, base + 256 * a + 256), (base + 256 * b, base + 256 * b + 256)]
+
+
+def relay_plan(q, t, raw):
+    if raw:
+        return "BIG", half_cols(q, 0, W0 if t % 2 == 0 else W1), "MG", "ax", "lx"
+    return "WM", half_cols(q, t, 0), "EG", "aw", "lw"
+
+
+def helper_program(g, core, T, topo, hs):
+    q = hs.index(core)
+    others = [T.cores[(q + d) % N] for d in range(1, N)]
+    eng = common_engines(topo, core, others)
+    blk = T.EA[:, ET + q * SO:ET + (q + 1) * SO]
+    far = far_plan(T, topo, hs)
+    qw = [i for i in range(N) if far[i][0] == core][0]
+    near = far[qw][1]
+    for k in range(TR):
+        g.wait_ge(T.sem.ah, len(eng) * (k + 1))
+        g.remote_dma_fused([RemoteDMATransfer(dst_ids=[dst_id(topo, c) for c in others], dma_engine_mask=as_mask(eng),
+                                              remote_sem=T.sem.ae, src=T.XG[:, k * SO:(k + 1) * SO], dsts=[blk] * len(others))],
+                           local_sem=T.sem.le)
+        for raw in (False, True):
+            name, ps, land, rsem, _ = relay_plan(qw, k, raw)
+            g.wait_ge(T.sem[rsem], len(eng) * (k + 1))
+            wd = SO // len(ps)
+            g.remote_dma_fused([RemoteDMATransfer(dst_ids=[dst_id(topo, c) for c in near], dma_engine_mask=as_mask(eng[i::len(ps)]),
+                                                  remote_sem=T.sem[rsem], src=T[land][:, k * SO + i * wd:k * SO + (i + 1) * wd],
+                                                  dsts=[T[name][:, lo:hi]] * len(near)) for i, (lo, hi) in enumerate(ps)],
+                               local_sem=T.sem.le)
+    g.wait_ge(T.sem.le, 3 * TR * len(eng))
+
+
+def rank_program(g, core, T, topo):
+    q = T.rank_of(core)
+    hs = helpers(T, topo)
+    if q is None:
+        if core in hs:
+            helper_program(g, core, T, topo, hs)
+        return
+    others = [T.cores[(q + d) % N] for d in range(1, N)]
+    eng = common_engines(topo, core, others)
+    NE = len(eng)
+    Q = {"v": g.vector, "s": g.scalar, "p": g.tensor, "g": g, "y": g.sync}
+    CS = {"v": "sv", "s": "ss", "p": "sp", "g": "sg"}
+    total = {n: 0 for n in SEMAPHORES}
+    known = {k: {} for k in Q}
+    clock = {}
+    acc = {n: [] for n in SCRATCH}
+
+    def R(name, lo, hi, step=1):
+        ap = T[name][:, lo:hi] if step == 1 else T[name][:, lo:hi:step]
+        return (ap, [(name, lo, hi)])
+
+    def G(win, off):
+        return (win[0].indirect(off[0]), win[1], off[1])
+
+    def wait(k, sem, n):
+        if known[k].get(sem, 0) >= n:
+            return
+        if sem not in CS.values():
+            n = total[sem]
+        Q[k].wait_ge(T.sem[sem], n)
+        known[k][sem] = n
+        for s, m in clock.get((sem, n), {}).items():
+            if known[k].get(s, 0) < m:
+                known[k][s] = m
+
+    def need(k, sem):
+        wait(k, sem, total[sem])
+
+    def order(k, reads, writes, chain=False):
+        dep = {}
+        for regs, wr in ((reads, False), (writes, True)):
+            for name, lo, hi in regs:
+                for (a, b, w2, k2, sem, n) in acc[name]:
+                    x, y, hit = lo, hi, wr or w2
+                    if name == "PS" and k2 != k:
+                        x, y, hit = lo // 512 * 512, -(-hi // 512) * 512, True
+                    if chain and k2 == k and name == "PS":
+                        hit = False
+                    if hit and a < y and x < b:
+                        dep[sem] = max(dep.get(sem, 0), n)
+        for sem in sorted(dep, key=lambda s: s not in CS.values()):
+            wait(k, sem, dep[sem])
+
+    def note(k, reads, writes, sem, n):
+        for name, lo, hi in writes:
+            acc[name][:] = [e for e in acc[name] if not (lo <= e[0] and e[1] <= hi and (name != "PS" or e[3] == k))]
+            acc[name].append((lo, hi, True, k, sem, n))
+        for name, lo, hi in reads:
+            acc[name][:] = [e for e in acc[name] if not (e[3] == k and e[4] == sem and not e[2] and lo <= e[0] and e[1] <= hi)]
+            acc[name].append((lo, hi, False, k, sem, n))
+
+    def op(k, out, ins, call, chain=False):
+        reads = [r for x in ins for r in x[1]] + [r for x in ins + [out] if len(x) > 2 for r in x[2]]
+        order(k, reads, out[1], chain)
+        sem = CS[k]
+        total[sem] += 1
+        call().then_inc(T.sem[sem], 1)
+        clock[(sem, total[sem])] = dict(known[k])
+        note(k, reads, out[1], sem, total[sem])
+
+    def isap(x):
+        return isinstance(x, tuple)
+
+    def tt(out, a, b, o):
+        op("v", out, [a, b], lambda: g.vector.tensor_tensor(out[0], a[0], b[0], o))
+
+    def ts(out, a, s1, o1, s2=None, o2=None):
+        ins = [a] + [s for s in (s1, s2) if isap(s)]
+        x1, x2 = (s1[0] if isap(s1) else s1), (s2[0] if isap(s2) else s2)
+        if o2 is None:
+            op("v", out, ins, lambda: g.vector.tensor_scalar(out[0], a[0], x1, None, o1))
+        else:
+            op("v", out, ins, lambda: g.vector.tensor_scalar(out[0], a[0], x1, x2, o1, o2))
+
+    def cp(out, a):
+        op("v", out, [a], lambda: g.vector.tensor_copy(out[0], a[0]))
+
+    def fill(out, c):
+        op("v", out, [], lambda: g.vector.memset(out[0], c))
+
+    def scan(out, d0, d1, init, o0, o1):
+        ins = [d0, d1] + ([init] if isap(init) else [])
+        op("v", out, ins, lambda: g.vector.tensor_tensor_scan(out[0], d0[0], d1[0], init[0] if isap(init) else init, o0, o1))
+
+    def act(out, a, scale=1.0):
+        op("s", out, [a], lambda: g.scalar.activation(out[0], a[0], F.Copy, scale=scale))
+
+    def mm(out, l, r, start, stop):
+        op("p", out, [l, r], lambda: g.tensor.matmul(out[0], l[0], r[0], start, stop), chain=not start)
+
+    def iota(out, pattern, base, cm, small=True):
+        if small:
+            op("g", out, [], lambda: g.iota(out[0], pattern, base, cm, allow_small_or_imprecise_dtypes=True))
+        else:
+            op("g", out, [], lambda: g.iota(out[0], pattern, base, cm))
+
+    def load(k, out, src, sem):
+        order(k, [], out[1])
+        total[sem] += 16
+        Q[k].dma_start(out[0], src).then_inc(T.sem[sem], 16)
+        note(k, [], out[1], sem, total[sem])
+
+    def store(k, dst, a):
+        order(k, a[1], [])
+        total["so"] += 16
+        Q[k].dma_start(dst, a[0]).then_inc(T.sem.so, 16)
+        note(k, a[1], [], "so", total["so"])
+
+    def send(pieces, cs, lands, rsem, lsem):
+        reads = [r for p in pieces for r in p[1]]
+        order("g", reads, [])
+        n = len(pieces)
+        g.remote_dma_fused([RemoteDMATransfer(dst_ids=[dst_id(topo, c) for c in cs], dma_engine_mask=as_mask(eng[i::n]),
+                                              remote_sem=T.sem[rsem], src=p[0], dsts=lands[i]) for i, p in enumerate(pieces)],
+                           local_sem=T.sem[lsem])
+        total[lsem] += NE
+        note("g", reads, [], lsem, total[lsem])
+
+    def send_all(pieces, rsem, lsem):
+        send(pieces, others, [[p[0]] * len(others) for p in pieces], rsem, lsem)
+
+    def send_across(t, raw):
+        name, cols, land, rsem, lsem = relay_plan(q, t, raw)
+        ps = [R(name, lo, hi) for lo, hi in cols]
+        h, _, near = far_plan(T, topo, hs)[q]
+        wd = SO // len(ps)
+        send(ps, [h] + near, [[T[land][:, t * SO + i * wd:t * SO + (i + 1) * wd]] + [p[0]] * len(near) for i, p in enumerate(ps)], rsem, lsem)
+
+    def send_e(k):
+        send([eown("EA")], [hs[q]], [[T.XG[:, k * SO:(k + 1) * SO]]], "ah", "le")
+
+    def arrive(name, base, width, sem, calls=1):
+        total[sem] += (N - 1) * NE * calls
+        note("x", [], [(name, base + r * width, base + (r + 1) * width) for r in range(N) if r != q], sem, total[sem])
+
+    def extract(bank, z, src, lo, n, last=True):
+        for r in range(16):
+            mm(R("PS", 512 * bank, 512 * bank + n), R(z, 16 - r, 144 - r), R(src, lo + r, lo + 16 * n, 16), r == 0, last and r == 15)
+
+    cown = R("CT", q * SO, (q + 1) * SO)
+    ctab = R("CT", 0, 2048)
+    lvtab = R("LV", 0, 2048)
+    mtab = R("WM", 0, 4096)
+    delta = float(4096 - RO * q)
+    sm = lambda i: R("SM", 32 * i, 32 * i + 32)
+    col = lambda i: R("COL", i, i + 1)
+    eown = lambda b, lo=0, hi=SO: R(b, ET + q * SO + lo, ET + q * SO + hi)
+    etab = lambda b: R(b, ET, ET + 2048)
+    egat = lambda b, lo, hi: G(etab(b), R("OT16", lo // 16, hi // 16))
+    mgat = lambda lo, hi: G(mtab, R("RX16", lo // 16, hi // 16))
+    wm = lambda a, b: R("WM", q * RO + 256 * a, q * RO + 256 * b)
+
+    def live():
+        for h in range(2):
+            ts(R("FL", 256 * h, 256 * h + 256), eown("EA", 256 * h, 256 * h + 256), 0.125, A.is_ge)
+            mm(R("PS", 1024 + 512 * h, 1280 + 512 * h), R("MX", 0, 128), R("FL", 256 * h, 256 * h + 256), True, True)
+        for h in range(2):
+            ts(R("LV", q * SO + 256 * h, q * SO + 256 * h + 256), R("PS", 1024 + 512 * h, 1280 + 512 * h), 24.0, A.is_ge)
+
+    def picks_count(t):
+        p = (128 * t) % SO
+        scan(R("SCL", p, SO), R("TY", p, SO), R("LV", q * SO + p, (q + 1) * SO), 0.0, A.mult, A.add)
+        if p:
+            cp(R("CAR", 0, 1), R("SCL", SO - 1, SO))
+            scan(R("SCL", 0, p), R("TY", 0, p), R("LV", q * SO, q * SO + p), R("CAR", 0, 1), A.mult, A.add)
+        extract(4, "Z2", "SCL", 0, 32)
+
+    def picks_slots(t, between=(list, list)):
+        y = R("PS", 2048, 2080)
+        x0 = 32 - 8 * (t % 4)
+        ts(sm(0), y, 192.0 - 2047.0, A.is_ge, 192.0, A.mult)
+        tt(sm(1), R("KT", x0, x0 + 32), y, A.subtract)
+        tt(sm(2), sm(0), y, A.add)
+        ts(sm(3), sm(1), 256.0 - 2047.0, A.is_ge, 512.0, A.mult)
+        between[0]()
+        tt(sm(4), sm(3), sm(1), A.add)
+        between[1]()
+        tt(sm(5), sm(2), sm(4), A.min)
+        ts(R("SL16", 0, 32), sm(5), 2047.0, A.add)
+
+    def picks_scatter():
+        cp(G(R("PK", 0, 1216), R("SL16", 0, 32)), R("PKD", 0, SO))
+
+    def picks_lists():
+        ts(R("O32", 0, 256), R("PK", 0, 256), 4095, A.bitwise_and)
+        ts(R("RX16", 0, 256), R("PK", 0, 256), 1.0 / 4096, A.mult)
+        cp(R("OT16", 0, 256), R("O32", 0, 256))
+
+    def back_1():
+        ts(sm(6), sm(5), 16.0, A.mult, 2047.0 * 16 + 15, A.add)
+        ts(sm(8), sm(5), 256.0 - 2047.0, A.is_ge, 512.0, A.mult)
+        tt(sm(7), sm(6), R("YE", 0, 32), A.min)
+        tt(sm(9), sm(8), R("JF", 0, 32), A.max)
+
+    def back_2():
+        cp(R("OU16", 0, 32), sm(9))
+        cp(R("OE16", 0, 32), sm(7))
+        ts(R("OD16", 0, 32), sm(5), 2047.0, A.add, 192.0, A.min)
+
+    def tau_picked():
+        act(R("TE", 0, SO), G(R("TAU", 0, 528), R("OU16", 0, 32)))
+
+    def rate_pre(lo, hi):
+        act(R("PS", lo, hi), R("KK", lo, hi))
+        act(R("TT", lo, hi), G(ctab, R("A16", lo // 16, hi // 16)))
+        act(R("CB", lo, hi), G(ctab, R("B16", lo // 16, hi // 16)))
+
+    def rate_1(lo, hi):
+        tt(R("PS", lo, hi), R("TT", lo, hi), R("PS", lo, hi), A.mult)
+
+    def rate_2(lo, hi, base):
+        tt(R("BIG", base + lo, base + hi), R("CB", lo, hi), R("PS", lo, hi), A.mult)
+
+    def maxscan(b, lo, hi):
+        scan(R(b, lo, hi), R("RM", 0, hi - lo), R("EG", lo, hi), 0.0, A.min, A.max)
+
+    def writeback(src, dst, lo, hi):
+        tt(eown(dst, lo, hi), G(R(src, 0, 6144), R("OE16", lo // 16, hi // 16)), R("TE", lo, hi), A.max)
+
+    def rates(t, wn, wo):
+        send_all([R("LV", q * SO, (q + 1) * SO)], "al", "ll")
+        send_e(t)
+        picks_count(t)
+        for k in "vs":
+            need(k, "lw")
+            need(k, "lx")
+        halves = [half_cols(0, t, 0), half_cols(0, t + 2, 0)]
+        for a, b in halves[0]:
+            rate_1(a, b)
+        picks_slots(t, [lambda: [rate_2(a, b, wo + 4096) for a, b in halves[0]], lambda: [rate_1(a, b) for a, b in halves[1]]])
+        picks_scatter()
+        arrive("LV", 0, SO, "al")
+        nq = [(k + t) % 4 for k in range(4)]
+        x0 = 16 * (t % 4)
+        win = R("BIG", wo + q * RO, wo + 5120)
+        for k in range(4):
+            act(R("LA", 256 * k, 256 * k + 256), G(lvtab, R("A16", 16 * nq[k], 16 * nq[k] + 16)))
+            tt(R("ACT", 256 * k, 256 * k + 256), G(lvtab, R("B16", 16 * nq[k], 16 * nq[k] + 16)), R("LA", 256 * k, 256 * k + 256), A.max)
+            if k == 1:
+                extract(5, "Z1", "ACT", 0, 32, last=False)
+                mm(R("PS", 2560, 2592), R("ONE", 0, 128), R("JB", x0, x0 + 32), False, True)
+
+        def select(half):
+            c = 32 * half
+            for (a, b), (x, y) in zip(half_cols(q, t + 2 * half, 0), half_cols(q, t + 2 * half, wn)):
+                src = G(win, R("SEL", c, c + (b - a) // 16))
+                ts(R("WM", a, b), src, 1.0, A.min)
+                act(R("BIG", x, y), src)
+                c += (b - a) // 16
+
+        ts(R("SEL", 0, 32), R("PS", 2560, 2592), col(2), A.add)
+        select(0)
+        send_across(t, False)
+        scan(R("SC", 0, RO), R("TY", 0, RO), R("ACT", 0, RO), 0.0, A.mult, A.add)
+        extract(6, "Z2", "SC", 512, 32)
+        for a, b in halves[1]:
+            rate_2(a, b, wo + 4096)
+        ts(sm(10), R("PS", 3072, 3104), 512.0 - 2048.0, A.is_le, delta, A.mult)
+        tt(sm(11), sm(10), R("JF", x0 + 32, x0 + 64), A.add)
+        cp(R("SEL", 32, 64), sm(11))
+        select(1)
+        send_all([R("WM", a, b) for a, b in half_cols(q, t + 2, 0)], "aw", "lw")
+
+    def first_rates():
+        wq = lambda a, b: R("BIG", W0 + q * RO + a, W0 + q * RO + b)
+        arrive("CT", 0, SO, "ac")
+        rate_pre(512, 1024)
+        tt(R("TT", 0, 512), G(ctab, R("A16", 0, 32)), R("KK", 0, 512), A.mult)
+        tt(wq(0, 512), G(ctab, R("B16", 0, 32)), R("TT", 0, 512), A.mult)
+        ts(wm(0, 2), wq(0, 512), 1.0, A.min)
+        send_across(0, False)
+        rate_1(512, 1024)
+        rate_2(512, 1024, W0 + q * RO)
+        ts(wm(2, 4), wq(512, 1024), 1.0, A.min)
+        send_all([wm(2, 4)], "aw", "lw")
+        ts(R("PKT", 0, SO), R("RXI", 0, SO), 4096.0, A.mult)
+        need("y", "sv")
+        load("y", R("TAU", 0, SO), T.tau[:], "ldt")
+        tt(R("PKD", 0, SO), R("PKT", 0, SO), R("OTI", 0, SO), A.add)
+        picks_scatter()
+
+    def amounts(t):
+        for c in range(3):
+            lo, hi = 1024 * c, 1024 * c + 1024
+            tt(R("PS", 256 * c, 256 * c + 256), R("XG", lo, hi, 4), R("XG", lo + 1, hi, 4), A.add)
+            tt(R("L1", 256 * c, 256 * c + 256), R("XG", lo + 2, hi, 4), R("XG", lo + 3, hi, 4), A.add)
+        tt(R("L2", 0, 384), R("L1", 1, 768, 2), R("PS", 1, 768, 2), A.add)
+        tt(R("PS", 0, 768, 2), R("PS", 0, 768, 2), R("L1", 0, 768, 2), A.add)
+        tt(R("L3", 0, 192), R("PS", 2, 768, 4), R("L2", 1, 384, 2), A.add)
+        tt(R("PS", 0, 768, 4), R("PS", 0, 768, 4), R("L2", 0, 384, 2), A.add)
+        tt(R("DD", 0, 192), R("PS", 0, 768, 4), R("L3", 0, 192), A.subtract)
+        tt(R("CN", 0, SO), G(R("DD", 0, 200), R("OD16", 0, 32)), cown, A.add)
+        ts(cown, R("CN", 0, SO), 0.125, A.max, 8.0, A.min)
+        if t < TR - 1:
+            send_all([cown], "ac", "lc")
+        else:
+            store("y", T.yc[:], cown)
+
+    def sweeps(t, wn):
+        send_across(t, True)
+        send_all([R("BIG", wn + q * RO + 512, wn + (q + 1) * RO)], "ax", "lx")
+        picks_lists()
+        if t:
+            back_1()
+            back_2()
+        arrive("EA", ET, SO, "ae")
+        pre, ca, ch1 = (PRE, CA, CH1) if t else (PRE0, CA0, CH10)
+        for lo, hi, k in pre:
+            (cp if k == "v" else act)(R("EG", lo, hi), egat("EA", lo, hi))
+        act(R("TT", 0, C0), egat("EA", 0, C0))
+        for lo, hi, k in sorted(pre, key=lambda x: x[2] != "v"):
+            cp(R("PS", lo, hi), R("EG", lo, hi))
+
+        arrive("WM", 0, RO, "aw", calls=2)
+        nc = len(ch1) - 1
+        for c in range(nc):
+            lo, hi = ch1[c], ch1[c + 1]
+            if c == 0:
+                tt(R("EG", lo, hi), mgat(lo, hi), R("TT", lo, hi), A.mult)
+                maxscan("EA", lo, hi)
+                continue
+            act(R("MG", lo, hi), mgat(lo, hi))
+            if hi <= ca:
+                tt(R("EG", lo, hi), R("MG", lo, hi), R("PS", lo, hi), A.mult)
+            else:
+                tt(R("EG", lo, hi), egat("EA", lo, hi), R("MG", lo, hi), A.mult)
+            if c >= 2:
+                maxscan("EA", ch1[c - 1], lo)
+        tau_picked()
+        maxscan("EA", ch1[nc - 1], ch1[nc])
+        writeback("EA", "EB", 0, SO)
+        send_all([eown("EB")], "af", "lf")
+
+        arrive("BIG", wn, RO, "ax", calls=2)
+        if t == TR - 1:
+            need("y", "ax")
+            store("y", T.yw[:], R("BIG", wn + q * RO, wn + (q + 1) * RO))
+        for c in range(3):
+            act(R("XG", 1024 * c, 1024 * c + 1024), G(R("BIG", wn, wn + 4096), R("RX16", 64 * c, 64 * c + 64)), 0.125)
+        act(R("MG", 0, C0), mgat(0, C0))
+        for lo in range(F2, 4096, 1024):
+            act(R("PS", lo, lo + 1024), R("MG", lo, lo + 1024))
+        amounts(t)
+
+        arrive("EB", ET, SO, "af")
+        nc = len(CH2) - 1
+        for c in range(nc + 1):
+            if c < nc:
+                lo, hi = CH2[c], CH2[c + 1]
+                if hi <= F2:
+                    tt(R("EG", lo, hi), egat("EB", lo, hi), R("MG", lo, hi), A.mult)
+                else:
+                    act(R("EG", lo, hi), egat("EB", lo, hi))
+                    tt(R("EG", lo, hi), R("EG", lo, hi), R("PS", lo, hi), A.mult)
+            if c >= 1:
+                maxscan("EB", CH2[c - 1], CH2[c])
+        if t < TR - 1:
+            arrive("CT", 0, SO, "ac")
+            rate_pre(0, RO)
+        writeback("EB", "EA", 0, 256)
+        writeback("EB", "EA", 256, 512)
+        if t < TR - 1:
+            live()
+        else:
+            store("y", T.ye[:, 0:256], eown("EA", 0, 256))
+            store("s", T.ye[:, 256:512], eown("EA", 256, 512))
+
+    load("y", cown, T.cin[:], "ldc")
+    load("y", eown("EA"), T.ein[:], "lde")
+    load("y", R("RAI", 0, 64), T.ra[:], "ldl")
+    load("y", R("RBI", 0, 64), T.rb[:], "ldl")
+    load("y", R("KK", 0, RO), T.kin[:], "ldk")
+    iota(R("PI", 0, 2), [[112, 2]], 0, 1, small=False)
+    iota(R("I2", 0, 128), [[1, 8], [0, 16]], 0, 0)
+    iota(R("I1", 0, 144), [[1, 144]], -16, -1)
+    iota(R("I3", 0, 64), [[0, 2], [16, 32]], 192 - 2047, 0)
+    iota(R("JB", 0, 128), [[0, 2], [16, 64]], 0, 0)
+    send_all([cown], "ac", "lc")
+    send_e(0)
+    iota(R("PK", 0, 1216), [[0, 1216]], 0, 0, small=False)
+    iota(R("RM", 0, 1024), [[0, 64], [1, 16]], 0, 0)
+    need("y", "lc")
+    load("y", R("RXI", 0, SO), T.rx[:], "ldx")
+    load("y", R("OTI", 0, SO), T.ot[:], "ldx")
+
+    fill(R("TY", 0, 1024), 1.0)
+    ts(R("PJ", 0, 2), R("PI", 0, 2), 4, A.arith_shift_right, 7, A.bitwise_and)
+    ts(R("PJ", 2, 3), R("PI", 0, 1), 15, A.bitwise_and)
+    cp(R("COL", 0, 3), R("PJ", 0, 3))
+    ts(R("M0", 0, 128), R("I2", 0, 128), col(0), A.is_equal, 2.0, A.mult)
+    ts(R("M1", 0, 128), R("I2", 0, 128), col(1), A.is_equal)
+    ts(col(4), col(2), 0.0, A.is_equal)
+    ts(col(5), col(2), 1.0, A.is_equal, -2048.0, A.mult)
+    ts(col(6), col(2), 1.0, A.not_equal)
+    tt(R("MX", 0, 128), R("M0", 0, 128), R("M1", 0, 128), A.add)
+    ts(R("TY", 0, 1024), R("TY", 0, 1024), col(6), A.mult)
+    ts(R("M0", 0, 144), R("I1", 0, 144), 0.0, A.is_equal, col(4), A.mult)
+    ts(R("M1", 0, 144), R("I1", 0, 144), -1.0, A.is_equal, col(5), A.mult)
+    live()
+    tt(R("Z2", 0, 144), R("M0", 0, 144), R("M1", 0, 144), A.add)
+    ts(R("KT", 0, 64), R("I3", 0, 64), col(2), A.add)
+    picks_count(0)
+    ts(R("Z1", 0, 144), R("M0", 0, 144), delta, A.mult)
+    ts(R("JF", 0, 128), R("JB", 0, 128), col(2), A.add)
+    cp(R("A16", 0, 64), R("RAI", 0, 64))
+    cp(R("B16", 0, 64), R("RBI", 0, 64))
+    fill(R("ONE", 0, 128), 1.0 / 128)
+    fill(R("DD", 0, 200), 0.0)
+    fill(R("TAU", 512, 528), 0.0)
+    ts(R("YE", 0, 32), R("JF", 0, 32), float(ET + SO * q), A.add)
+    picks_slots(0)
+    back_1()
+    back_2()
+
+    for t in range(TR):
+        wn, wo = (W0, W1) if t % 2 == 0 else (W1, W0)
+        if t == 0:
+            first_rates()
+        else:
+            rates(t, wn, wo)
+        sweeps(t, wn)
+
+    for sem in SEMAPHORES:
+        if total[sem]:
+            need("g", sem)

@@ -4,13 +4,18 @@ from concourse.mybir import AluOpType as A, ActivationFunctionType as F
 N, SO, RO, TR = 4, 512, 1024, 5
 W0, W1 = 0, 5120
 ET = 4096
-C0, CA, F2 = 512, 2560, 1024
-PRE = [(512, 1536, "s"), (1536, 2048, "v"), (2048, 2560, "s")]
-CH1 = [0, 512, 1024, 2048, 2560, 3328, 4096]
-CA0 = 1536
-PRE0 = [(512, 1024, "s"), (1024, 1536, "v")]
-CH10 = [0, 512, 1024, 1536, 2304, 3200, 4096]
-CH2 = [0, 512, 1024, 2048, 3072, 4096]
+OPT = dict(clr=1, unit=512, c0=512, first2=False, kat="s2",
+           pre=[(2048, 3072, "s", "p"), (1024, 2048, "v", "v")],
+           pre0=[(2048, 3072, "s", "p"), (1024, 2048, "v", "v")],
+           cpm=[(512, 1024, "p"), (2048, 3072, "s"), (3072, 4096, "l"), (1024, 2048, "l")],
+           s1="m12 s02 m24 m46 s24 m68 s46 s68 w0", f=[(0, 512, "d")],
+           l=[(0, 512, "d")], tail="w0 w1 g0 g1 t0 t1", s2=[(512, 1024), (2048, 3072), (3072, 4096), (1024, 2048)], own2=[],
+           ez="s", tau="b", la=[0, 256, 512, 768, 1024],
+           xg=[0, 1024, 2048, 3072], tb=[0, 2048, 3072], treeA=2048, wb=[0, 256, 512], ge=[0, 256, 512], th=2,
+           kcp="p", invk=-1, fill=0, cout=-1, loads="ceabko rt", wrot=0,
+           e=[(0, 512, "a")], m=[(0, 512, "a"), (512, 1024, "d")], w=[(0, 512, "a"), (512, 1024, "d")],
+           m0=[(0, 512, "a"), (512, 1024, "d")], w0=[(0, 512, "a"), (512, 1024, "d")], e0=[(0, 512, "a")],
+           steps="y2 n x2 k L p a256 a512 a768 a1024 o0 c1024 s0 r0 o1 s1 r1 i0 b0 i1 b1 l1 b2 l0 t1")
 
 f32, bf, f16, i32, u16 = "float32", "bfloat16", "float16", "int32", "uint16"
 SCRATCH = {
@@ -19,43 +24,34 @@ SCRATCH = {
     "CT": ("sbuf", [128, 2048], f32), "LV": ("sbuf", [128, 2048], bf),
     "XG": ("sbuf", [128, 3072], f32), "EG": ("sbuf", [128, 4096], f32), "RM": ("sbuf", [128, 1024], f32),
     "KK": ("sbuf", [128, 1024], f32), "TT": ("sbuf", [128, 1024], f32), "CB": ("sbuf", [128, 1024], f32),
-    "TAU": ("sbuf", [128, 528], f32), "TE": ("sbuf", [128, 512], f32),
+    "TAU": ("sbuf", [128, 528], f32), "TE": ("sbuf", [128, 512], f32), "TH": ("sbuf", [128, 512], f32),
     "RAI": ("sbuf", [128, 64], i32), "RBI": ("sbuf", [128, 64], i32),
-    "A16": ("sbuf", [128, 64], u16), "B16": ("sbuf", [128, 64], u16),
-    "RXI": ("sbuf", [128, 512], i32), "OTI": ("sbuf", [128, 512], i32), "PKT": ("sbuf", [128, 512], i32),
-    "PKD": ("sbuf", [128, 512], i32), "PK": ("sbuf", [128, 1216], i32), "O32": ("sbuf", [128, 256], i32),
-    "RX16": ("sbuf", [128, 256], u16), "OT16": ("sbuf", [128, 256], u16),
+    "A16": ("sbuf", [128, 128], u16), "B16": ("sbuf", [128, 128], u16),
+    "LI": ("sbuf", [128, 1920], i32),
+    "L16": ("sbuf", [128, 512], u16), "POS": ("sbuf", [128, 1024], f32), "INV": ("sbuf", [128, 1216], f32),
+    "IH": ("sbuf", [128, 256], f32), "IV16": ("sbuf", [128, 16], u16), "PM": ("sbuf", [128, 256], f32),
     "LA": ("sbuf", [128, 1024], bf), "ACT": ("sbuf", [128, 1024], bf), "SC": ("sbuf", [128, 1024], f16),
     "TY": ("sbuf", [128, 1024], bf), "SCL": ("sbuf", [128, 512], f16), "CAR": ("sbuf", [128, 8], f32),
     "FL": ("sbuf", [128, 512], bf), "MX": ("sbuf", [128, 128], bf), "M0": ("sbuf", [128, 144], f32),
     "M1": ("sbuf", [128, 144], f32), "Z1": ("sbuf", [128, 144], bf), "Z2": ("sbuf", [128, 144], f16),
+    "ID": ("sbuf", [128, 128], f32), "I4": ("sbuf", [128, 128], f32), "RH": ("sbuf", [128, 128], bf), "HB": ("sbuf", [128, 128], bf),
     "ONE": ("sbuf", [128, 128], bf), "JB": ("sbuf", [128, 128], bf), "JF": ("sbuf", [128, 128], f32),
     "I1": ("sbuf", [128, 144], f32), "I2": ("sbuf", [128, 128], f32), "I3": ("sbuf", [128, 64], f32),
     "PI": ("sbuf", [128, 8], i32), "PJ": ("sbuf", [128, 8], i32), "COL": ("sbuf", [128, 16], f32),
-    "KT": ("sbuf", [128, 64], f32), "YE": ("sbuf", [128, 32], f32), "SM": ("sbuf", [128, 512], f32),
-    "SL16": ("sbuf", [128, 32], u16), "OE16": ("sbuf", [128, 32], u16), "OD16": ("sbuf", [128, 32], u16),
-    "OU16": ("sbuf", [128, 32], u16), "SEL": ("sbuf", [128, 64], u16),
+    "KT": ("sbuf", [128, 64], f32), "YE": ("sbuf", [128, 64], f32), "SM": ("sbuf", [128, 512], f32),
+    "SL16": ("sbuf", [128, 32], u16), "OE16": ("sbuf", [128, 64], u16), "SEL": ("sbuf", [128, 64], u16),
     "L1": ("sbuf", [128, 768], f32), "L2": ("sbuf", [128, 384], f32), "L3": ("sbuf", [128, 192], f32),
-    "DD": ("sbuf", [128, 200], f32), "CN": ("sbuf", [128, 512], f32),
+    "DD": ("sbuf", [128, 1216], f32),
     "PS": ("psum", [128, 4096], f32),
 }
-SEMAPHORES = ["sv", "ss", "sp", "sg", "ldc", "lde", "ldl", "ldk", "ldx", "ldt", "so",
-              "ac", "ae", "af", "al", "aw", "ax", "ah", "lc", "le", "lf", "ll", "lw", "lx"]
+SEMAPHORES = ["sv", "ss", "sp", "sg", "ldc", "lde", "ldl", "ldk", "ldx", "ldo", "ldt", "so",
+              "ac", "lc", "le", "lf", "ll", "lw", "lx"] + ["a%s%d" % (w, i) for w in "emwfl" for i in range(4)]
 
 
 def helpers(T, topo):
-    out = []
-    for c in T.cores:
-        free = [h for h in topo.cores_of(c) if h not in T.cores and h not in out]
-        near = [h for h in free if topo.die(h) == topo.die(c)]
-        out.append((near or free)[0])
-    return out
-
-
-def far_plan(T, topo, hs):
     used, out = [], []
     for c in T.cores:
-        h = [x for x in hs if x not in used and topo.die(x) != topo.die(c)][0]
+        h = [x for x in topo.cores_of(c) if x not in T.cores and x not in used and topo.die(x) != topo.die(c)][0]
         used.append(h)
         out.append((h, [d for d in T.cores if topo.die(d) != topo.die(c)], [d for d in T.cores if d != c and topo.die(d) == topo.die(c)]))
     return out
@@ -78,50 +74,49 @@ def as_mask(engines):
     return sum(1 << e for e in engines)
 
 
-def half_cols(q, t, base):
-    base = base + q * RO
-    a, b = t % 4, (t + 1) % 4
-    if b == a + 1:
-        return [(base + 256 * a, base + 256 * a + 512)]
-    return [(base + 256 * a, base + 256 * a + 256), (base + 256 * b, base + 256 * b + 256)]
+def cyclic(p, a, b, width):
+    lo, n = (p + a) % width, b - a
+    if n == width:
+        return [(0, width)]
+    return [(lo, lo + n)] if lo + n <= width else [(lo, lo + n // 2), (0, n // 2)]
 
 
-def relay_plan(q, t, raw):
-    if raw:
-        return "BIG", half_cols(q, 0, W0 if t % 2 == 0 else W1), "MG", "ax", "lx"
-    return "WM", half_cols(q, t, 0), "EG", "aw", "lw"
+def pieces(q, t, what):
+    name, base, width, p, land, lsem = {"e": ("EA", ET + q * SO, SO, 0, "XG", "le"), "m": ("WM", q * RO, RO, 256 * t, "EA", "lw"),
+                                        "f": ("EB", ET + q * SO, SO, 128 * t, "EG", "lf"),
+                                        "l": ("LV", q * SO, SO, 0, "LV", "ll"),
+                                        "w": ("BIG", (W1 if t % 2 else W0) + q * RO, RO, 256 * t * OPT["wrot"], "EB", "lx")}[what]
+    return [(name, [(base + lo, base + hi) for lo, hi in cyclic(p, a, b, width)], way, land, t * width + a, "a%s%d" % (what, i), lsem)
+            for i, (a, b, way) in enumerate(OPT[what if t or what in "fl" else what + "0"])]
 
 
-def helper_program(g, core, T, topo, hs):
-    q = hs.index(core)
-    others = [T.cores[(q + d) % N] for d in range(1, N)]
-    eng = common_engines(topo, core, others)
-    blk = T.EA[:, ET + q * SO:ET + (q + 1) * SO]
-    far = far_plan(T, topo, hs)
+def helper_program(g, core, T, topo, far):
     qw = [i for i in range(N) if far[i][0] == core][0]
-    near = far[qw][1]
-    for k in range(TR):
-        g.wait_ge(T.sem.ah, len(eng) * (k + 1))
-        g.remote_dma_fused([RemoteDMATransfer(dst_ids=[dst_id(topo, c) for c in others], dma_engine_mask=as_mask(eng),
-                                              remote_sem=T.sem.ae, src=T.XG[:, k * SO:(k + 1) * SO], dsts=[blk] * len(others))],
-                           local_sem=T.sem.le)
-        for raw in (False, True):
-            name, ps, land, rsem, _ = relay_plan(qw, k, raw)
-            g.wait_ge(T.sem[rsem], len(eng) * (k + 1))
-            wd = SO // len(ps)
-            g.remote_dma_fused([RemoteDMATransfer(dst_ids=[dst_id(topo, c) for c in near], dma_engine_mask=as_mask(eng[i::len(ps)]),
-                                                  remote_sem=T.sem[rsem], src=T[land][:, k * SO + i * wd:k * SO + (i + 1) * wd],
-                                                  dsts=[T[name][:, lo:hi]] * len(near)) for i, (lo, hi) in enumerate(ps)],
-                               local_sem=T.sem.le)
-    g.wait_ge(T.sem.le, 3 * TR * len(eng))
+    eng = common_engines(topo, core, far[qw][1] + far[qw][2])
+    seen = {}
+    for t in range(TR):
+        for what in "emwf":
+            for name, cols, way, land, at, rsem, _ in pieces(qw, t, what):
+                if way == "d":
+                    continue
+                to = far[qw][1] + (far[qw][2] if way == "f" else [])
+                seen[rsem] = seen.get(rsem, 0) + len(eng)
+                g.wait_ge(T.sem[rsem], seen[rsem])
+                wd = cols[0][1] - cols[0][0]
+                g.remote_dma_fused([RemoteDMATransfer(dst_ids=[dst_id(topo, c) for c in to], dma_engine_mask=as_mask(eng[i::len(cols)]),
+                                                      remote_sem=T.sem[rsem], src=T[land][:, at + i * wd:at + (i + 1) * wd],
+                                                      dsts=[T[name][:, lo:hi]] * len(to)) for i, (lo, hi) in enumerate(cols)],
+                                   local_sem=T.sem.le)
+    if seen:
+        g.wait_ge(T.sem.le, sum(seen.values()))
 
 
 def rank_program(g, core, T, topo):
     q = T.rank_of(core)
-    hs = helpers(T, topo)
+    far = helpers(T, topo)
     if q is None:
-        if core in hs:
-            helper_program(g, core, T, topo, hs)
+        if core in [f[0] for f in far]:
+            helper_program(g, core, T, topo, far)
         return
     others = [T.cores[(q + d) % N] for d in range(1, N)]
     eng = common_engines(topo, core, others)
@@ -216,6 +211,16 @@ def rank_program(g, core, T, topo):
     def mm(out, l, r, start, stop):
         op("p", out, [l, r], lambda: g.tensor.matmul(out[0], l[0], r[0], start, stop), chain=not start)
 
+    def ident(out, srcs):
+        for i, s in enumerate(srcs):
+            mm(out, R("ID", 0, 128), s, i == 0, i == len(srcs) - 1)
+
+    def move(k, out, a):
+        if k in "pl":
+            ident(out, [a])
+        else:
+            (cp if k == "v" else act)(out, a)
+
     def iota(out, pattern, base, cm, small=True):
         if small:
             op("g", out, [], lambda: g.iota(out[0], pattern, base, cm, allow_small_or_imprecise_dtypes=True))
@@ -247,24 +252,33 @@ def rank_program(g, core, T, topo):
     def send_all(pieces, rsem, lsem):
         send(pieces, others, [[p[0]] * len(others) for p in pieces], rsem, lsem)
 
-    def send_across(t, raw):
-        name, cols, land, rsem, lsem = relay_plan(q, t, raw)
+    def send_piece(t, what, i):
+        name, cols, way, land, at, rsem, lsem = pieces(q, t, what)[i]
         ps = [R(name, lo, hi) for lo, hi in cols]
-        h, _, near = far_plan(T, topo, hs)[q]
-        wd = SO // len(ps)
-        send(ps, [h] + near, [[T[land][:, t * SO + i * wd:t * SO + (i + 1) * wd]] + [p[0]] * len(near) for i, p in enumerate(ps)], rsem, lsem)
+        if way == "d":
+            return send_all(ps, rsem, lsem)
+        near = far[q][2] if way == "a" else []
+        wd = cols[0][1] - cols[0][0]
+        send(ps, [far[q][0]] + near, [[T[land][:, at + j * wd:at + (j + 1) * wd]] + [p[0]] * len(near) for j, p in enumerate(ps)], rsem, lsem)
 
-    def send_e(k):
-        send([eown("EA")], [hs[q]], [[T.XG[:, k * SO:(k + 1) * SO]]], "ah", "le")
+    def send_block(t, what):
+        for i in range(len(pieces(q, t, what))):
+            send_piece(t, what, i)
 
     def arrive(name, base, width, sem, calls=1):
         total[sem] += (N - 1) * NE * calls
         note("x", [], [(name, base + r * width, base + (r + 1) * width) for r in range(N) if r != q], sem, total[sem])
 
+    def arrive_block(t, what):
+        for i, mine in enumerate(pieces(q, t, what)):
+            total[mine[5]] += (N - 1) * NE
+            note("x", [], [(mine[0], lo, hi) for r in range(N) if r != q for lo, hi in pieces(r, t, what)[i][1]], mine[5], total[mine[5]])
+
     def extract(bank, z, src, lo, n, last=True):
         for r in range(16):
             mm(R("PS", 512 * bank, 512 * bank + n), R(z, 16 - r, 144 - r), R(src, lo + r, lo + 16 * n, 16), r == 0, last and r == 15)
 
+    C0 = OPT["c0"]
     cown = R("CT", q * SO, (q + 1) * SO)
     ctab = R("CT", 0, 2048)
     lvtab = R("LV", 0, 2048)
@@ -274,16 +288,27 @@ def rank_program(g, core, T, topo):
     col = lambda i: R("COL", i, i + 1)
     eown = lambda b, lo=0, hi=SO: R(b, ET + q * SO + lo, ET + q * SO + hi)
     etab = lambda b: R(b, ET, ET + 2048)
-    egat = lambda b, lo, hi: G(etab(b), R("OT16", lo // 16, hi // 16))
-    mgat = lambda lo, hi: G(mtab, R("RX16", lo // 16, hi // 16))
+    rxl = lambda lo, hi: R("L16", lo // 16, hi // 16)
+    egat = lambda b, lo, hi: G(etab(b), R("L16", 256 + lo // 16, 256 + hi // 16))
+    mgat = lambda lo, hi: G(mtab, rxl(lo, hi))
     wm = lambda a, b: R("WM", q * RO + 256 * a, q * RO + 256 * b)
 
-    def live():
-        for h in range(2):
+    def live_count(h, ahead=False):
+        if ahead:
+            tt(R("FL", 256 * h, 256 * h + 256), G(R("EB", 0, 6144), R("OE16", 16 * h, 16 * h + 16)), R("TH", 256 * h, 256 * h + 256), A.is_ge)
+        else:
             ts(R("FL", 256 * h, 256 * h + 256), eown("EA", 256 * h, 256 * h + 256), 0.125, A.is_ge)
-            mm(R("PS", 1024 + 512 * h, 1280 + 512 * h), R("MX", 0, 128), R("FL", 256 * h, 256 * h + 256), True, True)
-        for h in range(2):
-            ts(R("LV", q * SO + 256 * h, q * SO + 256 * h + 256), R("PS", 1024 + 512 * h, 1280 + 512 * h), 24.0, A.is_ge)
+        mm(R("PS", 2048 + 512 * h, 2304 + 512 * h), R("MX", 0, 128), R("FL", 256 * h, 256 * h + 256), True, True)
+
+    def live_bound(h):
+        out, a = R("LV", q * SO + 256 * h, q * SO + 256 * h + 256), R("PS", 2048 + 512 * h, 2304 + 512 * h)
+        op("s", out, [a, col(8)], lambda: g.scalar.activation(out[0], a[0], F.Sign, bias=col(8)[0]))
+
+    def counts(bank, src, lo, n, at):
+        out = R("PS", 512 * bank, 512 * bank + n)
+        extract(bank, "Z2", src, lo, n, last=False)
+        mm(out, R("ONE", 0, 128), R("HB", at, at + n), False, False)
+        mm(out, R("RH", 0, 128), R("ONE", 0, n), False, True)
 
     def picks_count(t):
         p = (128 * t) % SO
@@ -291,45 +316,53 @@ def rank_program(g, core, T, topo):
         if p:
             cp(R("CAR", 0, 1), R("SCL", SO - 1, SO))
             scan(R("SCL", 0, p), R("TY", 0, p), R("LV", q * SO, q * SO + p), R("CAR", 0, 1), A.mult, A.add)
-        extract(4, "Z2", "SCL", 0, 32)
+        counts(6, "SCL", 0, 32, 32 - 8 * (t % 4))
 
-    def picks_slots(t, between=(list, list)):
-        y = R("PS", 2048, 2080)
+    def picks_slots(t, between=(list, list, list)):
+        y = R("PS", 3072, 3104)
         x0 = 32 - 8 * (t % 4)
-        ts(sm(0), y, 192.0 - 2047.0, A.is_ge, 192.0, A.mult)
         tt(sm(1), R("KT", x0, x0 + 32), y, A.subtract)
-        tt(sm(2), sm(0), y, A.add)
+        ts(sm(0), y, 192.0 - 2047.0, A.is_ge, 192.0, A.mult)
         ts(sm(3), sm(1), 256.0 - 2047.0, A.is_ge, 512.0, A.mult)
-        between[0]()
+        tt(sm(2), sm(0), y, A.add)
         tt(sm(4), sm(3), sm(1), A.add)
-        between[1]()
+        between[0]()
         tt(sm(5), sm(2), sm(4), A.min)
+        between[1]()
         ts(R("SL16", 0, 32), sm(5), 2047.0, A.add)
 
-    def picks_scatter():
-        cp(G(R("PK", 0, 1216), R("SL16", 0, 32)), R("PKD", 0, SO))
+    def slots_clear():
+        out, a = R("INV", 0, 256), R("POS", 0, 256)
+        op("s", out, [a], lambda: g.scalar.activation(out[0], a[0], F.Silu if OPT["clr"] else F.Copy, scale=4.0))
 
-    def picks_lists():
-        ts(R("O32", 0, 256), R("PK", 0, 256), 4095, A.bitwise_and)
-        ts(R("RX16", 0, 256), R("PK", 0, 256), 1.0 / 4096, A.mult)
-        cp(R("OT16", 0, 256), R("O32", 0, 256))
+    def picks_scatter(t):
+        p = (128 * t) % SO
+        out, a = G(R("INV", 0, 1216), R("SL16", 0, 32)), R("POS", SO - p, 2 * SO - p)
+        op("s", out, [a], lambda: g.scalar.activation(out[0], a[0], F.Silu))
 
-    def back_1():
-        ts(sm(6), sm(5), 16.0, A.mult, 2047.0 * 16 + 15, A.add)
-        ts(sm(8), sm(5), 256.0 - 2047.0, A.is_ge, 512.0, A.mult)
-        tt(sm(7), sm(6), R("YE", 0, 32), A.min)
-        tt(sm(9), sm(8), R("JF", 0, 32), A.max)
+    def picks_extract():
+        scan(R("IH", 0, 256), R("PM", 0, 256), R("INV", 0, 256), 0.0, A.max, A.min)
 
-    def back_2():
-        cp(R("OU16", 0, 32), sm(9))
-        cp(R("OE16", 0, 32), sm(7))
-        ts(R("OD16", 0, 32), sm(5), 2047.0, A.add, 192.0, A.min)
+    def picks_inv():
+        ts(R("IV16", 0, 16), R("IH", 15, 256, 16), -1024.0, A.add, 511.0, A.min)
 
-    def tau_picked():
-        act(R("TE", 0, SO), G(R("TAU", 0, 528), R("OU16", 0, 32)))
+    def picks_lists(t, h):
+        p = (128 * t) % SO
+        cp(R("L16", 256 * h, 256 * h + 256), G(R("LI", 1024 * h + p, 1024 * h + p + 512), R("IV16", 0, 16)))
+
+    def back(i):
+        if i == 0:
+            ts(sm(6), sm(5), 16.0, A.mult, 2047.0 * 16 + 15, A.add)
+            ts(sm(7), sm(5), 256.0 - 2047.0, A.is_lt, 1024.0, A.mult)
+        elif i == 1:
+            tt(R("SM", 256, 320), R("SM", 192, 256), R("YE", 0, 64), A.min)
+        else:
+            cp(R("OE16", 0, 64), R("SM", 256, 320))
+
+    def tau_picked(k):
+        move(k, R("TE", 0, SO), G(R("TAU", 0, 528), R("OE16", 32, 64)))
 
     def rate_pre(lo, hi):
-        act(R("PS", lo, hi), R("KK", lo, hi))
         act(R("TT", lo, hi), G(ctab, R("A16", lo // 16, hi // 16)))
         act(R("CB", lo, hi), G(ctab, R("B16", lo // 16, hi // 16)))
 
@@ -346,172 +379,277 @@ def rank_program(g, core, T, topo):
         tt(eown(dst, lo, hi), G(R(src, 0, 6144), R("OE16", lo // 16, hi // 16)), R("TE", lo, hi), A.max)
 
     def rates(t, wn, wo):
-        send_all([R("LV", q * SO, (q + 1) * SO)], "al", "ll")
-        send_e(t)
-        picks_count(t)
+        if "w" in OPT["tail"]:
+            send_block(t, "e")
         for k in "vs":
             need(k, "lw")
             need(k, "lx")
-        halves = [half_cols(0, t, 0), half_cols(0, t + 2, 0)]
-        for a, b in halves[0]:
-            rate_1(a, b)
-        picks_slots(t, [lambda: [rate_2(a, b, wo + 4096) for a, b in halves[0]], lambda: [rate_1(a, b) for a, b in halves[1]]])
-        picks_scatter()
-        arrive("LV", 0, SO, "al")
-        nq = [(k + t) % 4 for k in range(4)]
+        arrive_block(t, "l")
         x0 = 16 * (t % 4)
         win = R("BIG", wo + q * RO, wo + 5120)
-        for k in range(4):
-            act(R("LA", 256 * k, 256 * k + 256), G(lvtab, R("A16", 16 * nq[k], 16 * nq[k] + 16)))
-            tt(R("ACT", 256 * k, 256 * k + 256), G(lvtab, R("B16", 16 * nq[k], 16 * nq[k] + 16)), R("LA", 256 * k, 256 * k + 256), A.max)
-            if k == 1:
-                extract(5, "Z1", "ACT", 0, 32, last=False)
-                mm(R("PS", 2560, 2592), R("ONE", 0, 128), R("JB", x0, x0 + 32), False, True)
 
-        def select(half):
-            c = 32 * half
-            for (a, b), (x, y) in zip(half_cols(q, t + 2 * half, 0), half_cols(q, t + 2 * half, wn)):
-                src = G(win, R("SEL", c, c + (b - a) // 16))
-                ts(R("WM", a, b), src, 1.0, A.min)
-                act(R("BIG", x, y), src)
-                c += (b - a) // 16
+        plan = OPT["m"]
+        at = lambda i: R("PS", 2048 + 512 * i, 2048 + 512 * i + (plan[i][1] - plan[i][0]) // 16)
+        state = [0, 0]
 
-        ts(R("SEL", 0, 32), R("PS", 2560, 2592), col(2), A.add)
-        select(0)
-        send_across(t, False)
-        scan(R("SC", 0, RO), R("TY", 0, RO), R("ACT", 0, RO), 0.0, A.mult, A.add)
-        extract(6, "Z2", "SC", 512, 32)
-        for a, b in halves[1]:
-            rate_2(a, b, wo + 4096)
-        ts(sm(10), R("PS", 3072, 3104), 512.0 - 2048.0, A.is_le, delta, A.mult)
-        tt(sm(11), sm(10), R("JF", x0 + 32, x0 + 64), A.add)
-        cp(R("SEL", 32, 64), sm(11))
-        select(1)
-        send_all([R("WM", a, b) for a, b in half_cols(q, t + 2, 0)], "aw", "lw")
+        def select(a, b, k):
+            for lo, hi in cyclic(256 * t, a, b, RO):
+                src = G(win, R("SEL", a // 16, (a + hi - lo) // 16))
+                if k == "v":
+                    ts(R("WM", q * RO + lo, q * RO + hi), src, 1.0, A.min)
+                else:
+                    act(R("BIG", wn + q * RO + lo, wn + q * RO + hi), src)
+                a += hi - lo
+
+        def look(hi):
+            lo, state[0] = state[0], hi
+            tt(R("ACT", lo, hi), G(lvtab, R("B16", x0 + lo // 16, x0 + hi // 16)), R("LA", lo, hi), A.max)
+            for i, (a, b, _) in enumerate(plan):
+                if lo < b <= hi and b <= 512:
+                    extract(4 + i, "Z1", "ACT", a, (b - a) // 16, last=False)
+                    mm(at(i), R("ONE", 0, 128), R("JB", x0 + a // 16, x0 + b // 16), False, True)
+
+        def count(hi):
+            lo, state[1] = state[1], hi
+            if lo:
+                cp(R("CAR", 0, 1), R("SC", lo - 1, lo))
+            scan(R("SC", lo, hi), R("TY", lo, hi), R("ACT", lo, hi), R("CAR", 0, 1) if lo else 0.0, A.mult, A.add)
+            for i, (a, b, _) in enumerate(plan):
+                if lo < b <= hi and b > 512:
+                    counts(4 + i, "SC", a, (b - a) // 16, 64 + a // 16)
+
+        def offsets(i):
+            a, b = plan[i][0] // 16, plan[i][1] // 16
+            if b <= 32:
+                ts(R("SEL", a, b), at(i), col(7), A.add)
+            else:
+                ts(R("SM", 320 + a, 320 + b), at(i), 512.0 - 2048.0, A.is_le, delta, A.mult)
+                tt(R("SM", 384 + a, 384 + b), R("SM", 320 + a, 320 + b), R("JF", x0 + a, x0 + b), A.add)
+                cp(R("SEL", a, b), R("SM", 384 + a, 384 + b))
+
+        for step in OPT["steps"].split():
+            k, n = step[0], int(step[1:] or 0)
+            if k == "L":
+                cuts = OPT["la"]
+                for lo, hi in zip(cuts, cuts[1:]):
+                    act(R("LA", lo, hi), G(lvtab, R("A16", x0 + lo // 16, x0 + hi // 16)))
+            elif k == "A":
+                cp(R("LA", 0, n), G(lvtab, R("A16", x0, x0 + n // 16)))
+            elif k == "w":
+                writeback("EB", "EA", 0, SO)
+                send_block(t, "e")
+            elif k == "p":
+                picks_scatter(t)
+            elif k == "k":
+                picks_slots(t)
+            elif k == "n":
+                picks_count(t)
+            elif k == "y":
+                rate_1(512 * (n % 2), 512 * n + 512 if n < 2 else RO)
+            elif k == "i":
+                (picks_extract, picks_inv)[n]()
+            elif k == "b":
+                back(n)
+            elif k == "t":
+                tau_picked("sv"[n])
+            elif k == "x":
+                rate_2(512 * (n % 2), 512 * n + 512 if n < 2 else RO, wo + 4096)
+            elif k == "a":
+                look(n)
+            elif k == "c":
+                count(n)
+            elif k == "o":
+                offsets(n)
+            elif k == "s":
+                select(plan[n][0], plan[n][1], "v")
+                send_piece(t, "m", n)
+            elif k == "r":
+                select(plan[n][0], plan[n][1], "s")
+            elif k == "l":
+                picks_lists(t, n)
 
     def first_rates():
         wq = lambda a, b: R("BIG", W0 + q * RO + a, W0 + q * RO + b)
+        move("p", R("PS", 512, 1024), R("KK", 512, 1024))
         arrive("CT", 0, SO, "ac")
         rate_pre(512, 1024)
+        picks_scatter(0)
+        act(R("POS", 0, SO), R("POS", SO, 2 * SO))
         tt(R("TT", 0, 512), G(ctab, R("A16", 0, 32)), R("KK", 0, 512), A.mult)
         tt(wq(0, 512), G(ctab, R("B16", 0, 32)), R("TT", 0, 512), A.mult)
         ts(wm(0, 2), wq(0, 512), 1.0, A.min)
-        send_across(0, False)
+        for i, (a, b, _) in enumerate(OPT["m0"]):
+            if b <= 512:
+                send_piece(0, "m", i)
         rate_1(512, 1024)
         rate_2(512, 1024, W0 + q * RO)
         ts(wm(2, 4), wq(512, 1024), 1.0, A.min)
-        send_all([wm(2, 4)], "aw", "lw")
-        ts(R("PKT", 0, SO), R("RXI", 0, SO), 4096.0, A.mult)
-        need("y", "sv")
-        load("y", R("TAU", 0, SO), T.tau[:], "ldt")
-        tt(R("PKD", 0, SO), R("PKT", 0, SO), R("OTI", 0, SO), A.add)
-        picks_scatter()
+        for i, (a, b, _) in enumerate(OPT["m0"]):
+            if b > 512:
+                send_piece(0, "m", i)
+        ts(R("PM", 0, 256), R("RM", 0, 256), col(2), A.is_equal, 8192.0, A.mult)
+        picks_extract()
+        picks_inv()
+        for h in (1, 0):
+            picks_lists(0, h)
+        for h in range(2):
+            cp(R("LI", 1024 * h + 512, 1024 * h + 896), R("LI", 1024 * h, 1024 * h + 384))
 
-    def amounts(t):
-        for c in range(3):
-            lo, hi = 1024 * c, 1024 * c + 1024
-            tt(R("PS", 256 * c, 256 * c + 256), R("XG", lo, hi, 4), R("XG", lo + 1, hi, 4), A.add)
-            tt(R("L1", 256 * c, 256 * c + 256), R("XG", lo + 2, hi, 4), R("XG", lo + 3, hi, 4), A.add)
-        tt(R("L2", 0, 384), R("L1", 1, 768, 2), R("PS", 1, 768, 2), A.add)
-        tt(R("PS", 0, 768, 2), R("PS", 0, 768, 2), R("L1", 0, 768, 2), A.add)
-        tt(R("L3", 0, 192), R("PS", 2, 768, 4), R("L2", 1, 384, 2), A.add)
-        tt(R("PS", 0, 768, 4), R("PS", 0, 768, 4), R("L2", 0, 384, 2), A.add)
-        tt(R("DD", 0, 192), R("PS", 0, 768, 4), R("L3", 0, 192), A.subtract)
-        tt(R("CN", 0, SO), G(R("DD", 0, 200), R("OD16", 0, 32)), cown, A.add)
-        ts(cown, R("CN", 0, SO), 0.125, A.max, 8.0, A.min)
+    def amounts(t, wn):
+        ps = lambda lo, hi, step=1: R("PS", 1024 + lo, 1024 + hi, step)
+        x = lambda e, lo, hi: R("XG", lo + e, hi, 4)
+        wtab = R("BIG", wn, wn + 4096)
+        cuts = OPT["xg"]
+        for lo, hi in zip(cuts, cuts[1:]):
+            act(R("XG", lo, hi), G(wtab, rxl(lo, hi)), 0.125)
+            if hi <= OPT["treeA"]:
+                ident(ps(lo // 4, hi // 4), [x(0, lo, hi), x(1, lo, hi)])
+        if cuts[-1] < 3072:
+            ts(R("XG", cuts[-1], 3072), G(wtab, rxl(cuts[-1], 3072)), 0.125, A.mult)
+        act(R("MG", 0, C0), mgat(0, C0))
+        cuts = OPT["tb"]
+        for lo, hi in zip(cuts, cuts[1:]):
+            tt(R("L1", lo // 4, hi // 4), x(2, lo, hi), x(3, lo, hi), A.add)
+            lo = max(lo, OPT["treeA"])
+            if lo < hi:
+                tt(ps(lo // 4, hi // 4), x(0, lo, hi), x(1, lo, hi), A.add)
+        tt(R("L2", 0, 384), R("L1", 1, 768, 2), ps(1, 768, 2), A.add)
+        tt(ps(0, 768, 2), ps(0, 768, 2), R("L1", 0, 768, 2), A.add)
+        tt(R("L3", 0, 192), ps(2, 768, 4), R("L2", 1, 384, 2), A.add)
+        tt(ps(0, 768, 4), ps(0, 768, 4), R("L2", 0, 384, 2), A.add)
+        tt(R("DD", 0, 192), ps(0, 768, 4), R("L3", 0, 192), A.subtract)
+
+    def amounts_out(t):
+        tt(R("CB", 0, SO), G(R("DD", 0, 1216), R("SL16", 0, 32)), cown, A.add)
+        ts(cown, R("CB", 0, SO), 0.125, A.max, 8.0, A.min)
         if t < TR - 1:
             send_all([cown], "ac", "lc")
         else:
             store("y", T.yc[:], cown)
 
     def sweeps(t, wn):
-        send_across(t, True)
-        send_all([R("BIG", wn + q * RO + 512, wn + (q + 1) * RO)], "ax", "lx")
-        picks_lists()
-        if t:
-            back_1()
-            back_2()
-        arrive("EA", ET, SO, "ae")
-        pre, ca, ch1 = (PRE, CA, CH1) if t else (PRE0, CA0, CH10)
-        for lo, hi, k in pre:
-            (cp if k == "v" else act)(R("EG", lo, hi), egat("EA", lo, hi))
-        act(R("TT", 0, C0), egat("EA", 0, C0))
-        for lo, hi, k in sorted(pre, key=lambda x: x[2] != "v"):
-            cp(R("PS", lo, hi), R("EG", lo, hi))
+        send_block(t, "w")
+        arrive_block(t, "e")
 
-        arrive("WM", 0, RO, "aw", calls=2)
-        nc = len(ch1) - 1
-        for c in range(nc):
-            lo, hi = ch1[c], ch1[c + 1]
-            if c == 0:
-                tt(R("EG", lo, hi), mgat(lo, hi), R("TT", lo, hi), A.mult)
-                maxscan("EA", lo, hi)
-                continue
-            act(R("MG", lo, hi), mgat(lo, hi))
-            if hi <= ca:
-                tt(R("EG", lo, hi), R("MG", lo, hi), R("PS", lo, hi), A.mult)
+        def to_psum(k, name, lo, hi):
+            if k in "pl":
+                for x in range(lo // 512 * 512, hi, 512):
+                    move(k, R("PS", max(x, lo), min(x + 512, hi)), R(name, max(x, lo), min(x + 512, hi)))
             else:
-                tt(R("EG", lo, hi), egat("EA", lo, hi), R("MG", lo, hi), A.mult)
-            if c >= 2:
-                maxscan("EA", ch1[c - 1], lo)
-        tau_picked()
-        maxscan("EA", ch1[nc - 1], ch1[nc])
-        writeback("EA", "EB", 0, SO)
-        send_all([eown("EB")], "af", "lf")
+                move(k, R("PS", lo, hi), R(name, lo, hi))
 
-        arrive("BIG", wn, RO, "ax", calls=2)
-        if t == TR - 1:
-            need("y", "ax")
-            store("y", T.yw[:], R("BIG", wn + q * RO, wn + (q + 1) * RO))
-        for c in range(3):
-            act(R("XG", 1024 * c, 1024 * c + 1024), G(R("BIG", wn, wn + 4096), R("RX16", 64 * c, 64 * c + 64)), 0.125)
-        act(R("MG", 0, C0), mgat(0, C0))
-        for lo in range(F2, 4096, 1024):
-            act(R("PS", lo, lo + 1024), R("MG", lo, lo + 1024))
-        amounts(t)
+        if OPT["tau"] != "b" or t == 0:
+            tau_picked(OPT["tau"] if t else "v")
+        if "h" in OPT["tail"] and t < TR - 1:
+            ts(R("TH", 0, SO), R("TE", 0, SO), 0.125, A.is_lt, 0.125, A.mult)
+        pre = OPT["pre"] if t else OPT["pre0"]
+        move(OPT["ez"], R("TT", 0, C0), egat("EA", 0, C0))
+        for lo, hi, k, c in pre:
+            move(k, R("EG", lo, hi), egat("EA", lo, hi))
+            if c == "p":
+                to_psum(c, "EG", lo, hi)
+        for lo, hi, k, c in pre:
+            if c != "p":
+                to_psum(c, "EG", lo, hi)
+        ready = [p[:2] for p in pre]
 
-        arrive("EB", ET, SO, "af")
-        nc = len(CH2) - 1
-        for c in range(nc + 1):
-            if c < nc:
-                lo, hi = CH2[c], CH2[c + 1]
-                if hi <= F2:
-                    tt(R("EG", lo, hi), egat("EB", lo, hi), R("MG", lo, hi), A.mult)
+        arrive_block(t, "m")
+        tt(R("EG", 0, C0), mgat(0, C0), R("TT", 0, C0), A.mult)
+        for step in OPT["s1"].split():
+            k, lo, hi = step[0], *[OPT["unit"] * int(x, 17) for x in (step[1:] + "0")[:2]]
+            if k == "m":
+                act(R("MG", lo, hi), mgat(lo, hi))
+                if not any(a <= lo and hi <= b for a, b in ready):
+                    tt(R("EG", lo, hi), egat("EA", lo, hi), R("MG", lo, hi), A.mult)
                 else:
-                    act(R("EG", lo, hi), egat("EB", lo, hi))
-                    tt(R("EG", lo, hi), R("EG", lo, hi), R("PS", lo, hi), A.mult)
-            if c >= 1:
-                maxscan("EB", CH2[c - 1], CH2[c])
+                    tt(R("EG", lo, hi), R("MG", lo, hi), R("PS", lo, hi), A.mult)
+                for a, b, c in OPT["cpm"]:
+                    if c == "p" and lo < b <= hi:
+                        to_psum(c, "MG", a, b)
+            elif k == "s":
+                maxscan("EA", lo, hi)
+            else:
+                i = lo // OPT["unit"]
+                for a, b in cyclic(128 * t, OPT["f"][i][0], OPT["f"][i][1], SO):
+                    writeback("EA", "EB", a, b)
+                send_piece(t, "f", i)
+
+        if OPT["kat"] == "s1" and t < TR - 1:
+            to_psum(OPT["kcp"], "KK", 0, RO)
+        arrive_block(t, "w")
+        if t == TR - 1:
+            for p in pieces(q, t, "w"):
+                need("y", p[5])
+            store("y", T.yw[:], R("BIG", wn + q * RO, wn + (q + 1) * RO))
+        amounts(t, wn)
+        for a, b, k in OPT["cpm"]:
+            if k != "p":
+                to_psum(k, "MG", a, b)
+        if OPT["cout"] < 0:
+            amounts_out(t)
+
+        arrive_block(t, "f")
+        tt(R("EG", 0, C0), egat("EB", 0, C0), R("MG", 0, C0), A.mult)
+        behind = [(0, C0)]
+        if OPT["first2"]:
+            maxscan("EB", 0, C0)
+            behind = []
+        for i, (lo, hi) in enumerate(OPT["s2"]):
+            act(R("EG", lo, hi), egat("EB", lo, hi))
+            if i == OPT["cout"]:
+                amounts_out(t)
+            tt(R("EG", lo, hi), R("EG", lo, hi), R("PS", lo, hi), A.mult)
+            if i in OPT["own2"]:
+                behind = [(behind[0][0], hi)] if behind and behind[0][1] == lo else behind + [(lo, hi)]
+            for a, b in behind:
+                maxscan("EB", a, b)
+            behind = [] if i in OPT["own2"] else [(lo, hi)]
+        for a, b in behind:
+            maxscan("EB", a, b)
         if t < TR - 1:
+            if OPT["kat"] == "s2":
+                to_psum(OPT["kcp"], "KK", 0, RO)
             arrive("CT", 0, SO, "ac")
             rate_pre(0, RO)
-        writeback("EB", "EA", 0, 256)
-        writeback("EB", "EA", 256, 512)
-        if t < TR - 1:
-            live()
-        else:
-            store("y", T.ye[:, 0:256], eown("EA", 0, 256))
-            store("s", T.ye[:, 256:512], eown("EA", 256, 512))
+            slots_clear()
+        for k, h in (OPT["tail"] if t < TR - 1 else "w0 w1").split():
+            h = int(h)
+            if k == "w" and h == 2:
+                writeback("EB", "EA", 0, SO)
+            elif k == "w":
+                writeback("EB", "EA", 256 * h, 256 * h + 256)
+                if t == TR - 1:
+                    store("ys"[h], T.ye[:, 256 * h:256 * h + 256], eown("EA", 256 * h, 256 * h + 256))
+            elif k in "gh":
+                live_count(h, k == "h")
+            elif t < TR - 1:
+                live_bound(h)
+                for i, (a, b, _) in enumerate(OPT["l"]):
+                    if b == 256 * h + 256:
+                        send_piece(t + 1, "l", i)
 
-    load("y", cown, T.cin[:], "ldc")
-    load("y", eown("EA"), T.ein[:], "lde")
-    load("y", R("RAI", 0, 64), T.ra[:], "ldl")
-    load("y", R("RBI", 0, 64), T.rb[:], "ldl")
-    load("y", R("KK", 0, RO), T.kin[:], "ldk")
+    loads = {"c": (cown, T.cin[:], "ldc"), "e": (eown("EA"), T.ein[:], "lde"), "a": (R("RAI", 0, 64), T.ra[:], "ldl"),
+             "b": (R("RBI", 0, 64), T.rb[:], "ldl"), "k": (R("KK", 0, RO), T.kin[:], "ldk"), "o": (R("LI", 1024, 1536), T.ot[:], "ldo"),
+             "r": (R("LI", 0, SO), T.rx[:], "ldx"), "t": (R("TAU", 16, 528), T.tau[:], "ldt")}
+    early, late = OPT["loads"].split()
+    for k in early:
+        load("y", *loads[k])
     iota(R("PI", 0, 2), [[112, 2]], 0, 1, small=False)
     iota(R("I2", 0, 128), [[1, 8], [0, 16]], 0, 0)
     iota(R("I1", 0, 144), [[1, 144]], -16, -1)
     iota(R("I3", 0, 64), [[0, 2], [16, 32]], 192 - 2047, 0)
     iota(R("JB", 0, 128), [[0, 2], [16, 64]], 0, 0)
+    iota(R("I4", 0, 128), [[0, 8], [1, 16]], 1, 0)
     send_all([cown], "ac", "lc")
-    send_e(0)
-    iota(R("PK", 0, 1216), [[0, 1216]], 0, 0, small=False)
+    send_block(0, "e")
+    iota(R("POS", SO, 2 * SO), [[1, SO]], 1024, 0)
     iota(R("RM", 0, 1024), [[0, 64], [1, 16]], 0, 0)
     need("y", "lc")
-    load("y", R("RXI", 0, SO), T.rx[:], "ldx")
-    load("y", R("OTI", 0, SO), T.ot[:], "ldx")
+    for k in late:
+        load("y", *loads[k])
 
     fill(R("TY", 0, 1024), 1.0)
+    fill(R("INV", 0, 1216), 4096.0)
     ts(R("PJ", 0, 2), R("PI", 0, 2), 4, A.arith_shift_right, 7, A.bitwise_and)
     ts(R("PJ", 2, 3), R("PI", 0, 1), 15, A.bitwise_and)
     cp(R("COL", 0, 3), R("PJ", 0, 3))
@@ -519,26 +657,37 @@ def rank_program(g, core, T, topo):
     ts(R("M1", 0, 128), R("I2", 0, 128), col(1), A.is_equal)
     ts(col(4), col(2), 0.0, A.is_equal)
     ts(col(5), col(2), 1.0, A.is_equal, -2048.0, A.mult)
+    ts(col(7), col(2), delta / 2, A.add)
+    fill(col(8), -23.5)
     ts(col(6), col(2), 1.0, A.not_equal)
     tt(R("MX", 0, 128), R("M0", 0, 128), R("M1", 0, 128), A.add)
     ts(R("TY", 0, 1024), R("TY", 0, 1024), col(6), A.mult)
     ts(R("M0", 0, 144), R("I1", 0, 144), 0.0, A.is_equal, col(4), A.mult)
     ts(R("M1", 0, 144), R("I1", 0, 144), -1.0, A.is_equal, col(5), A.mult)
-    live()
-    tt(R("Z2", 0, 144), R("M0", 0, 144), R("M1", 0, 144), A.add)
+    ts(R("ID", 0, 128), R("I1", 16, 144), 0.0, A.is_equal)
+    tt(R("M1", 0, 144), R("M0", 0, 144), R("M1", 0, 144), A.add)
     ts(R("KT", 0, 64), R("I3", 0, 64), col(2), A.add)
-    picks_count(0)
-    ts(R("Z1", 0, 144), R("M0", 0, 144), delta, A.mult)
+    ts(R("Z2", 0, 144), R("M1", 0, 144), 0.5, A.mult)
+    ts(R("Z1", 0, 144), R("M0", 0, 144), delta / 2, A.mult)
+    ts(R("RH", 0, 128), R("I4", 0, 128), 0.5, A.mult)
+    ts(R("HB", 0, 64), R("I3", 0, 64), 2047.0 - 192 - 2048, A.add, 0.5, A.mult)
+    ts(R("HB", 64, 128), R("JB", 0, 64), -2048.0, A.add, 0.5, A.mult)
     ts(R("JF", 0, 128), R("JB", 0, 128), col(2), A.add)
-    cp(R("A16", 0, 64), R("RAI", 0, 64))
-    cp(R("B16", 0, 64), R("RBI", 0, 64))
     fill(R("ONE", 0, 128), 1.0 / 128)
-    fill(R("DD", 0, 200), 0.0)
-    fill(R("TAU", 512, 528), 0.0)
+    fill(R("TAU", 0, 16), 0.0)
+    for f in (live_count, live_bound):
+        for h in range(2):
+            f(h)
+    picks_count(0)
+    for h in range(2):
+        cp(R("A16", 64 * h, 64 * h + 64), R("RAI", 0, 64))
+        cp(R("B16", 64 * h, 64 * h + 64), R("RBI", 0, 64))
     ts(R("YE", 0, 32), R("JF", 0, 32), float(ET + SO * q), A.add)
+    ts(R("YE", 32, 64), R("JF", 0, 32), 16.0, A.add)
     picks_slots(0)
-    back_1()
-    back_2()
+    for i in range(3):
+        back(i)
+    fill(R("DD", 0, 1216), 0.0)
 
     for t in range(TR):
         wn, wo = (W0, W1) if t % 2 == 0 else (W1, W0)

@@ -4,48 +4,102 @@ from concourse.mybir import AluOpType as A, ActivationFunctionType as F
 N, SO, RO, TR = 4, 512, 1024, 5
 W0, W1 = 0, 5120
 ET = 4096
-OPT = dict(clr=1, unit=512, c0=512, first2=False, kat="s2",
-           pre=[(2048, 3072, "s", "p"), (1024, 2048, "v", "v")],
-           pre0=[(2048, 3072, "s", "p"), (1024, 2048, "v", "v")],
-           cpm=[(512, 1024, "p"), (2048, 3072, "s"), (3072, 4096, "l"), (1024, 2048, "l")],
-           s1="m12 s02 m24 m46 s24 m68 s46 s68 w0", f=[(0, 512, "d")],
-           l=[(0, 512, "d")], tail="w0 w1 g0 g1 t0 t1", s2=[(512, 1024), (2048, 3072), (3072, 4096), (1024, 2048)], own2=[],
-           ez="s", tau="b", la=[0, 256, 512, 768, 1024],
-           xg=[0, 1024, 2048, 3072], tb=[0, 2048, 3072], treeA=2048, wb=[0, 256, 512], ge=[0, 256, 512], th=2,
-           kcp="p", invk=-1, fill=0, cout=-1, loads="ceabko rt", wrot=0,
-           e=[(0, 512, "a")], m=[(0, 512, "a"), (512, 1024, "d")], w=[(0, 512, "a"), (512, 1024, "d")],
-           m0=[(0, 512, "a"), (512, 1024, "d")], w0=[(0, 512, "a"), (512, 1024, "d")], e0=[(0, 512, "a")],
-           steps="y2 n x2 k L p a256 a512 a768 a1024 o0 c1024 s0 r0 o1 s1 r1 i0 b0 i1 b1 l1 b2 l0 t1")
+U = 256
+OPT = dict(
+    bb=2048, war=0, tb=(0, 1), join=0, more0="", tree=8, slot=0, fold=0, wide="", k8="",
+    round="se r104 pc r204 ps aL Ls01 Ls12 Ls23 Ls34 px lk01 lk12 lk23 lk34 o0 ct mv02 M0 ws02 o1 mv24 M1 ws24 pi b0 pj b1 lo b2 lr tv "
+          "W_ aE Fs02 Es8c Ev48 Cp8c Cv48 aM P_02 ms24 P_24 Dp24 z_04 ms48 P_48 ms8c P_8c z_48 mscg P_cg z_8c z_cg w1 "
+          "aW Xs04 Xs48 Xs8c ms02 T108 T18c T2 T3 Ds8c Dpcg Dp48 ao "
+          "aF Q_02 es24 Q_24 Z_02 es8c Q_8c Z_24 escg Q_cg Z_8c es48 Q_48 Z_cg Z_48 Kp04 aC Ra04 Rb04 cl w20 w21 g_0 g_1 t_0 t_1", loads="ceabko rt",
+    e="a", m="ad", w="ad", f="d", l="d", e0="a", m0="ad", w0="ad",
+    rates="se r104 pc r204 ps aL Ls01 Ls12 Ls23 Ls34 px lk01 lk12 lk23 lk34 o0 ct mv02 M0 ws02 o1 mv24 M1 ws24 pi b0 pj b1 lo b2 lr tv",
+    ahead="W_ aE Fs02 Es8c Ev48 Cp8c Cv48",
+    first="W_ aE tv Fs02 Es8c Ev48 Cp8c Cv48",
+    one="aM P_02 ms24 P_24 Dp24 z_04 ms48 P_48 ms8c P_8c z_48 mscg P_cg z_8c z_cg w1",
+    amounts="aW Xs04 Xs48 Xs8c ms02 T108 T18c T2 T3 Ds8c Dpcg Dp48 ao",
+    two="aF Q_02 es24 Q_24 Z_02 es8c Q_8c Z_24 escg Q_cg Z_8c es48 Q_48 Z_cg Z_48",
+    next="Kp04 aC Ra04 Rb04 cl",
+    tail="w20 w21 g_0 g_1 t_0 t_1")
 
+OPT.update(slot=1, m="dd", m0="dd", e0="d", e="d", w="dd", w0="dd", wide="1", loads="ceabkort|", k8="W_", more0="Es48 Cv48",
+           round="se r104 pc r204 ps aL Ls01 Ls12 Ls23 Ls34 px lk01 lk12 lk23 lk34 ct o0 mv02 M0 "
+                 "ws02 o1 mv24 M1 ws24 pi pj lo aE Fs02 Es8c Cp8c lr b0 b1 b2 tv W_ "
+                 "aM P_02 ms24 P_24 Dp24 ms48 z_04 P_48 ms8c P_8c mscg z_4c P_cg z_cg w1 "
+                 "aW Xs04 Xs48 Xs8c ms02 Ds8c cs T108 Dpcg T18c T2 T3 T4 Dp48 "
+                 "aF Q_02 es24 Q_24 es8c Z_04 Q_8c cw escg Z_8c Q_cg es48 Z_cg Q_48 Z_48 Kp04 aC Ra04 Rb04 cl "
+                 "w20 w21 g_0 g_1 t_0 t_1")
+OPT.update(slot=0, m="ad", m0="ad", e0="a", e="a", w="ad", w0="ad", wide="", k8="", tree=12,
+           round="se r104 pc r204 ps aL Ls01 Ls12 Ls23 Ls34 px lk01 lk12 lk23 lk34 o0 ct mv02 M0 ws02 o1 mv24 M1 ws24 pi b0 pj b1 lo b2 lr tv "
+                 "W_ aE Fs02 Es8c Cp8c aM P_02 ms24 P_24 Dp24 z_04 ms48 P_48 ms8c P_8c z_48 mscg P_cg z_8c z_cg w1 "
+                 "aW Xs04 Xs48 Xs8c ms02 T108 T18c T2 T3 Ds8c Dpcg Dp48 ao "
+                 "aF Q_02 es24 Q_24 Z_02 es8c Q_8c Z_24 escg Q_cg Z_8c es48 Q_48 Z_cg Z_48 Kp04 aC Ra04 Rb04 cl w20 w21 g_0 g_1 t_0 t_1")
+OPT.update(slot=1, wide="1", k8="W_", more0="Es48 Cv48", tree=8,
+           round="se r104 pc r204 ps aL Ls01 Ls12 Ls23 Ls34 px lk01 lk12 lk23 lk34 ct o0 mv02 M0 "
+                 "ws02 o1 mv24 M1 ws24 pi pj lo aE Fs02 Es8c Cp8c lr b0 b1 b2 tv W_ "
+                 "aM P_02 ms24 P_24 Dp24 ms48 z_04 P_48 ms8c P_8c mscg z_4c P_cg z_cg w1 "
+                 "aW Xs04 Xs48 Xs8c ms02 Ds8c cs T108 Dpcg T18c T2 T3 T4 Dp48 "
+                 "aF Q_02 es24 Q_24 es8c Z_04 Q_8c cw escg Z_8c Q_cg es48 Z_cg Q_48 Z_48 Kp04 aC Ra04 Rb04 cl "
+                 "w20 w21 g_0 g_1 t_0 t_1")
+OPT.update(slot=0, wide="", k8="", m="dd", m0="dd", e0="d", e="d", w="d", w0="d",
+           round="se r104 pc r204 ps aL Ls12 Ls24 px Lv01 lk01 lk12 lk24 o0 ct mv02 M0 "
+                 "ws02 o1 mv24 M1 ws24 pi pj lo aE Fs04 Es8c Cp8c lr b0 b1 b2 tv W_ "
+                 "aM P_04 ms48 z_04 P_48 ms8c P_8c z_48 mscg P_cg z_8c z_cg w1 "
+                 "aW Ys04 Ys48 Ys8c ms04 V1 Dp8c V2 V3 Dp24 Dpcg Dp48 ao "
+                 "aF Q_02 es24 Q_24 Z_02 es8c Q_8c Z_24 escg Q_cg Z_8c es48 Q_48 Z_cg Z_48 Kp04 aC Ra04 Rb04 cl w20 w21 g_0 g_1 t_0 t_1")
+OPT.update(tree=12,
+           round="se r104 pc r204 ps aL Ls12 Ls24 px Lv01 lk01 lk12 lk24 ct o0 mv02 M0 ws02 o1 mv24 M1 ws24 pi pj lo aE Es8c Cp8c lr W_ Fv04 b0 b1 b2 tv "
+                 "aM P_04 ms48 z_04 P_48 cd ms8c P_8c z_48 mscg P_cg z_8c z_cg w1 aW Xs04 Xs48 Xs8c ms04 Ds8c T108 T18c T2 T3 Dpcg Dp48 ao "
+                 "aF Q_04 es8c Q_8c escg Z_04 Q_cg es48 Z_8c Q_48 Z_cg Z_48 Kp04 aC Rs w20 w21 g_0 g_1 t_0 t_1")
+OPT.update(round="se r104 pc r204 ps aL Ls12 Ls24 px Lv01 lk01 lk12 lk24 ct o0 mv02 M0 ws02 o1 mv24 M1 ws24 pi pj lo aE Fs04 Es8c Cp8c lr W_ b0 b1 b2 tv "
+                 "aM P_04 ms48 z_04 P_48 cd ms8c P_8c z_48 mscg P_cg z_8c z_cg w1 aW Xs04 Xs48 Xs8c Bs0c ms04 Dp24 T50c Ds8c T2 T3 Dpcg Dp48 ao "
+                 "aF Q_02 es24 Q_24 Z_02 es8c Q_8c Z_24 escg Q_cg Z_8c es48 Q_48 Z_cg Z_48 Kp04 aC Rs w20 w21 g_0 g_1 t_0 t_1")
+OPT.update(fold=0, wide="1",
+           round="se r104 pc r204 ps aL Ls12 Ls24 px Lv01 lk01 lk12 lk24 ct o0 mv02 M0 ws02 o1 mv24 M1 ws24 pi pj lo aE Fs04 Es8c Cp8c lr b0 b1 b2 tv W_ "
+                 "aM P_04 ms48 z_04 P_48 cd ms8c P_8c z_48 mscg P_cg z_8c z_cg w1 aW Xs04 Xs48 Xs8c ms04 Dp24 T108 T18c Ds8c T2 T3 Dpcg Dp48 ao "
+                 "aF Q_02 es24 Q_24 Z_02 es8c Q_8c Z_24 escg Q_cg Z_8c es48 Q_48 Z_cg Z_48 Kp04 aC Ra04 Rb04 w20 w21 g_0 g_1 t_0 t_1")
+OPT.update(wide="", war=0,
+           round="r104 pc w3 se r204 ps aL Ls12 Ls24 px Lv01 lk01 lk12 lk24 o0 ct mv02 M0 ws02 o1 mv24 M1 ws24 pi pj lo aE Fs04 Es8c Cp8c lr b0 b1 b2 tv th W_ "
+                 "aM P_04 ms48 z_04 P_48 ms8c P_8c z_48 mscg P_cg z_8c z_cg w1 aW Xs04 Xs48 Xs8c Bs0c ms04 Dp24 T50c Ds8c T2 T3 Dpcg Dp48 ao "
+                 "aF Q_02 es24 Q_24 Z_02 es8c Q_8c Z_24 escg Q_cg Z_8c es48 Q_48 Z_cg Z_48 Kp04 aC Ra04 Rb04 cl h_0 h_1 t_0 t_1")
+OPT.update(bb=0, tree=12,
+           round="se r104 pc r204 ps aL Ls02 Ls24 px lk02 lk24 o0 ct mv02 M0 ws02 o1.0 pi o1.1 o1.2 mv24 M1 ws24 pj lo aE Fs04 lr b0 b1 b2 tv W_ "
+                 "aM P_04 ms8c z_04 Dp8c P_8c cd ms48 z_8c P_48 mscg z_48 P_cg z_cg w1 aW As04 As48 As8c Bs0c ms04 T50c Ds24 S2 S5 Dpcg Dp48 ao "
+                 "aF Q_02 es24 Q_24 Z_02 es8c Q_8c Z_24 escg Q_cg Z_8c es48 Q_48 Z_cg Z_48 Kp04 aC Rs w20 w21 g_0 g_1 t_0 t_1")
+OPT.update(k8="W_", more0="Escg Cpcg",
+           round="se r104 pc r204 ps.0 ps.1 ps.2 ps.3 ps.4 ps.5 aL Lv01 ps.6 Ls12 Ls24 px lk01 lk12 lk24 o0 ct mv02 M0 ws02 o1.0 b0 o1.1 b1 o1.2 b2 mv24 M1 ws24 "
+                 "ts pi pj lo aE Fs24 lr W_ Fv02 Ev45 Cp45 "
+                 "aM P_04 ms8c Dp8c P_8c cd ms48 z_04 P_58 P_45 mscg z_8c P_cg z_48 z_cg w1 aW As04 As48 As8c Bs0c ms04 T50c Ds24 S2 S5 Dpcg Dp48 ao.0 "
+                 "aF Q_02 ao.1 es24 Q_24 Z_02 es8c Q_8c Z_24 escg Q_cg Z_8c es48 Q_48 Z_cg Z_48 Kp04 aC Rs w20 w21 g_0 g_1 t_0 t_1")
 f32, bf, f16, i32, u16 = "float32", "bfloat16", "float16", "int32", "uint16"
 SCRATCH = {
     "BIG": ("sbuf", [128, 10240], f32), "EA": ("sbuf", [128, 6144], f32), "EB": ("sbuf", [128, 6144], f32),
     "WM": ("sbuf", [128, 4096], f32), "MG": ("sbuf", [128, 4096], f32),
     "CT": ("sbuf", [128, 2048], f32), "LV": ("sbuf", [128, 2048], bf),
-    "XG": ("sbuf", [128, 3072], f32), "EG": ("sbuf", [128, 4096], f32), "RM": ("sbuf", [128, 1024], f32),
-    "KK": ("sbuf", [128, 1024], f32), "TT": ("sbuf", [128, 1024], f32), "CB": ("sbuf", [128, 1024], f32),
-    "TAU": ("sbuf", [128, 528], f32), "TE": ("sbuf", [128, 512], f32), "TH": ("sbuf", [128, 512], f32),
+    "XG": ("sbuf", [128, 6528], f32), "EG": ("sbuf", [128, 4096], f32), "RM": ("sbuf", [128, 2048], bf),
+    "KK": ("sbuf", [128, 1024], f32), "TC": ("sbuf", [128, 2048], f32), "AB16": ("sbuf", [128, 128], u16), "BV": ("sbuf", [128, 256], f32),
+    "TAU": ("sbuf", [128, 528], f32), "TE": ("sbuf", [128, 512], f32), "CN": ("sbuf", [128, 512], f32),
     "RAI": ("sbuf", [128, 64], i32), "RBI": ("sbuf", [128, 64], i32),
     "A16": ("sbuf", [128, 128], u16), "B16": ("sbuf", [128, 128], u16),
-    "LI": ("sbuf", [128, 1920], i32),
+    "LI": ("sbuf", [128, 1920], i32), "ON1": ("sbuf", [128, 512], f32),
     "L16": ("sbuf", [128, 512], u16), "POS": ("sbuf", [128, 1024], f32), "INV": ("sbuf", [128, 1216], f32),
     "IH": ("sbuf", [128, 256], f32), "IV16": ("sbuf", [128, 16], u16), "PM": ("sbuf", [128, 256], f32),
     "LA": ("sbuf", [128, 1024], bf), "ACT": ("sbuf", [128, 1024], bf), "SC": ("sbuf", [128, 1024], f16),
     "TY": ("sbuf", [128, 1024], bf), "SCL": ("sbuf", [128, 512], f16), "CAR": ("sbuf", [128, 8], f32),
-    "FL": ("sbuf", [128, 512], bf), "MX": ("sbuf", [128, 128], bf), "M0": ("sbuf", [128, 144], f32),
-    "M1": ("sbuf", [128, 144], f32), "Z1": ("sbuf", [128, 144], bf), "Z2": ("sbuf", [128, 144], f16),
-    "ID": ("sbuf", [128, 128], f32), "I4": ("sbuf", [128, 128], f32), "RH": ("sbuf", [128, 128], bf), "HB": ("sbuf", [128, 128], bf),
+    "FL": ("sbuf", [128, 512], bf), "MX": ("sbuf", [128, 128], bf),
+    "Z1": ("sbuf", [128, 144], bf), "Z2": ("sbuf", [128, 144], f16),
+    "ID": ("sbuf", [128, 128], f32), "RH": ("sbuf", [128, 128], bf), "HB": ("sbuf", [128, 128], bf),
     "ONE": ("sbuf", [128, 128], bf), "JB": ("sbuf", [128, 128], bf), "JF": ("sbuf", [128, 128], f32),
-    "I1": ("sbuf", [128, 144], f32), "I2": ("sbuf", [128, 128], f32), "I3": ("sbuf", [128, 64], f32),
     "PI": ("sbuf", [128, 8], i32), "PJ": ("sbuf", [128, 8], i32), "COL": ("sbuf", [128, 16], f32),
     "KT": ("sbuf", [128, 64], f32), "YE": ("sbuf", [128, 64], f32), "SM": ("sbuf", [128, 512], f32),
     "SL16": ("sbuf", [128, 32], u16), "OE16": ("sbuf", [128, 64], u16), "SEL": ("sbuf", [128, 64], u16),
-    "L1": ("sbuf", [128, 768], f32), "L2": ("sbuf", [128, 384], f32), "L3": ("sbuf", [128, 192], f32),
-    "DD": ("sbuf", [128, 1216], f32),
+    "SX": ("sbuf", [128, 128], u16), "CS": ("sbuf", [128, 256], f32), "TH": ("sbuf", [128, 512], f32),
+    "Y2": ("sbuf", [128, 144], f16), "CL": ("sbuf", [128, 128], f16), "CR": ("sbuf", [128, 64], f16),
     "PS": ("psum", [128, 4096], f32),
 }
-SEMAPHORES = ["sv", "ss", "sp", "sg", "ldc", "lde", "ldl", "ldk", "ldx", "ldo", "ldt", "so",
-              "ac", "lc", "le", "lf", "ll", "lw", "lx"] + ["a%s%d" % (w, i) for w in "emwfl" for i in range(4)]
+INSIDE = {"TT": ("TC", 0), "CB": ("TC", 1024), "L1": ("EB", 0), "L2": ("EB", 768), "L3": ("EB", 1152), "DD": ("XG", 3072),
+          "M0": ("MG", 0), "M1": ("MG", 144), "I1": ("MG", 288), "I2": ("MG", 432), "I3": ("MG", 560), "I4": ("MG", 624)}
+SEMAPHORES = ["sv", "ss", "sp", "sg", "ldc", "lde", "ldl", "ldk", "ldx", "ldo", "ldt", "so", "cd", "ci", "cr", "cc", "co", "an", "ax", "ln",
+              "ac", "lc", "le", "lf", "ll", "lw", "lx"] + ["a%s%d" % (w, i) for w in "emwfl" for i in range(2)]
 
 
 def helpers(T, topo):
@@ -83,23 +137,25 @@ def cyclic(p, a, b, width):
 
 def pieces(q, t, what):
     name, base, width, p, land, lsem = {"e": ("EA", ET + q * SO, SO, 0, "XG", "le"), "m": ("WM", q * RO, RO, 256 * t, "EA", "lw"),
-                                        "f": ("EB", ET + q * SO, SO, 128 * t, "EG", "lf"),
+                                        "f": ("EB", ET + q * SO, SO, 0, "EG", "lf"),
                                         "l": ("LV", q * SO, SO, 0, "LV", "ll"),
-                                        "w": ("BIG", (W1 if t % 2 else W0) + q * RO, RO, 256 * t * OPT["wrot"], "EB", "lx")}[what]
-    return [(name, [(base + lo, base + hi) for lo, hi in cyclic(p, a, b, width)], way, land, t * width + a, "a%s%d" % (what, i), lsem)
-            for i, (a, b, way) in enumerate(OPT[what if t or what in "fl" else what + "0"])]
+                                        "w": ("BIG", (W1 if t % 2 else W0) + q * RO, RO, 0, "EB", "lx")}[what]
+    ways = OPT[what if t or what in "fl" else what + "0"]
+    n = width // len(ways)
+    return [(name, [(base + lo, base + hi) for lo, hi in cyclic(p, i * n, i * n + n, width)], way, land, t * width + i * n, "a%s%d" % (what, i), lsem)
+            for i, way in enumerate(ways)]
 
 
 def helper_program(g, core, T, topo, far):
     qw = [i for i in range(N) if far[i][0] == core][0]
-    eng = common_engines(topo, core, far[qw][1] + far[qw][2])
+    eng = common_engines(topo, core, far[qw][1])
     seen = {}
     for t in range(TR):
         for what in "emwf":
             for name, cols, way, land, at, rsem, _ in pieces(qw, t, what):
                 if way == "d":
                     continue
-                to = far[qw][1] + (far[qw][2] if way == "f" else [])
+                to = far[qw][1]
                 seen[rsem] = seen.get(rsem, 0) + len(eng)
                 g.wait_ge(T.sem[rsem], seen[rsem])
                 wd = cols[0][1] - cols[0][0]
@@ -129,6 +185,9 @@ def rank_program(g, core, T, topo):
     acc = {n: [] for n in SCRATCH}
 
     def R(name, lo, hi, step=1):
+        if name in INSIDE:
+            name, at = INSIDE[name]
+            lo, hi = lo + at, hi + at
         ap = T[name][:, lo:hi] if step == 1 else T[name][:, lo:hi:step]
         return (ap, [(name, lo, hi)])
 
@@ -159,12 +218,16 @@ def rank_program(g, core, T, topo):
                         x, y, hit = lo // 512 * 512, -(-hi // 512) * 512, True
                     if chain and k2 == k and name == "PS":
                         hit = False
+                    if OPT["war"] and wr and k2 == k and k in "vs" and sem == CS[k]:
+                        hit = False
                     if hit and a < y and x < b:
                         dep[sem] = max(dep.get(sem, 0), n)
         for sem in sorted(dep, key=lambda s: s not in CS.values()):
             wait(k, sem, dep[sem])
 
     def note(k, reads, writes, sem, n):
+        if "log" in OPT and q == 0:
+            OPT["log"].append((OPT["cur"], k, reads, writes))
         for name, lo, hi in writes:
             acc[name][:] = [e for e in acc[name] if not (lo <= e[0] and e[1] <= hi and (name != "PS" or e[3] == k))]
             acc[name].append((lo, hi, True, k, sem, n))
@@ -172,7 +235,17 @@ def rank_program(g, core, T, topo):
             acc[name][:] = [e for e in acc[name] if not (e[3] == k and e[4] == sem and not e[2] and lo <= e[0] and e[1] <= hi)]
             acc[name].append((lo, hi, False, k, sem, n))
 
+    part = [None, -1]
+
+    def skipped(k):
+        if part[0] is None:
+            return False
+        part[1] += k == "v"
+        return part[1] != part[0]
+
     def op(k, out, ins, call, chain=False):
+        if skipped(k):
+            return
         reads = [r for x in ins for r in x[1]] + [r for x in ins + [out] if len(x) > 2 for r in x[2]]
         order(k, reads, out[1], chain)
         sem = CS[k]
@@ -216,7 +289,7 @@ def rank_program(g, core, T, topo):
             mm(out, R("ID", 0, 128), s, i == 0, i == len(srcs) - 1)
 
     def move(k, out, a):
-        if k in "pl":
+        if k == "p":
             ident(out, [a])
         else:
             (cp if k == "v" else act)(out, a)
@@ -227,50 +300,52 @@ def rank_program(g, core, T, topo):
         else:
             op("g", out, [], lambda: g.iota(out[0], pattern, base, cm))
 
-    def load(k, out, src, sem):
-        order(k, [], out[1])
+    def dma(k, out, a, sem):
+        if skipped(k):
+            return
+        writes, reads = (out[1] if isap(out) else []), (a[1] if isap(a) else [])
+        order(k, reads, writes)
         total[sem] += 16
-        Q[k].dma_start(out[0], src).then_inc(T.sem[sem], 16)
-        note(k, [], out[1], sem, total[sem])
+        Q[k].dma_start(out[0] if isap(out) else out, a[0] if isap(a) else a).then_inc(T.sem[sem], 16)
+        note(k, reads, writes, sem, total[sem])
 
-    def store(k, dst, a):
-        order(k, a[1], [])
-        total["so"] += 16
-        Q[k].dma_start(dst, a[0]).then_inc(T.sem.so, 16)
-        note(k, a[1], [], "so", total["so"])
-
-    def send(pieces, cs, lands, rsem, lsem):
-        reads = [r for p in pieces for r in p[1]]
+    def send(parts, cs, lands, rsem, lsem):
+        if skipped("g"):
+            return
+        reads = [r for p in parts for s in p for r in s[1]]
         order("g", reads, [])
-        n = len(pieces)
+        n = len(parts)
         g.remote_dma_fused([RemoteDMATransfer(dst_ids=[dst_id(topo, c) for c in cs], dma_engine_mask=as_mask(eng[i::n]),
-                                              remote_sem=T.sem[rsem], src=p[0], dsts=lands[i]) for i, p in enumerate(pieces)],
-                           local_sem=T.sem[lsem])
+                                              remote_sem=T.sem[rsem], srcs=[s[0] for s in p], dsts=lands[i], alu_op=3 if len(p) > 1 else 0)
+                            for i, p in enumerate(parts)], local_sem=T.sem[lsem])
         total[lsem] += NE
         note("g", reads, [], lsem, total[lsem])
 
-    def send_all(pieces, rsem, lsem):
-        send(pieces, others, [[p[0]] * len(others) for p in pieces], rsem, lsem)
-
-    def send_piece(t, what, i):
+    def send_piece(t, what, i, source=None):
         name, cols, way, land, at, rsem, lsem = pieces(q, t, what)[i]
-        ps = [R(name, lo, hi) for lo, hi in cols]
+        to = [T[name][:, lo:hi] for lo, hi in cols]
+        parts = [source(lo, hi) if source else [R(name, lo, hi)] for lo, hi in cols]
         if way == "d":
-            return send_all(ps, rsem, lsem)
-        near = far[q][2] if way == "a" else []
+            return send(parts, others, [[x] * len(others) for x in to], rsem, lsem)
+        near = far[q][2]
         wd = cols[0][1] - cols[0][0]
-        send(ps, [far[q][0]] + near, [[T[land][:, at + j * wd:at + (j + 1) * wd]] + [p[0]] * len(near) for j, p in enumerate(ps)], rsem, lsem)
+        send(parts, [far[q][0]] + near, [[T[land][:, at + j * wd:at + (j + 1) * wd]] + [x] * len(near) for j, x in enumerate(to)], rsem, lsem)
 
     def send_block(t, what):
         for i in range(len(pieces(q, t, what))):
             send_piece(t, what, i)
 
-    def arrive(name, base, width, sem, calls=1):
-        total[sem] += (N - 1) * NE * calls
-        note("x", [], [(name, base + r * width, base + (r + 1) * width) for r in range(N) if r != q], sem, total[sem])
+    def send_amounts(src):
+        send([[src]], others, [[cown[0]] * len(others)], "ac", "lc")
+
+    def arrive_amounts():
+        total["ac"] += (N - 1) * NE
+        note("x", [], [("CT", r * SO, (r + 1) * SO) for r in range(N) if r != q], "ac", total["ac"])
 
     def arrive_block(t, what):
         for i, mine in enumerate(pieces(q, t, what)):
+            if what == "m" and t and i and "o2" in OPT["round"]:
+                continue
             total[mine[5]] += (N - 1) * NE
             note("x", [], [(mine[0], lo, hi) for r in range(N) if r != q for lo, hi in pieces(r, t, what)[i][1]], mine[5], total[mine[5]])
 
@@ -278,7 +353,6 @@ def rank_program(g, core, T, topo):
         for r in range(16):
             mm(R("PS", 512 * bank, 512 * bank + n), R(z, 16 - r, 144 - r), R(src, lo + r, lo + 16 * n, 16), r == 0, last and r == 15)
 
-    C0 = OPT["c0"]
     cown = R("CT", q * SO, (q + 1) * SO)
     ctab = R("CT", 0, 2048)
     lvtab = R("LV", 0, 2048)
@@ -291,7 +365,24 @@ def rank_program(g, core, T, topo):
     rxl = lambda lo, hi: R("L16", lo // 16, hi // 16)
     egat = lambda b, lo, hi: G(etab(b), R("L16", 256 + lo // 16, 256 + hi // 16))
     mgat = lambda lo, hi: G(mtab, rxl(lo, hi))
-    wm = lambda a, b: R("WM", q * RO + 256 * a, q * RO + 256 * b)
+    cold = lambda lo, hi: R("XG", ET + q * SO + lo, ET + q * SO + hi)
+
+    def extract8(bank, z, src, lo, const):
+        out = R("PS", 512 * bank, 512 * bank + 64)
+        for r in range(8):
+            mm(out, R(z, 16 - r, 144 - r), R(src, lo + r, lo + 512, 8), r == 0, False)
+        mm(out, R("CL", 0, 128), const, False, True)
+
+    def wide_constants():
+        cp(R("Y2", 0, 8), R("Z2", 0, 8))
+        tt(R("Y2", 8, 144), R("Z2", 8, 144), R("Z2", 0, 136), A.add)
+        ts(R("CL", 0, 128), R("I1", 16, 144), 0.0, A.is_equal)
+        ts(col(9), col(2), 8.0, A.is_lt)
+        ts(col(10), col(2), 8.0, A.is_ge)
+        ts(R("COL", 11, 13), R("COL", 9, 11), 2000.0, A.mult)
+        ts(sm(13), R("JF", 32, 64), 0.5, A.mult, 0.5 - 512.0, A.add)
+        for h in range(2):
+            ts(R("CR", h, 64, 2), sm(13), col(9 + h), A.mult, col(12 - h), A.add)
 
     def live_count(h, ahead=False):
         if ahead:
@@ -316,9 +407,11 @@ def rank_program(g, core, T, topo):
         if p:
             cp(R("CAR", 0, 1), R("SCL", SO - 1, SO))
             scan(R("SCL", 0, p), R("TY", 0, p), R("LV", q * SO, q * SO + p), R("CAR", 0, 1), A.mult, A.add)
+        else:
+            part[1] += 2
         counts(6, "SCL", 0, 32, 32 - 8 * (t % 4))
 
-    def picks_slots(t, between=(list, list, list)):
+    def picks_slots(t):
         y = R("PS", 3072, 3104)
         x0 = 32 - 8 * (t % 4)
         tt(sm(1), R("KT", x0, x0 + 32), y, A.subtract)
@@ -326,14 +419,12 @@ def rank_program(g, core, T, topo):
         ts(sm(3), sm(1), 256.0 - 2047.0, A.is_ge, 512.0, A.mult)
         tt(sm(2), sm(0), y, A.add)
         tt(sm(4), sm(3), sm(1), A.add)
-        between[0]()
         tt(sm(5), sm(2), sm(4), A.min)
-        between[1]()
         ts(R("SL16", 0, 32), sm(5), 2047.0, A.add)
 
     def slots_clear():
         out, a = R("INV", 0, 256), R("POS", 0, 256)
-        op("s", out, [a], lambda: g.scalar.activation(out[0], a[0], F.Silu if OPT["clr"] else F.Copy, scale=4.0))
+        op("s", out, [a], lambda: g.scalar.activation(out[0], a[0], F.Silu, scale=4.0))
 
     def picks_scatter(t):
         p = (128 * t) % SO
@@ -359,300 +450,401 @@ def rank_program(g, core, T, topo):
         else:
             cp(R("OE16", 0, 64), R("SM", 256, 320))
 
-    def tau_picked(k):
-        move(k, R("TE", 0, SO), G(R("TAU", 0, 528), R("OE16", 32, 64)))
-
-    def rate_pre(lo, hi):
-        act(R("TT", lo, hi), G(ctab, R("A16", lo // 16, hi // 16)))
-        act(R("CB", lo, hi), G(ctab, R("B16", lo // 16, hi // 16)))
-
-    def rate_1(lo, hi):
-        tt(R("PS", lo, hi), R("TT", lo, hi), R("PS", lo, hi), A.mult)
-
-    def rate_2(lo, hi, base):
-        tt(R("BIG", base + lo, base + hi), R("CB", lo, hi), R("PS", lo, hi), A.mult)
-
-    def maxscan(b, lo, hi):
-        scan(R(b, lo, hi), R("RM", 0, hi - lo), R("EG", lo, hi), 0.0, A.min, A.max)
-
     def writeback(src, dst, lo, hi):
         tt(eown(dst, lo, hi), G(R(src, 0, 6144), R("OE16", lo // 16, hi // 16)), R("TE", lo, hi), A.max)
 
-    def rates(t, wn, wo):
-        if "w" in OPT["tail"]:
-            send_block(t, "e")
-        for k in "vs":
-            need(k, "lw")
-            need(k, "lx")
-        arrive_block(t, "l")
-        x0 = 16 * (t % 4)
-        win = R("BIG", wo + q * RO, wo + 5120)
-
-        plan = OPT["m"]
-        at = lambda i: R("PS", 2048 + 512 * i, 2048 + 512 * i + (plan[i][1] - plan[i][0]) // 16)
-        state = [0, 0]
-
-        def select(a, b, k):
-            for lo, hi in cyclic(256 * t, a, b, RO):
-                src = G(win, R("SEL", a // 16, (a + hi - lo) // 16))
-                if k == "v":
-                    ts(R("WM", q * RO + lo, q * RO + hi), src, 1.0, A.min)
-                else:
-                    act(R("BIG", wn + q * RO + lo, wn + q * RO + hi), src)
-                a += hi - lo
-
-        def look(hi):
-            lo, state[0] = state[0], hi
-            tt(R("ACT", lo, hi), G(lvtab, R("B16", x0 + lo // 16, x0 + hi // 16)), R("LA", lo, hi), A.max)
-            for i, (a, b, _) in enumerate(plan):
-                if lo < b <= hi and b <= 512:
-                    extract(4 + i, "Z1", "ACT", a, (b - a) // 16, last=False)
-                    mm(at(i), R("ONE", 0, 128), R("JB", x0 + a // 16, x0 + b // 16), False, True)
-
-        def count(hi):
-            lo, state[1] = state[1], hi
-            if lo:
-                cp(R("CAR", 0, 1), R("SC", lo - 1, lo))
-            scan(R("SC", lo, hi), R("TY", lo, hi), R("ACT", lo, hi), R("CAR", 0, 1) if lo else 0.0, A.mult, A.add)
-            for i, (a, b, _) in enumerate(plan):
-                if lo < b <= hi and b > 512:
-                    counts(4 + i, "SC", a, (b - a) // 16, 64 + a // 16)
-
-        def offsets(i):
-            a, b = plan[i][0] // 16, plan[i][1] // 16
-            if b <= 32:
-                ts(R("SEL", a, b), at(i), col(7), A.add)
-            else:
-                ts(R("SM", 320 + a, 320 + b), at(i), 512.0 - 2048.0, A.is_le, delta, A.mult)
-                tt(R("SM", 384 + a, 384 + b), R("SM", 320 + a, 320 + b), R("JF", x0 + a, x0 + b), A.add)
-                cp(R("SEL", a, b), R("SM", 384 + a, 384 + b))
-
-        for step in OPT["steps"].split():
-            k, n = step[0], int(step[1:] or 0)
-            if k == "L":
-                cuts = OPT["la"]
-                for lo, hi in zip(cuts, cuts[1:]):
-                    act(R("LA", lo, hi), G(lvtab, R("A16", x0 + lo // 16, x0 + hi // 16)))
-            elif k == "A":
-                cp(R("LA", 0, n), G(lvtab, R("A16", x0, x0 + n // 16)))
-            elif k == "w":
-                writeback("EB", "EA", 0, SO)
-                send_block(t, "e")
-            elif k == "p":
-                picks_scatter(t)
-            elif k == "k":
-                picks_slots(t)
-            elif k == "n":
-                picks_count(t)
-            elif k == "y":
-                rate_1(512 * (n % 2), 512 * n + 512 if n < 2 else RO)
-            elif k == "i":
-                (picks_extract, picks_inv)[n]()
-            elif k == "b":
-                back(n)
-            elif k == "t":
-                tau_picked("sv"[n])
-            elif k == "x":
-                rate_2(512 * (n % 2), 512 * n + 512 if n < 2 else RO, wo + 4096)
-            elif k == "a":
-                look(n)
-            elif k == "c":
-                count(n)
-            elif k == "o":
-                offsets(n)
-            elif k == "s":
-                select(plan[n][0], plan[n][1], "v")
-                send_piece(t, "m", n)
-            elif k == "r":
-                select(plan[n][0], plan[n][1], "s")
-            elif k == "l":
-                picks_lists(t, n)
+    def to_psum(k, name, lo, hi):
+        if k == "p":
+            for x in range(lo // 512 * 512, hi, 512):
+                move(k, R("PS", max(x, lo), min(x + 512, hi)), R(name, max(x, lo), min(x + 512, hi)))
+        else:
+            move(k, R("PS", lo, hi), R(name, lo, hi))
 
     def first_rates():
         wq = lambda a, b: R("BIG", W0 + q * RO + a, W0 + q * RO + b)
-        move("p", R("PS", 512, 1024), R("KK", 512, 1024))
-        arrive("CT", 0, SO, "ac")
-        rate_pre(512, 1024)
-        picks_scatter(0)
-        act(R("POS", 0, SO), R("POS", SO, 2 * SO))
+        wm = lambda a, b: R("WM", q * RO + a, q * RO + b)
+        arrive_amounts()
+        act(R("TT", 512, 1024), G(ctab, R("A16", 32, 64)))
+        act(R("CB", 512, 1024), G(ctab, R("B16", 32, 64)))
         tt(R("TT", 0, 512), G(ctab, R("A16", 0, 32)), R("KK", 0, 512), A.mult)
         tt(wq(0, 512), G(ctab, R("B16", 0, 32)), R("TT", 0, 512), A.mult)
-        ts(wm(0, 2), wq(0, 512), 1.0, A.min)
-        for i, (a, b, _) in enumerate(OPT["m0"]):
-            if b <= 512:
-                send_piece(0, "m", i)
-        rate_1(512, 1024)
-        rate_2(512, 1024, W0 + q * RO)
-        ts(wm(2, 4), wq(512, 1024), 1.0, A.min)
-        for i, (a, b, _) in enumerate(OPT["m0"]):
-            if b > 512:
-                send_piece(0, "m", i)
-        ts(R("PM", 0, 256), R("RM", 0, 256), col(2), A.is_equal, 8192.0, A.mult)
-        picks_extract()
-        picks_inv()
-        for h in (1, 0):
-            picks_lists(0, h)
-        for h in range(2):
-            cp(R("LI", 1024 * h + 512, 1024 * h + 896), R("LI", 1024 * h, 1024 * h + 384))
+        ts(wm(0, 512), wq(0, 512), 1.0, A.min)
+        if len(OPT["m0"]) == 2:
+            send_piece(0, "m", 0)
+        tt(R("PS", 512, 1024), R("TT", 512, 1024), R("PS", 512, 1024), A.mult)
+        tt(wq(512, 1024), R("CB", 512, 1024), R("PS", 512, 1024), A.mult)
+        ts(wm(512, 1024), wq(512, 1024), 1.0, A.min)
+        send_piece(0, "m", len(OPT["m0"]) - 1)
 
-    def amounts(t, wn):
+    def a_round(t):
+        wn, wo = (W0, W1) if t % 2 == 0 else (W1, W0)
+        last = t == TR - 1
+        x0 = 16 * (t % 4)
+        p = (128 * t) % SO
+        win = R("BIG", wo + q * RO, wo + 5120)
+        wtab = R("BIG", wn, wn + 4096)
+        wown = lambda lo, hi: R("BIG", wn + q * RO + lo, wn + q * RO + hi)
+        at = lambda i: R("PS", 2048 + 512 * i, 2080 + 512 * i)
         ps = lambda lo, hi, step=1: R("PS", 1024 + lo, 1024 + hi, step)
         x = lambda e, lo, hi: R("XG", lo + e, hi, 4)
-        wtab = R("BIG", wn, wn + 4096)
-        cuts = OPT["xg"]
-        for lo, hi in zip(cuts, cuts[1:]):
-            act(R("XG", lo, hi), G(wtab, rxl(lo, hi)), 0.125)
-            if hi <= OPT["treeA"]:
-                ident(ps(lo // 4, hi // 4), [x(0, lo, hi), x(1, lo, hi)])
-        if cuts[-1] < 3072:
-            ts(R("XG", cuts[-1], 3072), G(wtab, rxl(cuts[-1], 3072)), 0.125, A.mult)
-        act(R("MG", 0, C0), mgat(0, C0))
-        cuts = OPT["tb"]
-        for lo, hi in zip(cuts, cuts[1:]):
-            tt(R("L1", lo // 4, hi // 4), x(2, lo, hi), x(3, lo, hi), A.add)
-            lo = max(lo, OPT["treeA"])
-            if lo < hi:
-                tt(ps(lo // 4, hi // 4), x(0, lo, hi), x(1, lo, hi), A.add)
-        tt(R("L2", 0, 384), R("L1", 1, 768, 2), ps(1, 768, 2), A.add)
-        tt(ps(0, 768, 2), ps(0, 768, 2), R("L1", 0, 768, 2), A.add)
-        tt(R("L3", 0, 192), ps(2, 768, 4), R("L2", 1, 384, 2), A.add)
-        tt(ps(0, 768, 4), ps(0, 768, 4), R("L2", 0, 384, 2), A.add)
-        tt(R("DD", 0, 192), ps(0, 768, 4), R("L3", 0, 192), A.subtract)
+        have = {k: set() for k in "FCDGH"}
+        A_END = OPT["tree"] * U
+        TB = OPT["tb"]
 
-    def amounts_out(t):
-        tt(R("CB", 0, SO), G(R("DD", 0, 1216), R("SL16", 0, 32)), cown, A.add)
-        ts(cown, R("CB", 0, SO), 0.125, A.max, 8.0, A.min)
-        if t < TR - 1:
-            send_all([cown], "ac", "lc")
-        else:
-            store("y", T.yc[:], cown)
+        def places(a, b):
+            for lo, hi in cyclic(256 * t, a, b, RO):
+                yield lo, hi, G(win, R("SEL", a // 16, (a + hi - lo) // 16))
+                a += hi - lo
 
-    def sweeps(t, wn):
-        send_block(t, "w")
-        arrive_block(t, "e")
-
-        def to_psum(k, name, lo, hi):
-            if k in "pl":
-                for x in range(lo // 512 * 512, hi, 512):
-                    move(k, R("PS", max(x, lo), min(x + 512, hi)), R(name, max(x, lo), min(x + 512, hi)))
-            else:
-                move(k, R("PS", lo, hi), R(name, lo, hi))
-
-        if OPT["tau"] != "b" or t == 0:
-            tau_picked(OPT["tau"] if t else "v")
-        if "h" in OPT["tail"] and t < TR - 1:
-            ts(R("TH", 0, SO), R("TE", 0, SO), 0.125, A.is_lt, 0.125, A.mult)
-        pre = OPT["pre"] if t else OPT["pre0"]
-        move(OPT["ez"], R("TT", 0, C0), egat("EA", 0, C0))
-        for lo, hi, k, c in pre:
-            move(k, R("EG", lo, hi), egat("EA", lo, hi))
-            if c == "p":
-                to_psum(c, "EG", lo, hi)
-        for lo, hi, k, c in pre:
-            if c != "p":
-                to_psum(c, "EG", lo, hi)
-        ready = [p[:2] for p in pre]
-
-        arrive_block(t, "m")
-        tt(R("EG", 0, C0), mgat(0, C0), R("TT", 0, C0), A.mult)
-        for step in OPT["s1"].split():
-            k, lo, hi = step[0], *[OPT["unit"] * int(x, 17) for x in (step[1:] + "0")[:2]]
-            if k == "m":
-                act(R("MG", lo, hi), mgat(lo, hi))
-                if not any(a <= lo and hi <= b for a, b in ready):
-                    tt(R("EG", lo, hi), egat("EA", lo, hi), R("MG", lo, hi), A.mult)
+        def step(s):
+            s, _, only = s.partition(".")
+            part[:] = [int(only) if only else None, -1]
+            k, arg = s[:2], [int(c, 17) for c in s[2:]]
+            lo, hi = ([U * a for a in arg] + [0, 0])[:2]
+            units = set(range(lo // U, hi // U))
+            if k == "se":
+                send_block(t, "e")
+            elif k[0] == "a" and k != "ao":
+                if k == "aC":
+                    arrive_amounts()
                 else:
-                    tt(R("EG", lo, hi), R("MG", lo, hi), R("PS", lo, hi), A.mult)
-                for a, b, c in OPT["cpm"]:
-                    if c == "p" and lo < b <= hi:
-                        to_psum(c, "MG", a, b)
-            elif k == "s":
-                maxscan("EA", lo, hi)
-            else:
-                i = lo // OPT["unit"]
-                for a, b in cyclic(128 * t, OPT["f"][i][0], OPT["f"][i][1], SO):
-                    writeback("EA", "EB", a, b)
-                send_piece(t, "f", i)
-
-        if OPT["kat"] == "s1" and t < TR - 1:
-            to_psum(OPT["kcp"], "KK", 0, RO)
-        arrive_block(t, "w")
-        if t == TR - 1:
-            for p in pieces(q, t, "w"):
-                need("y", p[5])
-            store("y", T.yw[:], R("BIG", wn + q * RO, wn + (q + 1) * RO))
-        amounts(t, wn)
-        for a, b, k in OPT["cpm"]:
-            if k != "p":
-                to_psum(k, "MG", a, b)
-        if OPT["cout"] < 0:
-            amounts_out(t)
-
-        arrive_block(t, "f")
-        tt(R("EG", 0, C0), egat("EB", 0, C0), R("MG", 0, C0), A.mult)
-        behind = [(0, C0)]
-        if OPT["first2"]:
-            maxscan("EB", 0, C0)
-            behind = []
-        for i, (lo, hi) in enumerate(OPT["s2"]):
-            act(R("EG", lo, hi), egat("EB", lo, hi))
-            if i == OPT["cout"]:
-                amounts_out(t)
-            tt(R("EG", lo, hi), R("EG", lo, hi), R("PS", lo, hi), A.mult)
-            if i in OPT["own2"]:
-                behind = [(behind[0][0], hi)] if behind and behind[0][1] == lo else behind + [(lo, hi)]
-            for a, b in behind:
-                maxscan("EB", a, b)
-            behind = [] if i in OPT["own2"] else [(lo, hi)]
-        for a, b in behind:
-            maxscan("EB", a, b)
-        if t < TR - 1:
-            if OPT["kat"] == "s2":
-                to_psum(OPT["kcp"], "KK", 0, RO)
-            arrive("CT", 0, SO, "ac")
-            rate_pre(0, RO)
-            slots_clear()
-        for k, h in (OPT["tail"] if t < TR - 1 else "w0 w1").split():
-            h = int(h)
-            if k == "w" and h == 2:
+                    arrive_block(t, k[1].lower())
+                if k == "aW" and last:
+                    for pc in pieces(q, t, "w"):
+                        need("y", pc[5])
+                    dma("y", T.yw[:], wown(0, RO), "so")
+            elif k == "r1":
+                tt(R("PS", lo, hi), R("TT", lo, hi), R("PS", lo, hi), A.mult)
+            elif k == "r2":
+                tt(R("BIG", wo + 4096 + lo, wo + 4096 + hi), R("CB", lo, hi), R("PS", lo, hi), A.mult)
+            elif k == "r3":
+                for a, b in cyclic(256 * t, lo, hi, RO):
+                    tt(R("BIG", wo + 4096 + a, wo + 4096 + b), R("CB", a, b), R("PS", a, b), A.mult)
+            elif k == "pc":
+                picks_count(t)
+            elif k == "ps":
+                picks_slots(t)
+            elif k == "px":
+                picks_scatter(t)
+            elif k == "pi":
+                picks_extract()
+            elif k == "pj":
+                picks_inv()
+            elif k in ("lr", "lo"):
+                picks_lists(t, k == "lo")
+            elif k[0] == "b":
+                back(int(k[1]))
+            elif k in ("tv", "ts"):
+                move(k[1], R("TE", 0, SO), G(R("TAU", 0, 528), R("OE16", 32, 64)))
+            elif k[0] == "L":
+                move(k[1], R("LA", lo, hi), G(lvtab, R("A16", x0 + lo // 16, x0 + hi // 16)))
+            elif k == "lk":
+                tt(R("ACT", lo, hi), G(lvtab, R("B16", x0 + lo // 16, x0 + hi // 16)), R("LA", lo, hi), A.max)
+                if hi == 512 and "0" in OPT["wide"]:
+                    extract8(4, "Y1", "ACT", 0, R("CR", 2 * x0, 2 * x0 + 64))
+                elif hi == 512:
+                    extract(4, "Z1", "ACT", 0, 32, last=False)
+                    mm(at(0), R("ONE", 0, 128), R("JB", x0, x0 + 32), False, True)
+            elif k == "ct":
+                scan(R("SC", 0, RO), R("TY", 0, RO), R("ACT", 0, RO), 0.0, A.mult, A.add)
+                if "1" in OPT["wide"]:
+                    extract8(5, "Y2", "SC", 512, R("CR", 0, 64))
+                else:
+                    counts(5, "SC", 512, 32, 96)
+            elif k == "o0" and "0" in OPT["wide"]:
+                ts(R("SM", 448, 512), R("PS", 2048, 2112), col(7), A.add, 0.0, A.max)
+                tt(sm(10), R("SM", 448, 512, 2), R("SM", 449, 512, 2), A.add)
+                cp(R("SEL", 0, 32), sm(10))
+            elif k == "o0":
+                ts(R("SEL", 0, 32), at(0), col(7), A.add)
+            elif k == "o1" and "1" in OPT["wide"]:
+                ts(R("SM", 352, 416), R("PS", 2560, 2624), -1024.0, A.is_le, delta, A.mult)
+                tt(sm(13), R("SM", 352, 416, 2), R("JF", x0 + 32, x0 + 64), A.add)
+                tt(sm(13), sm(13), R("SM", 353, 416, 2), A.add)
+                cp(R("SEL", 32, 64), sm(13))
+            elif k == "o1":
+                ts(sm(11), at(1), 512.0 - 2048.0, A.is_le, delta, A.mult)
+                tt(sm(13), sm(11), R("JF", x0 + 32, x0 + 64), A.add)
+                cp(R("SEL", 32, 64), sm(13))
+            elif k == "oc":
+                need("y", "ll")
+                for r in range(N):
+                    a = 0
+                    for b, c in cyclic(256 * t, 512, RO, RO):
+                        dma("y", R("MG", RO * r + a, RO * r + a + c - b), R("WM", RO * r + b, RO * r + c), "co")
+                        a += c - b
+            elif k == "nm":
+                a = 0
+                for b, c in cyclic(256 * t, 512, RO, RO):
+                    ts(R("MG", RO * q + 512 + a, RO * q + 512 + a + c - b), R("BIG", wo + 4096 + b, wo + 4096 + c), 1.0, A.min)
+                    a += c - b
+            elif k == "N_":
+                total["an"] += (N - 1) * NE
+                need("g", "al0")
+                mine = R("MG", RO * q + 512, RO * q + RO)
+                send([[mine]], others, [[mine[0]] * len(others)], "an", "ln")
+                note("x", [], [("MG", RO * r + 512, RO * r + RO) for r in range(N) if r != q], "an", total["an"])
+            elif k == "o2":
+                if "1" in OPT["wide"]:
+                    ts(R("SM", 448, 512), R("PS", 2560, 2624), -1024.0, A.is_le, 512.0, A.mult)
+                    tt(sm(10), R("SM", 448, 512, 2), R("JF", 0, 32), A.add)
+                    tt(sm(10), sm(10), R("SM", 449, 512, 2), A.add)
+                else:
+                    ts(sm(14), at(1), 512.0 - 2048.0, A.is_le, 512.0, A.mult)
+                    tt(sm(10), sm(14), R("JF", 0, 32), A.add)
+                mine = R("SX", 32 * q, 32 * q + 32)
+                cp(mine, sm(10))
+                send([[mine]], others, [[mine[0]] * len(others)], "ax", "ln")
+                total["ax"] += (N - 1) * NE
+                note("x", [], [("SX", 32 * r, 32 * r + 32) for r in range(N) if r != q], "ax", total["ax"])
+            elif k in ("gv", "gs"):
+                d, h0, h1 = arg
+                r = (q + d) % N
+                for b, c in cyclic(256 * t, 512 + 128 * h0, 512 + 128 * h1, RO):
+                    a = (b - 256 * t - 512) % RO
+                    move(k[1], R("WM", RO * r + b, RO * r + c), G(R("MG", RO * r, RO * r + RO), R("SX", 32 * r + a // 16, 32 * r + (a + c - b) // 16)))
+            elif k == "th":
+                ts(R("TH", 0, SO), R("TE", 0, SO), 0.125, A.is_lt, 0.125, A.mult)
+            elif k == "h_":
+                live_count(arg[0], True)
+            elif k == "w3":
                 writeback("EB", "EA", 0, SO)
-            elif k == "w":
+            elif k == "cw" and False:
+                pass
+            elif k == "k8":
+                wide_constants()
+            elif k == "mv":
+                for a, b, src in places(lo, hi):
+                    ts(R("WM", q * RO + a, q * RO + b), src, 1.0, A.min)
+            elif k in ("wv", "ws"):
+                for a, b, src in places(lo, hi):
+                    move(k[1], wown(a, b), src)
+            elif k == "q_":
+                for a, b, _ in places(lo, hi):
+                    ts(R("WM", q * RO + a, q * RO + b), wown(a, b), 1.0, A.min)
+            elif k[0] == "M":
+                send_piece(t, "m", int(k[1]))
+            elif k[0] == "U":
+                send_piece(t, "m", int(k[1]), lambda a, b: [wown(a - q * RO, b - q * RO), R("ON1", 0, b - a)])
+            elif k == "W_":
+                send_block(t, "w")
+            elif k[0] == "W":
+                send_piece(t, "w", int(k[1]))
+            elif k[0] == "E":
+                move(k[1], R("EG", lo, hi), egat("EA", lo, hi))
+            elif k[0] == "F":
+                move(k[1], R("EA", lo, hi), egat("EA", lo, hi))
+                have["F"] |= units
+            elif k[0] in "CD":
+                to_psum(k[1], "EG" if k[0] == "C" else "MG", lo, hi)
+                have[k[0]] |= units
+            elif k in ("ms", "mg"):
+                move("s" if k == "ms" else "v", R("MG", lo, hi), mgat(lo, hi))
+            elif k == "P_":
+                if units <= have["C"]:
+                    tt(R("EG", lo, hi), R("MG", lo, hi), R("PS", lo, hi), A.mult)
+                elif units <= have["F"]:
+                    tt(R("EG", lo, hi), mgat(lo, hi), R("EA", lo, hi), A.mult)
+                elif units <= have["G"]:
+                    tt(R("MG", lo, hi), mgat(lo, hi), R("EG", lo, hi), A.mult)
+                else:
+                    tt(R("EG", lo, hi), egat("EA", lo, hi), R("MG", lo, hi), A.mult)
+            elif k in ("z_", "Z_"):
+                src = "MG" if (k == "z_" and units <= have["G"] - have["C"]) or (k == "Z_" and units <= have["H"]) else "EG"
+                scan(R("EA" if k == "z_" else "EB", lo, hi), R("RM", 0, hi - lo), R(src, lo, hi), 0.0, A.min, A.max)
+            elif k[0] == "G":
+                move(k[1], R("EG", lo, hi), egat("EA", lo, hi))
+                have["G"] |= units
+            elif k == "cd":
+                dma("y", R("INV", 0, 256), R("BV", 0, 256), "cc")
+            elif k in ("Rs", "RS"):
+                act(R("TC", 0, 2048), G(ctab, R("AB16", 0, 128)))
+            elif k == "g2":
+                for h in range(2):
+                    ts(R("FL", 256 * h, 256 * h + 256), eown("EA", 256 * h, 256 * h + 256), 0.125, A.is_ge)
+                    mm(R("PS", 2048 + 256 * h, 2304 + 256 * h), R("MX", 0, 128), R("FL", 256 * h, 256 * h + 256), True, True)
+                out, a = R("LV", q * SO, q * SO + SO), R("PS", 2048, 2560)
+                op("s", out, [a, col(8)], lambda: g.scalar.activation(out[0], a[0], F.Sign, bias=col(8)[0]))
+                send_piece(t + 1, "l", 0)
+            elif k == "w1":
+                writeback("EA", "EB", 0, SO)
+                send_block(t, "f")
+            elif k == "Xs":
+                act(R("XG", lo, hi), G(wtab, rxl(lo, hi)), 0.125)
+                if hi <= A_END:
+                    ident(ps(lo // 4, hi // 4), [x(0, lo, hi), x(1, lo, hi)])
+            elif k in ("Ys", "Yv"):
+                if k == "Ys":
+                    act(R("XG", lo, hi), G(wtab, rxl(lo, hi)), 0.125)
+                else:
+                    ts(R("XG", lo, hi), G(wtab, rxl(lo, hi)), 0.125, A.mult)
+                y = lambda e: R("XG", lo + e, hi, 8)
+                bank = lambda b: R("PS", 512 * b + lo // 8, 512 * b + hi // 8)
+                ident(bank(TB[0]), [y(3)])
+                ident(bank(TB[1]), [y(7)])
+                if OPT["join"]:
+                    mm(bank(2), R("ID", 0, 128), y(0), lo == 0, False)
+                    mm(bank(2), R("ID", 0, 128), y(1), False, False)
+                else:
+                    ident(bank(2), [y(0), y(1)])
+                ident(bank(3), [y(4), y(5)])
+            elif k == "As":
+                act(R("XG", lo, hi), G(wtab, rxl(lo, hi)), 0.125)
+                y = lambda e: R("XG", lo + e, hi, 8)
+                bank = lambda b: R("PS", 512 * b + lo // 8, 512 * b + hi // 8)
+                ident(bank(3), [y(4), y(5)])
+                if OPT["join"]:
+                    mm(bank(2), R("ID", 0, 128), y(0), lo == 0, False)
+                    mm(bank(2), R("ID", 0, 128), y(1), False, False)
+                else:
+                    ident(bank(2), [y(0), y(1)])
+            elif k == "J_":
+                mm(ps(0, 384), R("ID", 0, 128), R("L1", 0, 768, 2), False, True)
+            elif k == "S2":
+                tt(R("L2", 0, 384), R("L1", 1, 768, 2), ps(512, 896), A.add)
+                if not OPT["join"]:
+                    tt(ps(0, 384), ps(0, 384), R("L1", 0, 768, 2), A.add)
+            elif k == "S3":
+                tt(R("L3", 0, 192), ps(1, 384, 2), R("L2", 1, 384, 2), A.add)
+                tt(ps(896, 1024) if False else R("L3", 192, 384), ps(0, 384, 2), R("L2", 0, 384, 2), A.add)
+            elif k == "S4":
+                tt(R("DD", 0, 192), R("L3", 192, 384), R("L3", 0, 192), A.subtract)
+            elif k == "S5":
+                tt(R("L3", 0, 192), ps(1, 384, 2), R("L2", 1, 384, 2), A.add)
+                tt(ps(512, 704), ps(0, 384, 2), R("L2", 0, 384, 2), A.add)
+                tt(R("DD", 0, 192), ps(512, 704), R("L3", 0, 192), A.subtract)
+            elif k == "V1":
+                tt(R("L1", 0, 384), R("XG", 2, 3072, 8), R("PS", 512 * TB[0], 512 * TB[0] + 384), A.add)
+                if OPT["join"]:
+                    mm(ps(0, 384), R("ID", 0, 128), R("L1", 0, 384), False, True)
+                tt(R("L1", 384, 768), R("XG", 6, 3072, 8), R("PS", 512 * TB[1], 512 * TB[1] + 384), A.add)
+            elif k == "V2":
+                if not OPT["join"]:
+                    tt(ps(0, 384), ps(0, 384), R("L1", 0, 384), A.add)
+                tt(R("L2", 0, 384), R("L1", 384, 768), ps(512, 896), A.add)
+            elif k == "V3":
+                tt(R("L3", 0, 192), ps(1, 384, 2), R("L2", 1, 384, 2), A.add)
+                tt(ps(0, 384, 2), ps(0, 384, 2), R("L2", 0, 384, 2), A.add)
+                tt(R("DD", 0, 192), ps(0, 384, 2), R("L3", 0, 192), A.subtract)
+            elif k == "Xv":
+                ts(R("XG", lo, hi), G(wtab, rxl(lo, hi)), 0.125, A.mult)
+            elif k == "T1":
+                tt(R("L1", lo // 4, hi // 4), x(2, lo, hi), x(3, lo, hi), A.add)
+                lo = max(lo, A_END)
+                if lo < hi:
+                    tt(ps(lo // 4, hi // 4), x(0, lo, hi), x(1, lo, hi), A.add)
+            elif k[0] == "B":
+                move(k[1], R("PS", OPT["bb"] + lo // 4, OPT["bb"] + hi // 4), x(3, lo, hi))
+            elif k == "T5":
+                tt(R("L1", lo // 4, hi // 4), x(2, lo, hi), R("PS", OPT["bb"] + lo // 4, OPT["bb"] + hi // 4), A.add)
+            elif k == "T2":
+                tt(R("L2", 0, 384), R("L1", 1, 768, 2), ps(1, 768, 2), A.add)
+                tt(ps(0, 768, 2), ps(0, 768, 2), R("L1", 0, 768, 2), A.add)
+            elif k == "T3":
+                tt(R("L3", 0, 192), ps(2, 768, 4), R("L2", 1, 384, 2), A.add)
+                tt(ps(0, 768, 4), ps(0, 768, 4), R("L2", 0, 384, 2), A.add)
+                tt(ps(0, 768, 4) if OPT["slot"] else R("DD", 0, 192), ps(0, 768, 4), R("L3", 0, 192), A.subtract)
+            elif k == "cs":
+                act(R("CS", 0, 256), G(cold(p, p + SO), R("IV16", 0, 16)))
+                act(R("XG", 3087, 4096, 16), R("CS", 192, 256))
+            elif k == "T4":
+                tt(ps(0, 768, 4), ps(0, 768, 4), R("CS", 0, 192), A.add)
+                ts(R("XG", 15, 3072, 16), ps(0, 768, 4), 0.125, A.max, 8.0, A.min)
+            elif k in ("cv", "cw"):
+                new = R("CN", 0, SO)
+                move("v" if k == "cv" else "s", new, G(R("XG", 0, ET + (q + 1) * SO), R("OE16", 0, 32)))
+                if last:
+                    dma("y", T.yc[:], new, "so")
+                else:
+                    send_amounts(new)
+                    dma("y", cown, new, "ci")
+                    dma("y", cold(0, SO), new, "cd")
+                    dma("y", cold(SO, SO + 384), R("CN", 0, 384), "cd")
+            elif k == "ao":
+                tt(R("CB", 0, SO), G(R("DD", 0, 1216), R("SL16", 0, 32)), cown, A.add)
+                ts(cown, R("CB", 0, SO), 0.125, A.max, 8.0, A.min)
+                if last:
+                    dma("y", T.yc[:], cown, "so")
+                else:
+                    send_amounts(cown)
+            elif k == "es":
+                act(R("EG", lo, hi), egat("EB", lo, hi))
+            elif k == "Qf":
+                tt(R("MG", lo, hi), mgat(lo, hi), R("EG", lo, hi), A.mult)
+                have["H"] |= units
+            elif k == "Q_":
+                if units <= have["D"]:
+                    tt(R("EG", lo, hi), R("EG", lo, hi), R("PS", lo, hi), A.mult)
+                else:
+                    tt(R("EG", lo, hi), egat("EB", lo, hi), R("MG", lo, hi), A.mult)
+            elif k[0] == "K":
+                to_psum(k[1], "KK", lo, hi)
+            elif k in ("Ra", "Rb", "RA", "RB"):
+                act(R("TT" if k[1] in "aA" else "CB", lo, hi), G(ctab, R("A16" if k[1] in "aA" else "B16", lo // 16, hi // 16)))
+            elif k == "rg":
+                tt(R("TT", lo, hi), R("TT", lo, hi), R("PS", lo, hi), A.mult)
+            elif k == "rh":
+                tt(R("BIG", wo + 4096 + lo, wo + 4096 + hi), G(ctab, R("B16", lo // 16, hi // 16)), R("TT", lo, hi), A.mult)
+            elif k == "cl":
+                slots_clear()
+            elif k == "w2":
+                h = arg[0]
                 writeback("EB", "EA", 256 * h, 256 * h + 256)
-                if t == TR - 1:
-                    store("ys"[h], T.ye[:, 256 * h:256 * h + 256], eown("EA", 256 * h, 256 * h + 256))
-            elif k in "gh":
-                live_count(h, k == "h")
-            elif t < TR - 1:
-                live_bound(h)
-                for i, (a, b, _) in enumerate(OPT["l"]):
-                    if b == 256 * h + 256:
-                        send_piece(t + 1, "l", i)
+                if last:
+                    dma("ys"[h], T.ye[:, 256 * h:256 * h + 256], eown("EA", 256 * h, 256 * h + 256), "so")
+            elif k == "g_":
+                live_count(arg[0])
+            elif k == "t_":
+                live_bound(arg[0])
+                if arg[0] == len(OPT["l"]) - 1 or arg[0] == 1:
+                    send_piece(t + 1, "l", arg[0] if len(OPT["l"]) == 2 else 0) if (len(OPT["l"]) == 2 or arg[0] == 1) else None
+            else:
+                raise ValueError(s)
+
+        skip = ""
+        if t == 0:
+            skip = "oc nm N_ o2 gv gs RA RB RS rg rh se r1 r2 r3 pc ps aL Ls Lv px lk ct o0 o1 mv M0 M1 U0 U1 wv ws q_ pi pj lo lr b0 b1 b2 w3"
+        else:
+            for k in "vs":
+                need(k, "lw")
+                need(k, "lx")
+        steps = OPT["round"]
+        if last:
+            skip = "Kp Ks Kv aC Ra Rb Rs cl cd th g_ g2 t_ h_ w2"
+        for s in steps.split() + (["W20", "W21"] if last else []):
+            OPT["cur"] = (t, s)
+            if s[:2] not in skip.split():
+                s = s.replace("W2", "w2")
+                if t == 0 and s == OPT["k8"]:
+                    for more in OPT["more0"].split():
+                        step(more)
+                step(s)
 
     loads = {"c": (cown, T.cin[:], "ldc"), "e": (eown("EA"), T.ein[:], "lde"), "a": (R("RAI", 0, 64), T.ra[:], "ldl"),
              "b": (R("RBI", 0, 64), T.rb[:], "ldl"), "k": (R("KK", 0, RO), T.kin[:], "ldk"), "o": (R("LI", 1024, 1536), T.ot[:], "ldo"),
              "r": (R("LI", 0, SO), T.rx[:], "ldx"), "t": (R("TAU", 16, 528), T.tau[:], "ldt")}
-    early, late = OPT["loads"].split()
+    loads.update({"R": (R("LI", SO, 896), T.rx[:, 0:384], "cd"), "O": (R("LI", 1536, 1920), T.ot[:, 0:384], "cd")})
+    early, late = OPT["loads"].split("|")
     for k in early:
-        load("y", *loads[k])
+        dma("y", *loads[k])
     iota(R("PI", 0, 2), [[112, 2]], 0, 1, small=False)
     iota(R("I2", 0, 128), [[1, 8], [0, 16]], 0, 0)
     iota(R("I1", 0, 144), [[1, 144]], -16, -1)
+    iota(R("I4", 0, 128), [[0, 8], [1, 16]], 1, 0)
     iota(R("I3", 0, 64), [[0, 2], [16, 32]], 192 - 2047, 0)
     iota(R("JB", 0, 128), [[0, 2], [16, 64]], 0, 0)
-    iota(R("I4", 0, 128), [[0, 8], [1, 16]], 1, 0)
-    send_all([cown], "ac", "lc")
+    send_amounts(cown)
     send_block(0, "e")
-    iota(R("POS", SO, 2 * SO), [[1, SO]], 1024, 0)
     iota(R("RM", 0, 1024), [[0, 64], [1, 16]], 0, 0)
-    need("y", "lc")
-    for k in late:
-        load("y", *loads[k])
 
-    fill(R("TY", 0, 1024), 1.0)
-    fill(R("INV", 0, 1216), 4096.0)
+    fill(R("BV", 0, 256), 4096.0)
+    out, a = R("INV", 0, 256), R("BV", 0, 256)
+    op("s", out, [a], lambda: g.scalar.activation(out[0], a[0], F.Silu))
     ts(R("PJ", 0, 2), R("PI", 0, 2), 4, A.arith_shift_right, 7, A.bitwise_and)
     ts(R("PJ", 2, 3), R("PI", 0, 1), 15, A.bitwise_and)
+    fill(R("TY", 0, SO), 1.0)
     cp(R("COL", 0, 3), R("PJ", 0, 3))
+    scan(R("POS", SO, 2 * SO), R("TY", 0, SO), R("TY", 0, SO), 1023.0, A.mult, A.add)
     ts(R("M0", 0, 128), R("I2", 0, 128), col(0), A.is_equal, 2.0, A.mult)
     ts(R("M1", 0, 128), R("I2", 0, 128), col(1), A.is_equal)
     ts(col(4), col(2), 0.0, A.is_equal)
@@ -661,41 +853,66 @@ def rank_program(g, core, T, topo):
     fill(col(8), -23.5)
     ts(col(6), col(2), 1.0, A.not_equal)
     tt(R("MX", 0, 128), R("M0", 0, 128), R("M1", 0, 128), A.add)
-    ts(R("TY", 0, 1024), R("TY", 0, 1024), col(6), A.mult)
+    ts(R("TY", 0, SO), R("TY", 0, SO), col(6), A.mult)
     ts(R("M0", 0, 144), R("I1", 0, 144), 0.0, A.is_equal, col(4), A.mult)
+    for h in range(2):
+        live_count(h)
+        live_bound(h)
     ts(R("M1", 0, 144), R("I1", 0, 144), -1.0, A.is_equal, col(5), A.mult)
-    ts(R("ID", 0, 128), R("I1", 16, 144), 0.0, A.is_equal)
-    tt(R("M1", 0, 144), R("M0", 0, 144), R("M1", 0, 144), A.add)
-    ts(R("KT", 0, 64), R("I3", 0, 64), col(2), A.add)
-    ts(R("Z2", 0, 144), R("M1", 0, 144), 0.5, A.mult)
-    ts(R("Z1", 0, 144), R("M0", 0, 144), delta / 2, A.mult)
     ts(R("RH", 0, 128), R("I4", 0, 128), 0.5, A.mult)
+    tt(R("M1", 0, 144), R("M0", 0, 144), R("M1", 0, 144), A.add)
     ts(R("HB", 0, 64), R("I3", 0, 64), 2047.0 - 192 - 2048, A.add, 0.5, A.mult)
-    ts(R("HB", 64, 128), R("JB", 0, 64), -2048.0, A.add, 0.5, A.mult)
-    ts(R("JF", 0, 128), R("JB", 0, 128), col(2), A.add)
     fill(R("ONE", 0, 128), 1.0 / 128)
-    fill(R("TAU", 0, 16), 0.0)
-    for f in (live_count, live_bound):
-        for h in range(2):
-            f(h)
+    ts(R("Z2", 0, 144), R("M1", 0, 144), 0.5, A.mult)
     picks_count(0)
+    ts(R("KT", 0, 64), R("I3", 0, 64), col(2), A.add)
+    ts(R("ID", 0, 128), R("I1", 16, 144), 0.0, A.is_equal)
+    ts(col(13), col(2), 1.0, A.add)
+    move("p", R("PS", 512, 1024), R("KK", 512, 1024))
+    ts(R("JF", 0, 128), R("JB", 0, 128), col(2), A.add)
+    picks_slots(0)
+    picks_scatter(0)
     for h in range(2):
         cp(R("A16", 64 * h, 64 * h + 64), R("RAI", 0, 64))
         cp(R("B16", 64 * h, 64 * h + 64), R("RBI", 0, 64))
+        cp(R("AB16", 64 * h, 64 * h + 64), R("RBI" if h else "RAI", 0, 64))
+        ts(R("PM", 128 * h, 128 * h + 128), R("I4", 0, 128), col(13), A.is_equal, 8192.0, A.mult)
+    ts(R("Z1", 0, 144), R("M0", 0, 144), delta / 2, A.mult)
+    ts(R("HB", 64, 128), R("JB", 0, 64), -2048.0, A.add, 0.5, A.mult)
     ts(R("YE", 0, 32), R("JF", 0, 32), float(ET + SO * q), A.add)
     ts(R("YE", 32, 64), R("JF", 0, 32), 16.0, A.add)
-    picks_slots(0)
+    fill(R("TAU", 0, 16), 0.0)
     for i in range(3):
         back(i)
-    fill(R("DD", 0, 1216), 0.0)
+    if OPT["wide"]:
+        wide_constants()
+    picks_extract()
+    picks_inv()
+    if late:
+        need("y", "lc")
+    for k in late:
+        dma("y", *loads[k])
+    for h in (1, 0):
+        picks_lists(0, h)
+    first_rates()
+    dma("y", R("RM", 1024, 2048), R("RM", 0, 1024), "cr")
+    need("y", "lw")
+    for k in "RO":
+        dma("y", *loads[k])
+    dma("y", R("POS", 0, SO), R("POS", SO, 2 * SO), "ci")
+    dma("y", R("TY", SO, 2 * SO), R("TY", 0, SO), "ci")
+    if OPT["slot"]:
+        dma("y", cold(0, SO), T.cin[:], "cd")
+        dma("y", cold(SO, SO + 384), T.cin[:, 0:384], "cd")
+        for lo in range(3072, ET + q * SO, SO):
+            dma("y", R("XG", lo, lo + SO), T.cin[:], "cd")
+    else:
+        fill(R("DD", 0, 1216), 0.0)
+    if OPT["fold"]:
+        fill(R("ON1", 0, 512), 1.0)
 
     for t in range(TR):
-        wn, wo = (W0, W1) if t % 2 == 0 else (W1, W0)
-        if t == 0:
-            first_rates()
-        else:
-            rates(t, wn, wo)
-        sweeps(t, wn)
+        a_round(t)
 
     for sem in SEMAPHORES:
         if total[sem]:

@@ -6,109 +6,50 @@ W0, W1 = 0, 5120
 ET = 4096
 U = 256
 OPT = dict(
-    bb=2048, war=0, tb=(0, 1), join=0, more0="", tree=8, slot=0, fold=0, wide="", k8="",
-    round="se r104 pc r204 ps aL Ls01 Ls12 Ls23 Ls34 px lk01 lk12 lk23 lk34 o0 ct mv02 M0 ws02 o1 mv24 M1 ws24 pi b0 pj b1 lo b2 lr tv "
-          "W_ aE Fs02 Es8c Ev48 Cp8c Cv48 aM P_02 ms24 P_24 Dp24 z_04 ms48 P_48 ms8c P_8c z_48 mscg P_cg z_8c z_cg w1 "
-          "aW Xs04 Xs48 Xs8c ms02 T108 T18c T2 T3 Ds8c Dpcg Dp48 ao "
-          "aF Q_02 es24 Q_24 Z_02 es8c Q_8c Z_24 escg Q_cg Z_8c es48 Q_48 Z_cg Z_48 Kp04 aC Ra04 Rb04 cl w20 w21 g_0 g_1 t_0 t_1", loads="ceabko rt",
-    e="a", m="ad", w="ad", f="d", l="d", e0="a", m0="ad", w0="ad",
-    rates="se r104 pc r204 ps aL Ls01 Ls12 Ls23 Ls34 px lk01 lk12 lk23 lk34 o0 ct mv02 M0 ws02 o1 mv24 M1 ws24 pi b0 pj b1 lo b2 lr tv",
-    ahead="W_ aE Fs02 Es8c Ev48 Cp8c Cv48",
-    first="W_ aE tv Fs02 Es8c Ev48 Cp8c Cv48",
-    one="aM P_02 ms24 P_24 Dp24 z_04 ms48 P_48 ms8c P_8c z_48 mscg P_cg z_8c z_cg w1",
-    amounts="aW Xs04 Xs48 Xs8c ms02 T108 T18c T2 T3 Ds8c Dpcg Dp48 ao",
-    two="aF Q_02 es24 Q_24 Z_02 es8c Q_8c Z_24 escg Q_cg Z_8c es48 Q_48 Z_cg Z_48",
-    next="Kp04 aC Ra04 Rb04 cl",
-    tail="w20 w21 g_0 g_1 t_0 t_1")
-
-OPT.update(slot=1, m="dd", m0="dd", e0="d", e="d", w="dd", w0="dd", wide="1", loads="ceabkort|", k8="W_", more0="Es48 Cv48",
-           round="se r104 pc r204 ps aL Ls01 Ls12 Ls23 Ls34 px lk01 lk12 lk23 lk34 ct o0 mv02 M0 "
-                 "ws02 o1 mv24 M1 ws24 pi pj lo aE Fs02 Es8c Cp8c lr b0 b1 b2 tv W_ "
-                 "aM P_02 ms24 P_24 Dp24 ms48 z_04 P_48 ms8c P_8c mscg z_4c P_cg z_cg w1 "
-                 "aW Xs04 Xs48 Xs8c ms02 Ds8c cs T108 Dpcg T18c T2 T3 T4 Dp48 "
-                 "aF Q_02 es24 Q_24 es8c Z_04 Q_8c cw escg Z_8c Q_cg es48 Z_cg Q_48 Z_48 Kp04 aC Ra04 Rb04 cl "
-                 "w20 w21 g_0 g_1 t_0 t_1")
-OPT.update(slot=0, m="ad", m0="ad", e0="a", e="a", w="ad", w0="ad", wide="", k8="", tree=12,
-           round="se r104 pc r204 ps aL Ls01 Ls12 Ls23 Ls34 px lk01 lk12 lk23 lk34 o0 ct mv02 M0 ws02 o1 mv24 M1 ws24 pi b0 pj b1 lo b2 lr tv "
-                 "W_ aE Fs02 Es8c Cp8c aM P_02 ms24 P_24 Dp24 z_04 ms48 P_48 ms8c P_8c z_48 mscg P_cg z_8c z_cg w1 "
-                 "aW Xs04 Xs48 Xs8c ms02 T108 T18c T2 T3 Ds8c Dpcg Dp48 ao "
-                 "aF Q_02 es24 Q_24 Z_02 es8c Q_8c Z_24 escg Q_cg Z_8c es48 Q_48 Z_cg Z_48 Kp04 aC Ra04 Rb04 cl w20 w21 g_0 g_1 t_0 t_1")
-OPT.update(slot=1, wide="1", k8="W_", more0="Es48 Cv48", tree=8,
-           round="se r104 pc r204 ps aL Ls01 Ls12 Ls23 Ls34 px lk01 lk12 lk23 lk34 ct o0 mv02 M0 "
-                 "ws02 o1 mv24 M1 ws24 pi pj lo aE Fs02 Es8c Cp8c lr b0 b1 b2 tv W_ "
-                 "aM P_02 ms24 P_24 Dp24 ms48 z_04 P_48 ms8c P_8c mscg z_4c P_cg z_cg w1 "
-                 "aW Xs04 Xs48 Xs8c ms02 Ds8c cs T108 Dpcg T18c T2 T3 T4 Dp48 "
-                 "aF Q_02 es24 Q_24 es8c Z_04 Q_8c cw escg Z_8c Q_cg es48 Z_cg Q_48 Z_48 Kp04 aC Ra04 Rb04 cl "
-                 "w20 w21 g_0 g_1 t_0 t_1")
-OPT.update(slot=0, wide="", k8="", m="dd", m0="dd", e0="d", e="d", w="d", w0="d",
-           round="se r104 pc r204 ps aL Ls12 Ls24 px Lv01 lk01 lk12 lk24 o0 ct mv02 M0 "
-                 "ws02 o1 mv24 M1 ws24 pi pj lo aE Fs04 Es8c Cp8c lr b0 b1 b2 tv W_ "
-                 "aM P_04 ms48 z_04 P_48 ms8c P_8c z_48 mscg P_cg z_8c z_cg w1 "
-                 "aW Ys04 Ys48 Ys8c ms04 V1 Dp8c V2 V3 Dp24 Dpcg Dp48 ao "
-                 "aF Q_02 es24 Q_24 Z_02 es8c Q_8c Z_24 escg Q_cg Z_8c es48 Q_48 Z_cg Z_48 Kp04 aC Ra04 Rb04 cl w20 w21 g_0 g_1 t_0 t_1")
-OPT.update(tree=12,
-           round="se r104 pc r204 ps aL Ls12 Ls24 px Lv01 lk01 lk12 lk24 ct o0 mv02 M0 ws02 o1 mv24 M1 ws24 pi pj lo aE Es8c Cp8c lr W_ Fv04 b0 b1 b2 tv "
-                 "aM P_04 ms48 z_04 P_48 cd ms8c P_8c z_48 mscg P_cg z_8c z_cg w1 aW Xs04 Xs48 Xs8c ms04 Ds8c T108 T18c T2 T3 Dpcg Dp48 ao "
-                 "aF Q_04 es8c Q_8c escg Z_04 Q_cg es48 Z_8c Q_48 Z_cg Z_48 Kp04 aC Rs w20 w21 g_0 g_1 t_0 t_1")
-OPT.update(round="se r104 pc r204 ps aL Ls12 Ls24 px Lv01 lk01 lk12 lk24 ct o0 mv02 M0 ws02 o1 mv24 M1 ws24 pi pj lo aE Fs04 Es8c Cp8c lr W_ b0 b1 b2 tv "
-                 "aM P_04 ms48 z_04 P_48 cd ms8c P_8c z_48 mscg P_cg z_8c z_cg w1 aW Xs04 Xs48 Xs8c Bs0c ms04 Dp24 T50c Ds8c T2 T3 Dpcg Dp48 ao "
-                 "aF Q_02 es24 Q_24 Z_02 es8c Q_8c Z_24 escg Q_cg Z_8c es48 Q_48 Z_cg Z_48 Kp04 aC Rs w20 w21 g_0 g_1 t_0 t_1")
-OPT.update(fold=0, wide="1",
-           round="se r104 pc r204 ps aL Ls12 Ls24 px Lv01 lk01 lk12 lk24 ct o0 mv02 M0 ws02 o1 mv24 M1 ws24 pi pj lo aE Fs04 Es8c Cp8c lr b0 b1 b2 tv W_ "
-                 "aM P_04 ms48 z_04 P_48 cd ms8c P_8c z_48 mscg P_cg z_8c z_cg w1 aW Xs04 Xs48 Xs8c ms04 Dp24 T108 T18c Ds8c T2 T3 Dpcg Dp48 ao "
-                 "aF Q_02 es24 Q_24 Z_02 es8c Q_8c Z_24 escg Q_cg Z_8c es48 Q_48 Z_cg Z_48 Kp04 aC Ra04 Rb04 w20 w21 g_0 g_1 t_0 t_1")
-OPT.update(wide="", war=0,
-           round="r104 pc w3 se r204 ps aL Ls12 Ls24 px Lv01 lk01 lk12 lk24 o0 ct mv02 M0 ws02 o1 mv24 M1 ws24 pi pj lo aE Fs04 Es8c Cp8c lr b0 b1 b2 tv th W_ "
-                 "aM P_04 ms48 z_04 P_48 ms8c P_8c z_48 mscg P_cg z_8c z_cg w1 aW Xs04 Xs48 Xs8c Bs0c ms04 Dp24 T50c Ds8c T2 T3 Dpcg Dp48 ao "
-                 "aF Q_02 es24 Q_24 Z_02 es8c Q_8c Z_24 escg Q_cg Z_8c es48 Q_48 Z_cg Z_48 Kp04 aC Ra04 Rb04 cl h_0 h_1 t_0 t_1")
-OPT.update(bb=0, tree=12,
-           round="se r104 pc r204 ps aL Ls02 Ls24 px lk02 lk24 o0 ct mv02 M0 ws02 o1.0 pi o1.1 o1.2 mv24 M1 ws24 pj lo aE Fs04 lr b0 b1 b2 tv W_ "
-                 "aM P_04 ms8c z_04 Dp8c P_8c cd ms48 z_8c P_48 mscg z_48 P_cg z_cg w1 aW As04 As48 As8c Bs0c ms04 T50c Ds24 S2 S5 Dpcg Dp48 ao "
-                 "aF Q_02 es24 Q_24 Z_02 es8c Q_8c Z_24 escg Q_cg Z_8c es48 Q_48 Z_cg Z_48 Kp04 aC Rs w20 w21 g_0 g_1 t_0 t_1")
-OPT.update(k8="W_", more0="Escg Cpcg",
-           round="se r104 pc r204 ps.0 ps.1 ps.2 ps.3 ps.4 ps.5 aL Lv01 ps.6 Ls12 Ls24 px lk01 lk12 lk24 o0 ct mv02 M0 ws02 o1.0 b0 o1.1 b1 o1.2 b2 mv24 M1 ws24 "
-                 "ts pi pj lo aE Fs24 lr W_ Fv02 Ev45 Cp45 "
-                 "aM P_04 ms8c Dp8c P_8c cd ms48 z_04 P_58 P_45 mscg z_8c P_cg z_48 z_cg w1 aW As04 As48 As8c Bs0c ms04 T50c Ds24 S2 S5 Dpcg Dp48 ao.0 "
-                 "aF Q_02 ao.1 es24 Q_24 Z_02 es8c Q_8c Z_24 escg Q_cg Z_8c es48 Q_48 Z_cg Z_48 Kp04 aC Rs w20 w21 g_0 g_1 t_0 t_1")
+    end="W201 W212",
+    first="xtt xta xj1 xj0 xbv xcc xc4 xm1 xc6 xn0 xc5 xcd xm0 xiv xon xn1 xrh xmx xg0 xc8 xg1 xn2 xt0 xp0 xty xhb xt1 xb0 xdd xa0 xz2 xid xp1 "
+          "pc xzc xz1 xcp xkt xy0 xa1 ps.0 xzm ps.1 ps.2 xzp ps.3 ps.4 xy1 xa2 ps.5 xzd ps.6 xb2 KP24 xb1 "
+          "AC RA24 RB24 b0 f101 f112 f201 f212 q_02 M0 r124 b1 px f324 b2 q_24 M1 xll ts pi pj lo lr W_ "
+          "aE Fs02 Ev46 Cp46 cd Fv23 Fs34 aM P_02 P_24 ms8c ms48 z_02 z_24 P_8c mscg P_46 Dp8c z_8c P_68 P_cg z_48 z_cg",
+    head="RB24 w3 se pc.0 r123 pc.1 r134 pc.2 r202 r224 ps.0 ps.1 "
+         "aL Ls12 Ls24 Lv01 ps.3 ps.2 lk01 ps.4 lk12 ps.5 sa lk24 ps.6 o0 cu mv02 M0 b0 o1 mv24 M1 "
+         "px pi pj lo lr aE ws02 ws24 W_ Fs24 b1 Fv12 b2 ts Fv01 Ev45 Cp45 "
+         "aM ms8c P_02 cd P_24 Dp8c ms48 z_02 mscg z_24 P_8c P_45 P_58 P_cg z_8c z_48 z_cg",
+    rest="aW As04 As48 As8c Bs0c th01 w1 T506 T56c ms04 Dpcg U206 U306 U26c U36c aF U406 U506 U46c U56c U606 Ds24 es24 U66c th12 "
+         "c101 c112 c201 Q_02 c212 c3 Q_24 Dp48 es8b esbe eseg es48 Z_02 Z_24 Q_8b Q_be Z_8b aC Kp04 Q_eg Z_be Q_48 Z_eg "
+         "Ra04 Rb02 Z_48 h_01 h_12 +r102 t_01 t_12")
 f32, bf, f16, i32, u16 = "float32", "bfloat16", "float16", "int32", "uint16"
 SCRATCH = {
     "BIG": ("sbuf", [128, 10240], f32), "EA": ("sbuf", [128, 6144], f32), "EB": ("sbuf", [128, 6144], f32),
     "WM": ("sbuf", [128, 4096], f32), "MG": ("sbuf", [128, 4096], f32),
     "CT": ("sbuf", [128, 2048], f32), "LV": ("sbuf", [128, 2048], bf),
-    "XG": ("sbuf", [128, 6528], f32), "EG": ("sbuf", [128, 4096], f32), "RM": ("sbuf", [128, 2048], bf),
+    "XG": ("sbuf", [128, 4608], f32), "EG": ("sbuf", [128, 4096], f32), "RM": ("sbuf", [128, 2048], bf),
     "KK": ("sbuf", [128, 1024], f32), "TC": ("sbuf", [128, 2048], f32), "AB16": ("sbuf", [128, 128], u16), "BV": ("sbuf", [128, 256], f32),
-    "TAU": ("sbuf", [128, 528], f32), "TE": ("sbuf", [128, 512], f32), "CN": ("sbuf", [128, 512], f32),
+    "TAU": ("sbuf", [128, 528], f32), "TE": ("sbuf", [128, 512], f32),
+    "TB": ("sbuf", [128, 528], f32), "TH": ("sbuf", [128, 512], f32),
+    "CD": ("sbuf", [128, 896], f32), "CS": ("sbuf", [128, 256], f32),
     "RAI": ("sbuf", [128, 64], i32), "RBI": ("sbuf", [128, 64], i32),
     "A16": ("sbuf", [128, 128], u16), "B16": ("sbuf", [128, 128], u16),
-    "LI": ("sbuf", [128, 1920], i32), "ON1": ("sbuf", [128, 512], f32),
+    "LI": ("sbuf", [128, 1920], i32),
     "L16": ("sbuf", [128, 512], u16), "POS": ("sbuf", [128, 1024], f32), "INV": ("sbuf", [128, 1216], f32),
     "IH": ("sbuf", [128, 256], f32), "IV16": ("sbuf", [128, 16], u16), "PM": ("sbuf", [128, 256], f32),
-    "LA": ("sbuf", [128, 1024], bf), "ACT": ("sbuf", [128, 1024], bf), "SC": ("sbuf", [128, 1024], f16),
-    "TY": ("sbuf", [128, 1024], bf), "SCL": ("sbuf", [128, 512], f16), "CAR": ("sbuf", [128, 8], f32),
+    "LA": ("sbuf", [128, 1024], bf), "ACT": ("sbuf", [128, 1024], bf), "SC": ("sbuf", [128, 1024], f16), "CAP": ("sbuf", [128, 1024], bf),
+    "TY": ("sbuf", [128, 512], bf), "SCL": ("sbuf", [128, 512], f16), "CAR": ("sbuf", [128, 8], f32),
     "FL": ("sbuf", [128, 512], bf), "MX": ("sbuf", [128, 128], bf),
-    "Z1": ("sbuf", [128, 144], bf), "Z2": ("sbuf", [128, 144], f16),
-    "ID": ("sbuf", [128, 128], f32), "RH": ("sbuf", [128, 128], bf), "HB": ("sbuf", [128, 128], bf),
-    "ONE": ("sbuf", [128, 128], bf), "JB": ("sbuf", [128, 128], bf), "JF": ("sbuf", [128, 128], f32),
+    "Z1": ("sbuf", [128, 144], bf), "Z2": ("sbuf", [128, 144], f16), "ZD": ("sbuf", [128, 144], f16),
+    "ZP": ("sbuf", [128, 144], f16), "ZM": ("sbuf", [128, 128], f16),
+    "ID": ("sbuf", [128, 128], f32), "RH": ("sbuf", [128, 128], bf), "HB": ("sbuf", [128, 64], bf),
+    "ONE": ("sbuf", [128, 128], bf), "JB": ("sbuf", [128, 128], bf), "JF": ("sbuf", [128, 32], f32),
     "PI": ("sbuf", [128, 8], i32), "PJ": ("sbuf", [128, 8], i32), "COL": ("sbuf", [128, 16], f32),
-    "KT": ("sbuf", [128, 64], f32), "YE": ("sbuf", [128, 64], f32), "SM": ("sbuf", [128, 512], f32),
+    "KT": ("sbuf", [128, 64], f32), "YE": ("sbuf", [128, 64], f32), "SM": ("sbuf", [128, 320], f32),
     "SL16": ("sbuf", [128, 32], u16), "OE16": ("sbuf", [128, 64], u16), "SEL": ("sbuf", [128, 64], u16),
-    "SX": ("sbuf", [128, 128], u16), "CS": ("sbuf", [128, 256], f32), "TH": ("sbuf", [128, 512], f32),
-    "Y2": ("sbuf", [128, 144], f16), "CL": ("sbuf", [128, 128], f16), "CR": ("sbuf", [128, 64], f16),
     "PS": ("psum", [128, 4096], f32),
 }
 INSIDE = {"TT": ("TC", 0), "CB": ("TC", 1024), "L1": ("EB", 0), "L2": ("EB", 768), "L3": ("EB", 1152), "DD": ("XG", 3072),
-          "M0": ("MG", 0), "M1": ("MG", 144), "I1": ("MG", 288), "I2": ("MG", 432), "I3": ("MG", 560), "I4": ("MG", 624)}
-SEMAPHORES = ["sv", "ss", "sp", "sg", "ldc", "lde", "ldl", "ldk", "ldx", "ldo", "ldt", "so", "cd", "ci", "cr", "cc", "co", "an", "ax", "ln",
-              "ac", "lc", "le", "lf", "ll", "lw", "lx"] + ["a%s%d" % (w, i) for w in "emwfl" for i in range(2)]
-
-
-def helpers(T, topo):
-    used, out = [], []
-    for c in T.cores:
-        h = [x for x in topo.cores_of(c) if x not in T.cores and x not in used and topo.die(x) != topo.die(c)][0]
-        used.append(h)
-        out.append((h, [d for d in T.cores if topo.die(d) != topo.die(c)], [d for d in T.cores if d != c and topo.die(d) == topo.die(c)]))
-    return out
+          "M0": ("MG", 0), "M1": ("MG", 144), "I1": ("MG", 288), "I2": ("MG", 432), "I3": ("MG", 560), "I4": ("MG", 624),
+          "M2": ("MG", 752), "M3": ("MG", 880), "M4": ("MG", 1008)}
+SEMAPHORES = ["sv", "ss", "sp", "sg", "ldc", "lde", "ldl", "ldk", "ldx", "ldo", "ldt", "so", "cd", "ci", "ce", "cc",
+              "ac", "lc", "le", "lf", "ll", "lw", "lx"] + ["a%s%d" % (w, i) for w in "emwfl" for i in range(3)]
 
 
 def dst_id(topo, c):
@@ -130,49 +71,21 @@ def as_mask(engines):
 
 def cyclic(p, a, b, width):
     lo, n = (p + a) % width, b - a
-    if n == width:
-        return [(0, width)]
-    return [(lo, lo + n)] if lo + n <= width else [(lo, lo + n // 2), (0, n // 2)]
+    return [(lo, lo + n)] if lo + n <= width else [(lo, width), (0, lo + n - width)]
 
 
 def pieces(q, t, what):
-    name, base, width, p, land, lsem = {"e": ("EA", ET + q * SO, SO, 0, "XG", "le"), "m": ("WM", q * RO, RO, 256 * t, "EA", "lw"),
-                                        "f": ("EB", ET + q * SO, SO, 0, "EG", "lf"),
-                                        "l": ("LV", q * SO, SO, 0, "LV", "ll"),
-                                        "w": ("BIG", (W1 if t % 2 else W0) + q * RO, RO, 0, "EB", "lx")}[what]
-    ways = OPT[what if t or what in "fl" else what + "0"]
-    n = width // len(ways)
-    return [(name, [(base + lo, base + hi) for lo, hi in cyclic(p, i * n, i * n + n, width)], way, land, t * width + i * n, "a%s%d" % (what, i), lsem)
-            for i, way in enumerate(ways)]
-
-
-def helper_program(g, core, T, topo, far):
-    qw = [i for i in range(N) if far[i][0] == core][0]
-    eng = common_engines(topo, core, far[qw][1])
-    seen = {}
-    for t in range(TR):
-        for what in "emwf":
-            for name, cols, way, land, at, rsem, _ in pieces(qw, t, what):
-                if way == "d":
-                    continue
-                to = far[qw][1]
-                seen[rsem] = seen.get(rsem, 0) + len(eng)
-                g.wait_ge(T.sem[rsem], seen[rsem])
-                wd = cols[0][1] - cols[0][0]
-                g.remote_dma_fused([RemoteDMATransfer(dst_ids=[dst_id(topo, c) for c in to], dma_engine_mask=as_mask(eng[i::len(cols)]),
-                                                      remote_sem=T.sem[rsem], src=T[land][:, at + i * wd:at + (i + 1) * wd],
-                                                      dsts=[T[name][:, lo:hi]] * len(to)) for i, (lo, hi) in enumerate(cols)],
-                                   local_sem=T.sem.le)
-    if seen:
-        g.wait_ge(T.sem.le, sum(seen.values()))
+    name, base, width, p, lsem = {"e": ("EA", ET + q * SO, SO, 0, "le"), "m": ("WM", q * RO, RO, 256 * t, "lw"),
+                                  "f": ("EB", ET + q * SO, SO, 0, "lf"), "l": ("LV", q * SO, SO, 0, "ll"),
+                                  "w": ("BIG", (W1 if t % 2 else W0) + q * RO, RO, 0, "lx")}[what]
+    k = 2 if what == "m" else 1
+    n = width // k
+    return [(name, [(base + lo, base + hi) for lo, hi in cyclic(p, i * n, i * n + n, width)], "a%s%d" % (what, i), lsem) for i in range(k)]
 
 
 def rank_program(g, core, T, topo):
     q = T.rank_of(core)
-    far = helpers(T, topo)
     if q is None:
-        if core in [f[0] for f in far]:
-            helper_program(g, core, T, topo, far)
         return
     others = [T.cores[(q + d) % N] for d in range(1, N)]
     eng = common_engines(topo, core, others)
@@ -218,16 +131,12 @@ def rank_program(g, core, T, topo):
                         x, y, hit = lo // 512 * 512, -(-hi // 512) * 512, True
                     if chain and k2 == k and name == "PS":
                         hit = False
-                    if OPT["war"] and wr and k2 == k and k in "vs" and sem == CS[k]:
-                        hit = False
                     if hit and a < y and x < b:
                         dep[sem] = max(dep.get(sem, 0), n)
         for sem in sorted(dep, key=lambda s: s not in CS.values()):
             wait(k, sem, dep[sem])
 
     def note(k, reads, writes, sem, n):
-        if "log" in OPT and q == 0:
-            OPT["log"].append((OPT["cur"], k, reads, writes))
         for name, lo, hi in writes:
             acc[name][:] = [e for e in acc[name] if not (lo <= e[0] and e[1] <= hi and (name != "PS" or e[3] == k))]
             acc[name].append((lo, hi, True, k, sem, n))
@@ -309,34 +218,25 @@ def rank_program(g, core, T, topo):
         Q[k].dma_start(out[0] if isap(out) else out, a[0] if isap(a) else a).then_inc(T.sem[sem], 16)
         note(k, reads, writes, sem, total[sem])
 
-    def send(parts, cs, lands, rsem, lsem):
+    def send(parts, rsem, lsem):
         if skipped("g"):
             return
-        reads = [r for p in parts for s in p for r in s[1]]
+        reads = [r for p in parts for r in p[1]]
         order("g", reads, [])
         n = len(parts)
-        g.remote_dma_fused([RemoteDMATransfer(dst_ids=[dst_id(topo, c) for c in cs], dma_engine_mask=as_mask(eng[i::n]),
-                                              remote_sem=T.sem[rsem], srcs=[s[0] for s in p], dsts=lands[i], alu_op=3 if len(p) > 1 else 0)
+        g.remote_dma_fused([RemoteDMATransfer(dst_ids=[dst_id(topo, c) for c in others], dma_engine_mask=as_mask(eng[i::n]),
+                                              remote_sem=T.sem[rsem], src=p[0], dsts=[p[0]] * len(others))
                             for i, p in enumerate(parts)], local_sem=T.sem[lsem])
         total[lsem] += NE
         note("g", reads, [], lsem, total[lsem])
 
-    def send_piece(t, what, i, source=None):
-        name, cols, way, land, at, rsem, lsem = pieces(q, t, what)[i]
-        to = [T[name][:, lo:hi] for lo, hi in cols]
-        parts = [source(lo, hi) if source else [R(name, lo, hi)] for lo, hi in cols]
-        if way == "d":
-            return send(parts, others, [[x] * len(others) for x in to], rsem, lsem)
-        near = far[q][2]
-        wd = cols[0][1] - cols[0][0]
-        send(parts, [far[q][0]] + near, [[T[land][:, at + j * wd:at + (j + 1) * wd]] + [x] * len(near) for j, x in enumerate(to)], rsem, lsem)
+    def send_piece(t, what, i):
+        name, cols, rsem, lsem = pieces(q, t, what)[i]
+        send([R(name, lo, hi) for lo, hi in cols], rsem, lsem)
 
     def send_block(t, what):
         for i in range(len(pieces(q, t, what))):
             send_piece(t, what, i)
-
-    def send_amounts(src):
-        send([[src]], others, [[cown[0]] * len(others)], "ac", "lc")
 
     def arrive_amounts():
         total["ac"] += (N - 1) * NE
@@ -344,14 +244,12 @@ def rank_program(g, core, T, topo):
 
     def arrive_block(t, what):
         for i, mine in enumerate(pieces(q, t, what)):
-            if what == "m" and t and i and "o2" in OPT["round"]:
-                continue
-            total[mine[5]] += (N - 1) * NE
-            note("x", [], [(mine[0], lo, hi) for r in range(N) if r != q for lo, hi in pieces(r, t, what)[i][1]], mine[5], total[mine[5]])
+            total[mine[2]] += (N - 1) * NE
+            note("x", [], [(mine[0], lo, hi) for r in range(N) if r != q for lo, hi in pieces(r, t, what)[i][1]], mine[2], total[mine[2]])
 
-    def extract(bank, z, src, lo, n, last=True):
+    def extract(bank, z, src, lo, n):
         for r in range(16):
-            mm(R("PS", 512 * bank, 512 * bank + n), R(z, 16 - r, 144 - r), R(src, lo + r, lo + 16 * n, 16), r == 0, last and r == 15)
+            mm(R("PS", 512 * bank, 512 * bank + n), R(z, 16 - r, 144 - r), R(src, lo + r, lo + 16 * n, 16), r == 0, False)
 
     cown = R("CT", q * SO, (q + 1) * SO)
     ctab = R("CT", 0, 2048)
@@ -365,41 +263,17 @@ def rank_program(g, core, T, topo):
     rxl = lambda lo, hi: R("L16", lo // 16, hi // 16)
     egat = lambda b, lo, hi: G(etab(b), R("L16", 256 + lo // 16, 256 + hi // 16))
     mgat = lambda lo, hi: G(mtab, rxl(lo, hi))
-    cold = lambda lo, hi: R("XG", ET + q * SO + lo, ET + q * SO + hi)
 
-    def extract8(bank, z, src, lo, const):
-        out = R("PS", 512 * bank, 512 * bank + 64)
-        for r in range(8):
-            mm(out, R(z, 16 - r, 144 - r), R(src, lo + r, lo + 512, 8), r == 0, False)
-        mm(out, R("CL", 0, 128), const, False, True)
-
-    def wide_constants():
-        cp(R("Y2", 0, 8), R("Z2", 0, 8))
-        tt(R("Y2", 8, 144), R("Z2", 8, 144), R("Z2", 0, 136), A.add)
-        ts(R("CL", 0, 128), R("I1", 16, 144), 0.0, A.is_equal)
-        ts(col(9), col(2), 8.0, A.is_lt)
-        ts(col(10), col(2), 8.0, A.is_ge)
-        ts(R("COL", 11, 13), R("COL", 9, 11), 2000.0, A.mult)
-        ts(sm(13), R("JF", 32, 64), 0.5, A.mult, 0.5 - 512.0, A.add)
-        for h in range(2):
-            ts(R("CR", h, 64, 2), sm(13), col(9 + h), A.mult, col(12 - h), A.add)
-
-    def live_count(h, ahead=False):
+    def live_count(lo, hi, ahead=False):
         if ahead:
-            tt(R("FL", 256 * h, 256 * h + 256), G(R("EB", 0, 6144), R("OE16", 16 * h, 16 * h + 16)), R("TH", 256 * h, 256 * h + 256), A.is_ge)
+            tt(R("FL", lo, hi), G(R("EB", 0, 6144), R("OE16", lo // 16, hi // 16)), R("TH", lo, hi), A.is_ge)
         else:
-            ts(R("FL", 256 * h, 256 * h + 256), eown("EA", 256 * h, 256 * h + 256), 0.125, A.is_ge)
-        mm(R("PS", 2048 + 512 * h, 2304 + 512 * h), R("MX", 0, 128), R("FL", 256 * h, 256 * h + 256), True, True)
+            ts(R("FL", lo, hi), eown("EA", lo, hi), 0.125, A.is_ge)
+        mm(R("PS", 2048 + 2 * lo, 2048 + lo + hi), R("MX", 0, 128), R("FL", lo, hi), True, True)
 
-    def live_bound(h):
-        out, a = R("LV", q * SO + 256 * h, q * SO + 256 * h + 256), R("PS", 2048 + 512 * h, 2304 + 512 * h)
+    def live_bound(lo, hi):
+        out, a = R("LV", q * SO + lo, q * SO + hi), R("PS", 2048 + 2 * lo, 2048 + lo + hi)
         op("s", out, [a, col(8)], lambda: g.scalar.activation(out[0], a[0], F.Sign, bias=col(8)[0]))
-
-    def counts(bank, src, lo, n, at):
-        out = R("PS", 512 * bank, 512 * bank + n)
-        extract(bank, "Z2", src, lo, n, last=False)
-        mm(out, R("ONE", 0, 128), R("HB", at, at + n), False, False)
-        mm(out, R("RH", 0, 128), R("ONE", 0, n), False, True)
 
     def picks_count(t):
         p = (128 * t) % SO
@@ -409,7 +283,10 @@ def rank_program(g, core, T, topo):
             scan(R("SCL", 0, p), R("TY", 0, p), R("LV", q * SO, q * SO + p), R("CAR", 0, 1), A.mult, A.add)
         else:
             part[1] += 2
-        counts(6, "SCL", 0, 32, 32 - 8 * (t % 4))
+        out, at = R("PS", 3072, 3104), 32 - 8 * (t % 4)
+        extract(6, "Z2", "SCL", 0, 32)
+        mm(out, R("ONE", 0, 128), R("HB", at, at + 32), False, False)
+        mm(out, R("RH", 0, 128), R("ONE", 0, 32), False, True)
 
     def picks_slots(t):
         y = R("PS", 3072, 3104)
@@ -421,10 +298,6 @@ def rank_program(g, core, T, topo):
         tt(sm(4), sm(3), sm(1), A.add)
         tt(sm(5), sm(2), sm(4), A.min)
         ts(R("SL16", 0, 32), sm(5), 2047.0, A.add)
-
-    def slots_clear():
-        out, a = R("INV", 0, 256), R("POS", 0, 256)
-        op("s", out, [a], lambda: g.scalar.activation(out[0], a[0], F.Silu, scale=4.0))
 
     def picks_scatter(t):
         p = (128 * t) % SO
@@ -460,36 +333,17 @@ def rank_program(g, core, T, topo):
         else:
             move(k, R("PS", lo, hi), R(name, lo, hi))
 
-    def first_rates():
-        wq = lambda a, b: R("BIG", W0 + q * RO + a, W0 + q * RO + b)
-        wm = lambda a, b: R("WM", q * RO + a, q * RO + b)
-        arrive_amounts()
-        act(R("TT", 512, 1024), G(ctab, R("A16", 32, 64)))
-        act(R("CB", 512, 1024), G(ctab, R("B16", 32, 64)))
-        tt(R("TT", 0, 512), G(ctab, R("A16", 0, 32)), R("KK", 0, 512), A.mult)
-        tt(wq(0, 512), G(ctab, R("B16", 0, 32)), R("TT", 0, 512), A.mult)
-        ts(wm(0, 512), wq(0, 512), 1.0, A.min)
-        if len(OPT["m0"]) == 2:
-            send_piece(0, "m", 0)
-        tt(R("PS", 512, 1024), R("TT", 512, 1024), R("PS", 512, 1024), A.mult)
-        tt(wq(512, 1024), R("CB", 512, 1024), R("PS", 512, 1024), A.mult)
-        ts(wm(512, 1024), wq(512, 1024), 1.0, A.min)
-        send_piece(0, "m", len(OPT["m0"]) - 1)
-
     def a_round(t):
         wn, wo = (W0, W1) if t % 2 == 0 else (W1, W0)
         last = t == TR - 1
         x0 = 16 * (t % 4)
-        p = (128 * t) % SO
         win = R("BIG", wo + q * RO, wo + 5120)
         wtab = R("BIG", wn, wn + 4096)
         wown = lambda lo, hi: R("BIG", wn + q * RO + lo, wn + q * RO + hi)
         at = lambda i: R("PS", 2048 + 512 * i, 2080 + 512 * i)
         ps = lambda lo, hi, step=1: R("PS", 1024 + lo, 1024 + hi, step)
         x = lambda e, lo, hi: R("XG", lo + e, hi, 4)
-        have = {k: set() for k in "FCDGH"}
-        A_END = OPT["tree"] * U
-        TB = OPT["tb"]
+        have = {k: set() for k in "FCDG"}
 
         def places(a, b):
             for lo, hi in cyclic(256 * t, a, b, RO):
@@ -504,20 +358,22 @@ def rank_program(g, core, T, topo):
             units = set(range(lo // U, hi // U))
             if k == "se":
                 send_block(t, "e")
+            elif k == "AC":
+                arrive_amounts()
+            elif k == "KP":
+                to_psum("p", "KK", lo, hi)
             elif k[0] == "a" and k != "ao":
                 if k == "aC":
                     arrive_amounts()
                 else:
                     arrive_block(t, k[1].lower())
                 if k == "aW" and last:
-                    for pc in pieces(q, t, "w"):
-                        need("y", pc[5])
+                    need("y", "aw0")
                     dma("y", T.yw[:], wown(0, RO), "so")
             elif k == "r1":
-                tt(R("PS", lo, hi), R("TT", lo, hi), R("PS", lo, hi), A.mult)
+                for a, b in cyclic(256 * t, lo, hi, RO):
+                    tt(R("PS", a, b), R("TT", a, b), R("PS", a, b), A.mult)
             elif k == "r2":
-                tt(R("BIG", wo + 4096 + lo, wo + 4096 + hi), R("CB", lo, hi), R("PS", lo, hi), A.mult)
-            elif k == "r3":
                 for a, b in cyclic(256 * t, lo, hi, RO):
                     tt(R("BIG", wo + 4096 + a, wo + 4096 + b), R("CB", a, b), R("PS", a, b), A.mult)
             elif k == "pc":
@@ -536,83 +392,28 @@ def rank_program(g, core, T, topo):
                 back(int(k[1]))
             elif k in ("tv", "ts"):
                 move(k[1], R("TE", 0, SO), G(R("TAU", 0, 528), R("OE16", 32, 64)))
+            elif k in ("uv", "us"):
+                move(k[1], R("TH", 0, SO), G(R("TB", 0, 528), R("OE16", 32, 64)))
             elif k[0] == "L":
-                move(k[1], R("LA", lo, hi), G(lvtab, R("A16", x0 + lo // 16, x0 + hi // 16)))
+                out, src = R("LA", lo, hi), G(lvtab, R("A16", x0 + lo // 16, x0 + hi // 16))
+                if k == "Ls":
+                    act(out, src, -1.0)
+                else:
+                    ts(out, src, -1.0, A.mult)
             elif k == "lk":
-                tt(R("ACT", lo, hi), G(lvtab, R("B16", x0 + lo // 16, x0 + hi // 16)), R("LA", lo, hi), A.max)
-                if hi == 512 and "0" in OPT["wide"]:
-                    extract8(4, "Y1", "ACT", 0, R("CR", 2 * x0, 2 * x0 + 64))
-                elif hi == 512:
-                    extract(4, "Z1", "ACT", 0, 32, last=False)
+                tt(R("ACT", lo, hi), G(lvtab, R("B16", x0 + lo // 16, x0 + hi // 16)), R("LA", lo, hi), A.is_ge)
+                if hi == 512:
+                    extract(4, "Z1", "ACT", 0, 32)
                     mm(at(0), R("ONE", 0, 128), R("JB", x0, x0 + 32), False, True)
             elif k == "ct":
-                scan(R("SC", 0, RO), R("TY", 0, RO), R("ACT", 0, RO), 0.0, A.mult, A.add)
-                if "1" in OPT["wide"]:
-                    extract8(5, "Y2", "SC", 512, R("CR", 0, 64))
-                else:
-                    counts(5, "SC", 512, 32, 96)
-            elif k == "o0" and "0" in OPT["wide"]:
-                ts(R("SM", 448, 512), R("PS", 2048, 2112), col(7), A.add, 0.0, A.max)
-                tt(sm(10), R("SM", 448, 512, 2), R("SM", 449, 512, 2), A.add)
-                cp(R("SEL", 0, 32), sm(10))
-            elif k == "o0":
-                ts(R("SEL", 0, 32), at(0), col(7), A.add)
-            elif k == "o1" and "1" in OPT["wide"]:
-                ts(R("SM", 352, 416), R("PS", 2560, 2624), -1024.0, A.is_le, delta, A.mult)
-                tt(sm(13), R("SM", 352, 416, 2), R("JF", x0 + 32, x0 + 64), A.add)
-                tt(sm(13), sm(13), R("SM", 353, 416, 2), A.add)
-                cp(R("SEL", 32, 64), sm(13))
-            elif k == "o1":
-                ts(sm(11), at(1), 512.0 - 2048.0, A.is_le, delta, A.mult)
-                tt(sm(13), sm(11), R("JF", x0 + 32, x0 + 64), A.add)
-                cp(R("SEL", 32, 64), sm(13))
-            elif k == "oc":
-                need("y", "ll")
-                for r in range(N):
-                    a = 0
-                    for b, c in cyclic(256 * t, 512, RO, RO):
-                        dma("y", R("MG", RO * r + a, RO * r + a + c - b), R("WM", RO * r + b, RO * r + c), "co")
-                        a += c - b
-            elif k == "nm":
-                a = 0
-                for b, c in cyclic(256 * t, 512, RO, RO):
-                    ts(R("MG", RO * q + 512 + a, RO * q + 512 + a + c - b), R("BIG", wo + 4096 + b, wo + 4096 + c), 1.0, A.min)
-                    a += c - b
-            elif k == "N_":
-                total["an"] += (N - 1) * NE
-                need("g", "al0")
-                mine = R("MG", RO * q + 512, RO * q + RO)
-                send([[mine]], others, [[mine[0]] * len(others)], "an", "ln")
-                note("x", [], [("MG", RO * r + 512, RO * r + RO) for r in range(N) if r != q], "an", total["an"])
-            elif k == "o2":
-                if "1" in OPT["wide"]:
-                    ts(R("SM", 448, 512), R("PS", 2560, 2624), -1024.0, A.is_le, 512.0, A.mult)
-                    tt(sm(10), R("SM", 448, 512, 2), R("JF", 0, 32), A.add)
-                    tt(sm(10), sm(10), R("SM", 449, 512, 2), A.add)
-                else:
-                    ts(sm(14), at(1), 512.0 - 2048.0, A.is_le, 512.0, A.mult)
-                    tt(sm(10), sm(14), R("JF", 0, 32), A.add)
-                mine = R("SX", 32 * q, 32 * q + 32)
-                cp(mine, sm(10))
-                send([[mine]], others, [[mine[0]] * len(others)], "ax", "ln")
-                total["ax"] += (N - 1) * NE
-                note("x", [], [("SX", 32 * r, 32 * r + 32) for r in range(N) if r != q], "ax", total["ax"])
-            elif k in ("gv", "gs"):
-                d, h0, h1 = arg
-                r = (q + d) % N
-                for b, c in cyclic(256 * t, 512 + 128 * h0, 512 + 128 * h1, RO):
-                    a = (b - 256 * t - 512) % RO
-                    move(k[1], R("WM", RO * r + b, RO * r + c), G(R("MG", RO * r, RO * r + RO), R("SX", 32 * r + a // 16, 32 * r + (a + c - b) // 16)))
-            elif k == "th":
-                ts(R("TH", 0, SO), R("TE", 0, SO), 0.125, A.is_lt, 0.125, A.mult)
-            elif k == "h_":
-                live_count(arg[0], True)
-            elif k == "w3":
-                writeback("EB", "EA", 0, SO)
-            elif k == "cw" and False:
-                pass
-            elif k == "k8":
-                wide_constants()
+                scan(R("SC", 0, RO), R("ACT", 0, RO), R("CAP", 0, RO), 0.0, A.add, A.min)
+                mm(at(1), R("ZM", 0, 128), R("SC", 511, RO - 1, 16), True, False)
+                for r in range(16):
+                    mm(at(1), R("ZD" if r < 15 else "ZP", 16 - r, 144 - r), R("SC", 512 + r, RO, 16), False, False)
+                mm(at(1), R("ONE", 0, 128), R("JB", x0 + 32, x0 + 64), False, True)
+            elif k[0] == "o":
+                h = int(k[1])
+                ts(R("SEL", 32 * h, 32 * h + 32), at(h), col(2), A.add)
             elif k == "mv":
                 for a, b, src in places(lo, hi):
                     ts(R("WM", q * RO + a, q * RO + b), src, 1.0, A.min)
@@ -624,14 +425,12 @@ def rank_program(g, core, T, topo):
                     ts(R("WM", q * RO + a, q * RO + b), wown(a, b), 1.0, A.min)
             elif k[0] == "M":
                 send_piece(t, "m", int(k[1]))
-            elif k[0] == "U":
-                send_piece(t, "m", int(k[1]), lambda a, b: [wown(a - q * RO, b - q * RO), R("ON1", 0, b - a)])
             elif k == "W_":
                 send_block(t, "w")
-            elif k[0] == "W":
-                send_piece(t, "w", int(k[1]))
-            elif k[0] == "E":
+            elif k[0] in "EG":
                 move(k[1], R("EG", lo, hi), egat("EA", lo, hi))
+                if k[0] == "G":
+                    have["G"] |= units
             elif k[0] == "F":
                 move(k[1], R("EA", lo, hi), egat("EA", lo, hi))
                 have["F"] |= units
@@ -643,135 +442,122 @@ def rank_program(g, core, T, topo):
             elif k == "P_":
                 if units <= have["C"]:
                     tt(R("EG", lo, hi), R("MG", lo, hi), R("PS", lo, hi), A.mult)
+                elif units <= have["G"] & have["D"]:
+                    tt(R("EG", lo, hi), R("EG", lo, hi), R("PS", lo, hi), A.mult)
                 elif units <= have["F"]:
                     tt(R("EG", lo, hi), mgat(lo, hi), R("EA", lo, hi), A.mult)
-                elif units <= have["G"]:
-                    tt(R("MG", lo, hi), mgat(lo, hi), R("EG", lo, hi), A.mult)
                 else:
                     tt(R("EG", lo, hi), egat("EA", lo, hi), R("MG", lo, hi), A.mult)
             elif k in ("z_", "Z_"):
-                src = "MG" if (k == "z_" and units <= have["G"] - have["C"]) or (k == "Z_" and units <= have["H"]) else "EG"
-                scan(R("EA" if k == "z_" else "EB", lo, hi), R("RM", 0, hi - lo), R(src, lo, hi), 0.0, A.min, A.max)
-            elif k[0] == "G":
-                move(k[1], R("EG", lo, hi), egat("EA", lo, hi))
-                have["G"] |= units
+                scan(R("EA" if k == "z_" else "EB", lo, hi), R("RM", 0, hi - lo), R("EG", lo, hi), 0.0, A.min, A.max)
             elif k == "cd":
+                need("y", "lw")
                 dma("y", R("INV", 0, 256), R("BV", 0, 256), "cc")
-            elif k in ("Rs", "RS"):
+            elif k == "Rs":
                 act(R("TC", 0, 2048), G(ctab, R("AB16", 0, 128)))
-            elif k == "g2":
-                for h in range(2):
-                    ts(R("FL", 256 * h, 256 * h + 256), eown("EA", 256 * h, 256 * h + 256), 0.125, A.is_ge)
-                    mm(R("PS", 2048 + 256 * h, 2304 + 256 * h), R("MX", 0, 128), R("FL", 256 * h, 256 * h + 256), True, True)
-                out, a = R("LV", q * SO, q * SO + SO), R("PS", 2048, 2560)
-                op("s", out, [a, col(8)], lambda: g.scalar.activation(out[0], a[0], F.Sign, bias=col(8)[0]))
-                send_piece(t + 1, "l", 0)
+            elif k in ("Ra", "Rb", "RA", "RB"):
+                for a, b in cyclic(256 * (t + k[1].islower()), lo, hi, RO):
+                    act(R("TT" if k[1] in "aA" else "CB", a, b), G(ctab, R("A16" if k[1] in "aA" else "B16", a // 16, b // 16)))
+            elif k == "r3":
+                for a, b in cyclic(256 * t, lo, hi, RO):
+                    tt(R("TT", a, b), G(ctab, R("A16", a // 16, b // 16)), R("KK", a, b), A.mult)
+            elif k == "r4":
+                for a, b in cyclic(256 * t, lo, hi, RO):
+                    tt(R("BIG", wo + 4096 + a, wo + 4096 + b), G(ctab, R("B16", a // 16, b // 16)), R("TT", a, b), A.mult)
+            elif k == "f1":
+                tt(R("TT", lo, hi), G(ctab, R("A16", lo // 16, hi // 16)), R("KK", lo, hi), A.mult)
+            elif k == "f2":
+                tt(wown(lo, hi), G(ctab, R("B16", lo // 16, hi // 16)), R("TT", lo, hi), A.mult)
+            elif k == "f3":
+                tt(wown(lo, hi), R("CB", lo, hi), R("PS", lo, hi), A.mult)
             elif k == "w1":
                 writeback("EA", "EB", 0, SO)
                 send_block(t, "f")
-            elif k == "Xs":
-                act(R("XG", lo, hi), G(wtab, rxl(lo, hi)), 0.125)
-                if hi <= A_END:
-                    ident(ps(lo // 4, hi // 4), [x(0, lo, hi), x(1, lo, hi)])
-            elif k in ("Ys", "Yv"):
-                if k == "Ys":
-                    act(R("XG", lo, hi), G(wtab, rxl(lo, hi)), 0.125)
-                else:
-                    ts(R("XG", lo, hi), G(wtab, rxl(lo, hi)), 0.125, A.mult)
-                y = lambda e: R("XG", lo + e, hi, 8)
-                bank = lambda b: R("PS", 512 * b + lo // 8, 512 * b + hi // 8)
-                ident(bank(TB[0]), [y(3)])
-                ident(bank(TB[1]), [y(7)])
-                if OPT["join"]:
-                    mm(bank(2), R("ID", 0, 128), y(0), lo == 0, False)
-                    mm(bank(2), R("ID", 0, 128), y(1), False, False)
-                else:
-                    ident(bank(2), [y(0), y(1)])
-                ident(bank(3), [y(4), y(5)])
             elif k == "As":
                 act(R("XG", lo, hi), G(wtab, rxl(lo, hi)), 0.125)
                 y = lambda e: R("XG", lo + e, hi, 8)
                 bank = lambda b: R("PS", 512 * b + lo // 8, 512 * b + hi // 8)
                 ident(bank(3), [y(4), y(5)])
-                if OPT["join"]:
+                if "J2" in OPT["rest"]:
                     mm(bank(2), R("ID", 0, 128), y(0), lo == 0, False)
                     mm(bank(2), R("ID", 0, 128), y(1), False, False)
                 else:
                     ident(bank(2), [y(0), y(1)])
-            elif k == "J_":
-                mm(ps(0, 384), R("ID", 0, 128), R("L1", 0, 768, 2), False, True)
             elif k == "S2":
                 tt(R("L2", 0, 384), R("L1", 1, 768, 2), ps(512, 896), A.add)
-                if not OPT["join"]:
-                    tt(ps(0, 384), ps(0, 384), R("L1", 0, 768, 2), A.add)
-            elif k == "S3":
-                tt(R("L3", 0, 192), ps(1, 384, 2), R("L2", 1, 384, 2), A.add)
-                tt(ps(896, 1024) if False else R("L3", 192, 384), ps(0, 384, 2), R("L2", 0, 384, 2), A.add)
-            elif k == "S4":
-                tt(R("DD", 0, 192), R("L3", 192, 384), R("L3", 0, 192), A.subtract)
+                tt(ps(0, 384), ps(0, 384), R("L1", 0, 768, 2), A.add)
             elif k == "S5":
                 tt(R("L3", 0, 192), ps(1, 384, 2), R("L2", 1, 384, 2), A.add)
                 tt(ps(512, 704), ps(0, 384, 2), R("L2", 0, 384, 2), A.add)
                 tt(R("DD", 0, 192), ps(512, 704), R("L3", 0, 192), A.subtract)
-            elif k == "V1":
-                tt(R("L1", 0, 384), R("XG", 2, 3072, 8), R("PS", 512 * TB[0], 512 * TB[0] + 384), A.add)
-                if OPT["join"]:
-                    mm(ps(0, 384), R("ID", 0, 128), R("L1", 0, 384), False, True)
-                tt(R("L1", 384, 768), R("XG", 6, 3072, 8), R("PS", 512 * TB[1], 512 * TB[1] + 384), A.add)
-            elif k == "V2":
-                if not OPT["join"]:
-                    tt(ps(0, 384), ps(0, 384), R("L1", 0, 384), A.add)
-                tt(R("L2", 0, 384), R("L1", 384, 768), ps(512, 896), A.add)
-            elif k == "V3":
-                tt(R("L3", 0, 192), ps(1, 384, 2), R("L2", 1, 384, 2), A.add)
-                tt(ps(0, 384, 2), ps(0, 384, 2), R("L2", 0, 384, 2), A.add)
-                tt(R("DD", 0, 192), ps(0, 384, 2), R("L3", 0, 192), A.subtract)
-            elif k == "Xv":
-                ts(R("XG", lo, hi), G(wtab, rxl(lo, hi)), 0.125, A.mult)
-            elif k == "T1":
-                tt(R("L1", lo // 4, hi // 4), x(2, lo, hi), x(3, lo, hi), A.add)
-                lo = max(lo, A_END)
-                if lo < hi:
-                    tt(ps(lo // 4, hi // 4), x(0, lo, hi), x(1, lo, hi), A.add)
-            elif k[0] == "B":
-                move(k[1], R("PS", OPT["bb"] + lo // 4, OPT["bb"] + hi // 4), x(3, lo, hi))
-            elif k == "T5":
-                tt(R("L1", lo // 4, hi // 4), x(2, lo, hi), R("PS", OPT["bb"] + lo // 4, OPT["bb"] + hi // 4), A.add)
-            elif k == "T2":
-                tt(R("L2", 0, 384), R("L1", 1, 768, 2), ps(1, 768, 2), A.add)
-                tt(ps(0, 768, 2), ps(0, 768, 2), R("L1", 0, 768, 2), A.add)
-            elif k == "T3":
-                tt(R("L3", 0, 192), ps(2, 768, 4), R("L2", 1, 384, 2), A.add)
-                tt(ps(0, 768, 4), ps(0, 768, 4), R("L2", 0, 384, 2), A.add)
-                tt(ps(0, 768, 4) if OPT["slot"] else R("DD", 0, 192), ps(0, 768, 4), R("L3", 0, 192), A.subtract)
+            elif k == "U2":
+                tt(R("L2", lo // 8, hi // 8), R("L1", lo // 4 + 1, hi // 4, 2), ps(512 + lo // 8, 512 + hi // 8), A.add)
+            elif k == "U3":
+                tt(ps(lo // 8, hi // 8), ps(lo // 8, hi // 8), R("L1", lo // 4, hi // 4, 2), A.add)
+            elif k == "U4":
+                tt(R("L3", lo // 16, hi // 16), ps(lo // 8 + 1, hi // 8, 2), R("L2", lo // 8 + 1, hi // 8, 2), A.add)
+            elif k == "U5":
+                tt(ps(512 + lo // 16, 512 + hi // 16), ps(lo // 8, hi // 8, 2), R("L2", lo // 8, hi // 8, 2), A.add)
+            elif k == "U6":
+                tt(R("DD", lo // 16, hi // 16), ps(512 + lo // 16, 512 + hi // 16), R("L3", lo // 16, hi // 16), A.subtract)
+            elif k == "U7":
+                tt(ps(lo // 16, hi // 16), ps(512 + lo // 16, 512 + hi // 16), R("L3", lo // 16, hi // 16), A.subtract)
+            elif k == "U8":
+                tt(ps(lo // 16, hi // 16), ps(lo // 16, hi // 16), R("CS", lo // 16, hi // 16), A.add)
+            elif k == "U9":
+                ts(R("EA", lo + 15, hi, 16), ps(lo // 16, hi // 16), 0.125, A.max, 8.0, A.min)
+            elif k in ("Xv", "Xs"):
+                move(k[1], R("EA", 3087, 4096, 16), R("CS", 192, 256))
+            elif k == "th":
+                ts(R("TH", lo, hi), R("TE", lo, hi), 0.125, A.is_lt, 0.125, A.mult)
+            elif k == "J2":
+                mm(ps(0, 384), R("ID", 0, 128), R("L1", 0, 768, 2), False, True)
+            elif k == "J3":
+                mm(ps(0, 384, 2), R("ID", 0, 128), R("L2", 0, 384, 2), False, True)
+            elif k == "S6":
+                tt(ps(512, 704), ps(0, 384, 2), R("L3", 0, 192), A.subtract)
+            elif k == "S7":
+                tt(ps(0, 192), ps(512, 704), R("L3", 0, 192), A.subtract)
             elif k == "cs":
-                act(R("CS", 0, 256), G(cold(p, p + SO), R("IV16", 0, 16)))
-                act(R("XG", 3087, 4096, 16), R("CS", 192, 256))
-            elif k == "T4":
-                tt(ps(0, 768, 4), ps(0, 768, 4), R("CS", 0, 192), A.add)
-                ts(R("XG", 15, 3072, 16), ps(0, 768, 4), 0.125, A.max, 8.0, A.min)
+                p = (128 * t) % SO
+                act(R("CS", 0, 256), G(R("CD", p, p + SO), R("IV16", 0, 16)))
+            elif k == "ce":
+                dma("y", eown("EA"), R("CD", 0, SO), "ce")
+            elif k in ("T6", "T7"):
+                d = ps(512, 704) if k == "T6" else ps(0, 192)
+                tt(d, d, R("CS", 0, 192), A.add)
+                cp(R("EA", 3087, 4096, 16), R("CS", 192, 256))
+                ts(R("EA", 15, 3072, 16), d, 0.125, A.max, 8.0, A.min)
             elif k in ("cv", "cw"):
-                new = R("CN", 0, SO)
-                move("v" if k == "cv" else "s", new, G(R("XG", 0, ET + (q + 1) * SO), R("OE16", 0, 32)))
+                move("v" if k == "cv" else "s", cown, G(R("EA", 0, ET + (q + 1) * SO), R("OE16", 0, 32)))
                 if last:
-                    dma("y", T.yc[:], new, "so")
+                    dma("y", T.yc[:], cown, "so")
                 else:
-                    send_amounts(new)
-                    dma("y", cown, new, "ci")
-                    dma("y", cold(0, SO), new, "cd")
-                    dma("y", cold(SO, SO + 384), R("CN", 0, 384), "cd")
+                    send([cown], "ac", "lc")
+                    dma("y", R("CD", 0, SO), cown, "ci")
+                    dma("y", R("CD", SO, SO + 384), R("CT", q * SO, q * SO + 384), "ci")
+            elif k[0] == "B":
+                move(k[1], R("PS", lo // 4, hi // 4), x(3, lo, hi))
+            elif k == "T5":
+                tt(R("L1", lo // 4, hi // 4), x(2, lo, hi), R("PS", lo // 4, hi // 4), A.add)
             elif k == "ao":
                 tt(R("CB", 0, SO), G(R("DD", 0, 1216), R("SL16", 0, 32)), cown, A.add)
                 ts(cown, R("CB", 0, SO), 0.125, A.max, 8.0, A.min)
                 if last:
                     dma("y", T.yc[:], cown, "so")
                 else:
-                    send_amounts(cown)
+                    send([cown], "ac", "lc")
+            elif k == "c1":
+                tt(R("CB", lo, hi), G(R("DD", 0, 1216), R("SL16", lo // 16, hi // 16)), R("CT", q * SO + lo, q * SO + hi), A.add)
+            elif k == "c2":
+                ts(R("CT", q * SO + lo, q * SO + hi), R("CB", lo, hi), 0.125, A.max, 8.0, A.min)
+            elif k == "c3":
+                if last:
+                    dma("y", T.yc[:], cown, "so")
+                else:
+                    send([cown], "ac", "lc")
             elif k == "es":
                 act(R("EG", lo, hi), egat("EB", lo, hi))
-            elif k == "Qf":
-                tt(R("MG", lo, hi), mgat(lo, hi), R("EG", lo, hi), A.mult)
-                have["H"] |= units
             elif k == "Q_":
                 if units <= have["D"]:
                     tt(R("EG", lo, hi), R("EG", lo, hi), R("PS", lo, hi), A.mult)
@@ -779,53 +565,77 @@ def rank_program(g, core, T, topo):
                     tt(R("EG", lo, hi), egat("EB", lo, hi), R("MG", lo, hi), A.mult)
             elif k[0] == "K":
                 to_psum(k[1], "KK", lo, hi)
-            elif k in ("Ra", "Rb", "RA", "RB"):
-                act(R("TT" if k[1] in "aA" else "CB", lo, hi), G(ctab, R("A16" if k[1] in "aA" else "B16", lo // 16, hi // 16)))
-            elif k == "rg":
-                tt(R("TT", lo, hi), R("TT", lo, hi), R("PS", lo, hi), A.mult)
-            elif k == "rh":
-                tt(R("BIG", wo + 4096 + lo, wo + 4096 + hi), G(ctab, R("B16", lo // 16, hi // 16)), R("TT", lo, hi), A.mult)
-            elif k == "cl":
-                slots_clear()
             elif k == "w2":
-                h = arg[0]
-                writeback("EB", "EA", 256 * h, 256 * h + 256)
+                writeback("EB", "EA", lo, hi)
                 if last:
-                    dma("ys"[h], T.ye[:, 256 * h:256 * h + 256], eown("EA", 256 * h, 256 * h + 256), "so")
-            elif k == "g_":
-                live_count(arg[0])
+                    dma("s" if lo else "y", T.ye[:, lo:hi], eown("EA", lo, hi), "so")
+            elif k == "w3":
+                writeback("EB", "EA", 0, SO)
+            elif k in ("g_", "h_"):
+                live_count(lo, hi, k == "h_")
             elif k == "t_":
-                live_bound(arg[0])
-                if arg[0] == len(OPT["l"]) - 1 or arg[0] == 1:
-                    send_piece(t + 1, "l", arg[0] if len(OPT["l"]) == 2 else 0) if (len(OPT["l"]) == 2 or arg[0] == 1) else None
+                live_bound(lo, hi)
+                if hi == SO:
+                    send_piece(t + 1, "l", 0)
+            elif k in ("hh", "tt"):
+                p = (128 * (t + 1)) % SO or 256
+                a, b = sorted([(0, p), (p, SO)], key=lambda x: x[1] - x[0])[arg[0]]
+                bank = R("PS", 2048 + 512 * arg[0], 2048 + 512 * arg[0] + b - a)
+                if k == "hh":
+                    tt(R("FL", a, b), G(R("EB", 0, 6144), R("OE16", a // 16, b // 16)), R("TH", a, b), A.is_ge)
+                    mm(bank, R("MX", 0, 128), R("FL", a, b), True, True)
+                else:
+                    out, acc_ = R("LV", q * SO + a, q * SO + b), R("CAR", 4 * (a > 0), 4 * (a > 0) + 1)
+                    op("s", (out[0], out[1] + acc_[1]), [bank, col(8)],
+                       lambda: g.scalar.activation(out[0], bank[0], F.Sign, bias=col(8)[0], accum_out=acc_[0]))
+                    if arg[0]:
+                        send_piece(t + 1, "l", 0)
+            elif k == "pd":
+                p = (128 * t) % SO
+                scan(R("SCL", p, SO), R("TY", p, SO), R("LV", q * SO + p, (q + 1) * SO), 0.0, A.mult, A.add)
+                if p:
+                    scan(R("SCL", 0, p), R("TY", 0, p), R("LV", q * SO, q * SO + p), R("CAR", 4, 5), A.mult, A.add)
+                else:
+                    part[1] += 1
+                out, x1 = R("PS", 3072, 3104), 32 - 8 * (t % 4)
+                extract(6, "Z2", "SCL", 0, 32)
+                mm(out, R("ONE", 0, 128), R("HB", x1, x1 + 32), False, False)
+                mm(out, R("RH", 0, 128), R("ONE", 0, 32), False, True)
+            elif k == "sa":
+                out, a, acc_ = R("LA", 0, 511), R("ACT", 0, 511), R("CAR", 2, 3)
+                op("s", (out[0], out[1] + acc_[1]), [a], lambda: g.scalar.activation(out[0], a[0], F.Copy, accum_out=acc_[0]))
+            elif k == "cu":
+                scan(R("SC", 511, RO), R("ACT", 511, RO), R("CAP", 511, RO), R("CAR", 2, 3), A.add, A.min)
+                mm(at(1), R("ZM", 0, 128), R("SC", 511, RO - 1, 16), True, False)
+                for r in range(16):
+                    mm(at(1), R("ZD" if r < 15 else "ZP", 16 - r, 144 - r), R("SC", 512 + r, RO, 16), False, False)
+                mm(at(1), R("ONE", 0, 128), R("JB", x0 + 32, x0 + 64), False, True)
             else:
                 raise ValueError(s)
 
-        skip = ""
-        if t == 0:
-            skip = "oc nm N_ o2 gv gs RA RB RS rg rh se r1 r2 r3 pc ps aL Ls Lv px lk ct o0 o1 mv M0 M1 U0 U1 wv ws q_ pi pj lo lr b0 b1 b2 w3"
-        else:
-            for k in "vs":
-                need(k, "lw")
-                need(k, "lx")
-        steps = OPT["round"]
-        if last:
-            skip = "Kp Ks Kv aC Ra Rb Rs cl cd th g_ g2 t_ h_ w2"
-        for s in steps.split() + (["W20", "W21"] if last else []):
-            OPT["cur"] = (t, s)
-            if s[:2] not in skip.split():
-                s = s.replace("W2", "w2")
-                if t == 0 and s == OPT["k8"]:
-                    for more in OPT["more0"].split():
-                        step(more)
-                step(s)
+        return step
+
+    def rounds():
+        step = [a_round(t) for t in range(TR)]
+        for t in range(TR):
+            last = t == TR - 1
+            skip = "Kp Ks Kv aC Ra Rb Rs cd us uv th hh tt g_ t_ h_ w2 +" if last else ""
+            for s in (OPT["head" if t else "first"] + " " + OPT["rest"]).split() + (OPT["end"].split() if last else []):
+                OPT["cur"] = (t, s)
+                if s[0] == "x":
+                    part[:] = [None, -1]
+                    once[s]()
+                elif s[0] == "+" and not last:
+                    step[t + 1](s[1:])
+                elif s[:2] not in skip.split() and s[0] != "+":
+                    step[t](s.replace("W2", "w2"))
 
     loads = {"c": (cown, T.cin[:], "ldc"), "e": (eown("EA"), T.ein[:], "lde"), "a": (R("RAI", 0, 64), T.ra[:], "ldl"),
              "b": (R("RBI", 0, 64), T.rb[:], "ldl"), "k": (R("KK", 0, RO), T.kin[:], "ldk"), "o": (R("LI", 1024, 1536), T.ot[:], "ldo"),
              "r": (R("LI", 0, SO), T.rx[:], "ldx"), "t": (R("TAU", 16, 528), T.tau[:], "ldt")}
     loads.update({"R": (R("LI", SO, 896), T.rx[:, 0:384], "cd"), "O": (R("LI", 1536, 1920), T.ot[:, 0:384], "cd")})
-    early, late = OPT["loads"].split("|")
-    for k in early:
+    OPT["cur"] = (-1, "start")
+    for k in "ceabkort":
         dma("y", *loads[k])
     iota(R("PI", 0, 2), [[112, 2]], 0, 1, small=False)
     iota(R("I2", 0, 128), [[1, 8], [0, 16]], 0, 0)
@@ -833,86 +643,69 @@ def rank_program(g, core, T, topo):
     iota(R("I4", 0, 128), [[0, 8], [1, 16]], 1, 0)
     iota(R("I3", 0, 64), [[0, 2], [16, 32]], 192 - 2047, 0)
     iota(R("JB", 0, 128), [[0, 2], [16, 64]], 0, 0)
-    send_amounts(cown)
+    send([cown], "ac", "lc")
     send_block(0, "e")
+    iota(R("POS", 0, 2 * SO), [[0, 2], [1, SO]], 1024, 0)
     iota(R("RM", 0, 1024), [[0, 64], [1, 16]], 0, 0)
 
-    fill(R("BV", 0, 256), 4096.0)
-    out, a = R("INV", 0, 256), R("BV", 0, 256)
-    op("s", out, [a], lambda: g.scalar.activation(out[0], a[0], F.Silu))
-    ts(R("PJ", 0, 2), R("PI", 0, 2), 4, A.arith_shift_right, 7, A.bitwise_and)
-    ts(R("PJ", 2, 3), R("PI", 0, 1), 15, A.bitwise_and)
-    fill(R("TY", 0, SO), 1.0)
-    cp(R("COL", 0, 3), R("PJ", 0, 3))
-    scan(R("POS", SO, 2 * SO), R("TY", 0, SO), R("TY", 0, SO), 1023.0, A.mult, A.add)
-    ts(R("M0", 0, 128), R("I2", 0, 128), col(0), A.is_equal, 2.0, A.mult)
-    ts(R("M1", 0, 128), R("I2", 0, 128), col(1), A.is_equal)
-    ts(col(4), col(2), 0.0, A.is_equal)
-    ts(col(5), col(2), 1.0, A.is_equal, -2048.0, A.mult)
-    ts(col(7), col(2), delta / 2, A.add)
-    fill(col(8), -23.5)
-    ts(col(6), col(2), 1.0, A.not_equal)
-    tt(R("MX", 0, 128), R("M0", 0, 128), R("M1", 0, 128), A.add)
-    ts(R("TY", 0, SO), R("TY", 0, SO), col(6), A.mult)
-    ts(R("M0", 0, 144), R("I1", 0, 144), 0.0, A.is_equal, col(4), A.mult)
-    for h in range(2):
-        live_count(h)
-        live_bound(h)
-    ts(R("M1", 0, 144), R("I1", 0, 144), -1.0, A.is_equal, col(5), A.mult)
-    ts(R("RH", 0, 128), R("I4", 0, 128), 0.5, A.mult)
-    tt(R("M1", 0, 144), R("M0", 0, 144), R("M1", 0, 144), A.add)
-    ts(R("HB", 0, 64), R("I3", 0, 64), 2047.0 - 192 - 2048, A.add, 0.5, A.mult)
-    fill(R("ONE", 0, 128), 1.0 / 128)
-    ts(R("Z2", 0, 144), R("M1", 0, 144), 0.5, A.mult)
-    picks_count(0)
-    ts(R("KT", 0, 64), R("I3", 0, 64), col(2), A.add)
-    ts(R("ID", 0, 128), R("I1", 16, 144), 0.0, A.is_equal)
-    ts(col(13), col(2), 1.0, A.add)
-    move("p", R("PS", 512, 1024), R("KK", 512, 1024))
-    ts(R("JF", 0, 128), R("JB", 0, 128), col(2), A.add)
-    picks_slots(0)
-    picks_scatter(0)
-    for h in range(2):
-        cp(R("A16", 64 * h, 64 * h + 64), R("RAI", 0, 64))
-        cp(R("B16", 64 * h, 64 * h + 64), R("RBI", 0, 64))
-        cp(R("AB16", 64 * h, 64 * h + 64), R("RBI" if h else "RAI", 0, 64))
-        ts(R("PM", 128 * h, 128 * h + 128), R("I4", 0, 128), col(13), A.is_equal, 8192.0, A.mult)
-    ts(R("Z1", 0, 144), R("M0", 0, 144), delta / 2, A.mult)
-    ts(R("HB", 64, 128), R("JB", 0, 64), -2048.0, A.add, 0.5, A.mult)
-    ts(R("YE", 0, 32), R("JF", 0, 32), float(ET + SO * q), A.add)
-    ts(R("YE", 32, 64), R("JF", 0, 32), 16.0, A.add)
-    fill(R("TAU", 0, 16), 0.0)
-    for i in range(3):
-        back(i)
-    if OPT["wide"]:
-        wide_constants()
-    picks_extract()
-    picks_inv()
-    if late:
-        need("y", "lc")
-    for k in late:
-        dma("y", *loads[k])
-    for h in (1, 0):
-        picks_lists(0, h)
-    first_rates()
-    dma("y", R("RM", 1024, 2048), R("RM", 0, 1024), "cr")
-    need("y", "lw")
-    for k in "RO":
-        dma("y", *loads[k])
-    dma("y", R("POS", 0, SO), R("POS", SO, 2 * SO), "ci")
-    dma("y", R("TY", SO, 2 * SO), R("TY", 0, SO), "ci")
-    if OPT["slot"]:
-        dma("y", cold(0, SO), T.cin[:], "cd")
-        dma("y", cold(SO, SO + 384), T.cin[:, 0:384], "cd")
-        for lo in range(3072, ET + q * SO, SO):
-            dma("y", R("XG", lo, lo + SO), T.cin[:], "cd")
-    else:
-        fill(R("DD", 0, 1216), 0.0)
-    if OPT["fold"]:
-        fill(R("ON1", 0, 512), 1.0)
+    def clear_slots():
+        out, a = R("INV", 0, 256), R("BV", 0, 256)
+        op("s", out, [a], lambda: g.scalar.activation(out[0], a[0], F.Silu))
 
-    for t in range(TR):
-        a_round(t)
+    def zeros():
+        if "ao" in OPT["rest"] or "c1" in OPT["rest"]:
+            act(R("DD", 192, 1216), R("KK", 0, RO), 0.0)
+        else:
+            dma("y", R("CD", 0, SO), T.cin[:], "ci")
+            dma("y", R("CD", SO, SO + 384), T.cin[:, 0:384], "ci")
+
+    def lists_again():
+        need("y", "lw")
+        for k in "RO":
+            dma("y", *loads[k])
+
+    once = {
+        "xbv": lambda: fill(R("BV", 0, 256), 4096.0), "xiv": clear_slots,
+        "xj0": lambda: ts(R("PJ", 0, 2), R("PI", 0, 2), 4, A.arith_shift_right, 7, A.bitwise_and),
+        "xj1": lambda: ts(R("PJ", 2, 3), R("PI", 0, 1), 15, A.bitwise_and),
+        "xcc": lambda: cp(R("COL", 0, 3), R("PJ", 0, 3)),
+        "xc8": lambda: fill(col(8), -23.5), "xon": lambda: fill(R("ONE", 0, 128), 1.0 / 128), "xta": lambda: fill(R("TAU", 0, 16), 0.0),
+        "xm0": lambda: ts(R("M2", 0, 128), R("I2", 0, 128), col(0), A.is_equal, 2.0, A.mult),
+        "xm1": lambda: ts(R("M3", 0, 128), R("I2", 0, 128), col(1), A.is_equal),
+        "xmx": lambda: tt(R("MX", 0, 128), R("M2", 0, 128), R("M3", 0, 128), A.add),
+        "xc4": lambda: ts(col(4), col(2), 0.0, A.is_equal),
+        "xc5": lambda: ts(col(5), col(2), 1.0, A.is_equal, -1024.0, A.mult),
+        "xc6": lambda: ts(col(6), col(2), 1.0, A.not_equal),
+        "xty": lambda: ts(R("TY", 0, SO), R("TY", 0, SO), col(6), A.mult),
+        "xtt": lambda: fill(R("TY", 0, SO), 1.0),
+        "xn0": lambda: ts(R("M0", 0, 144), R("I1", 0, 144), 0.0, A.is_equal, col(4), A.mult),
+        "xn1": lambda: ts(R("M1", 0, 144), R("I1", 0, 144), -1.0, A.is_equal, col(5), A.mult),
+        "xn2": lambda: ts(R("M4", 0, 144), R("M0", 0, 144), 0.5, A.mult),
+        "xz2": lambda: tt(R("Z2", 0, 144), R("M4", 0, 144), R("M1", 0, 144), A.add),
+        "xrh": lambda: ts(R("RH", 0, 128), R("I4", 0, 128), 0.5, A.mult),
+        "xhb": lambda: ts(R("HB", 0, 64), R("I3", 0, 64), 2047.0 - 192 - 2048, A.add, 0.5, A.mult),
+        "xid": lambda: ts(R("ID", 0, 128), R("I1", 16, 144), 0.0, A.is_equal),
+        "xkt": lambda: ts(R("KT", 0, 64), R("I3", 0, 64), col(2), A.add),
+        "xcd": lambda: ts(col(13), col(2), 1.0, A.add),
+        "xa0": lambda: cp(R("A16", 0, 64), R("RAI", 0, 64)), "xb0": lambda: cp(R("B16", 0, 64), R("RBI", 0, 64)),
+        "xa1": lambda: cp(R("A16", 64, 128), R("RAI", 0, 64)), "xb1": lambda: cp(R("B16", 64, 128), R("RBI", 0, 64)),
+        "xa2": lambda: cp(R("AB16", 0, 64), R("RAI", 0, 64)), "xb2": lambda: cp(R("AB16", 64, 128), R("RBI", 0, 64)),
+        "xp0": lambda: ts(R("PM", 0, 128), R("I4", 0, 128), col(13), A.is_equal, 8192.0, A.mult),
+        "xp1": lambda: ts(R("PM", 128, 256), R("I4", 0, 128), col(13), A.is_equal, 8192.0, A.mult),
+        "xy0": lambda: ts(R("YE", 0, 32), R("JB", 0, 32), col(2), A.add, float(ET + SO * q), A.add),
+        "xy1": lambda: ts(R("YE", 32, 64), R("JB", 0, 32), col(2), A.add, 16.0, A.add),
+        "xz1": lambda: ts(R("Z1", 0, 144), R("M0", 0, 144), delta, A.mult),
+        "xzp": lambda: ts(R("ZP", 0, 144), R("M0", 0, 144), delta, A.mult),
+        "xzm": lambda: ts(R("ZM", 0, 128), R("M0", 16, 144), -delta, A.mult),
+        "xzc": lambda: ts(R("ZD", 0, 8), R("M0", 0, 8), delta, A.mult),
+        "xzd": lambda: tt(R("ZD", 8, 144), R("ZP", 8, 144), R("ZP", 7, 143), A.subtract),
+        "xcp": lambda: fill(R("CAP", 0, RO), 512.0),
+        "xtb": lambda: ts(R("TB", 0, 528), R("TAU", 0, 528), 0.125, A.is_lt, 0.125, A.mult),
+        "xdd": zeros, "xll": lists_again,
+        "xg0": lambda: live_count(0, 256), "xg1": lambda: live_count(256, SO),
+        "xt0": lambda: live_bound(0, 256), "xt1": lambda: live_bound(256, SO),
+    }
+    rounds()
 
     for sem in SEMAPHORES:
         if total[sem]:

from concourse.bass import DstId, RemoteDMATransfer
from concourse.mybir import AluOpType as A, ActivationFunctionType as F

N, SO, RO, TR = 4, 512, 1024, 5
W0, W1 = 0, 5120
ET = 4096
U = 256
OPT = dict(
    end="W201 W212",
    first="xtt xta xj1 xj0 xbv xcc xc4 xm1 xc6 xn0 xc5 xcd xm0 xiv xon xn1 xrh xmx xg0 xc8 xg1 xn2 xt0 xp0 xty xhb xt1 xb0 xdd xa0 xz2 xid xp1 "
          "pc xzc xz1 xcp xkt xy0 xa1 ps.0 xzm ps.1 ps.2 xzp ps.3 ps.4 xy1 xa2 ps.5 xzd ps.6 xb2 KP24 xb1 "
          "AC RA24 RB24 b0 f101 f112 f201 f212 q_02 M0 r124 b1 px f324 b2 q_24 M1 xll ts pi pj lo lr W_ "
          "aE Fs02 Ev46 Cp46 cd Fv23 Fs34 aM P_02 P_24 ms8c ms48 z_02 z_24 P_8c mscg P_46 Dp8c z_8c P_68 P_cg z_48 z_cg",
    head="RB24 w3 se pc.0 r123 pc.1 r134 pc.2 r202 r224 ps.0 ps.1 "
         "aL Ls12 Ls24 Lv01 ps.3 ps.2 lk01 ps.4 lk12 ps.5 sa lk24 ps.6 o0 cu mv02 M0 b0 o1 mv24 M1 "
         "px pi pj lo lr aE ws02 ws24 W_ Fs24 b1 Fv12 b2 ts Fv01 Ev45 Cp45 "
         "aM ms8c P_02 cd P_24 Dp8c ms48 z_02 mscg z_24 P_8c P_45 P_58 P_cg z_8c z_48 z_cg",
    rest="aW As04 As48 As8c Bs0c th01 w1 T506 T56c ms04 Dpcg U206 U306 U26c U36c aF U406 U506 U46c U56c U606 Ds24 es24 U66c th12 "
         "c101 c112 c201 Q_02 c212 c3 Q_24 Dp48 es8b esbe eseg es48 Z_02 Z_24 Q_8b Q_be Z_8b aC Kp04 Q_eg Z_be Q_48 Z_eg "
         "Ra04 Rb02 Z_48 h_01 h_12 +r102 t_01 t_12")
f32, bf, f16, i32, u16 = "float32", "bfloat16", "float16", "int32", "uint16"
SCRATCH = {
    "BIG": ("sbuf", [128, 10240], f32), "EA": ("sbuf", [128, 6144], f32), "EB": ("sbuf", [128, 6144], f32),
    "WM": ("sbuf", [128, 4096], f32), "MG": ("sbuf", [128, 4096], f32),
    "CT": ("sbuf", [128, 2048], f32), "LV": ("sbuf", [128, 2048], bf),
    "XG": ("sbuf", [128, 4608], f32), "EG": ("sbuf", [128, 4096], f32), "RM": ("sbuf", [128, 2048], bf),
    "KK": ("sbuf", [128, 1024], f32), "TC": ("sbuf", [128, 2048], f32), "AB16": ("sbuf", [128, 128], u16), "BV": ("sbuf", [128, 256], f32),
    "TAU": ("sbuf", [128, 528], f32), "TE": ("sbuf", [128, 512], f32),
    "TB": ("sbuf", [128, 528], f32), "TH": ("sbuf", [128, 512], f32),
    "CD": ("sbuf", [128, 896], f32), "CS": ("sbuf", [128, 256], f32),
    "RAI": ("sbuf", [128, 64], i32), "RBI": ("sbuf", [128, 64], i32),
    "A16": ("sbuf", [128, 128], u16), "B16": ("sbuf", [128, 128], u16),
    "LI": ("sbuf", [128, 1920], i32),
    "L16": ("sbuf", [128, 512], u16), "POS": ("sbuf", [128, 1024], f32), "INV": ("sbuf", [128, 1216], f32),
    "IH": ("sbuf", [128, 256], f32), "IV16": ("sbuf", [128, 16], u16), "PM": ("sbuf", [128, 256], f32),
    "LA": ("sbuf", [128, 1024], bf), "ACT": ("sbuf", [128, 1024], bf), "SC": ("sbuf", [128, 1024], f16), "CAP": ("sbuf", [128, 1024], bf),
    "TY": ("sbuf", [128, 512], bf), "SCL": ("sbuf", [128, 512], f16), "CAR": ("sbuf", [128, 8], f32),
    "FL": ("sbuf", [128, 512], bf), "MX": ("sbuf", [128, 128], bf),
    "Z1": ("sbuf", [128, 144], bf), "Z2": ("sbuf", [128, 144], f16), "ZD": ("sbuf", [128, 144], f16),
    "ZP": ("sbuf", [128, 144], f16), "ZM": ("sbuf", [128, 128], f16),
    "ID": ("sbuf", [128, 128], f32), "RH": ("sbuf", [128, 128], bf), "HB": ("sbuf", [128, 64], bf),
    "ONE": ("sbuf", [128, 128], bf), "JB": ("sbuf", [128, 128], bf), "JF": ("sbuf", [128, 32], f32),
    "PI": ("sbuf", [128, 8], i32), "PJ": ("sbuf", [128, 8], i32), "COL": ("sbuf", [128, 16], f32),
    "KT": ("sbuf", [128, 64], f32), "YE": ("sbuf", [128, 64], f32), "SM": ("sbuf", [128, 320], f32),
    "SL16": ("sbuf", [128, 32], u16), "OE16": ("sbuf", [128, 64], u16), "SEL": ("sbuf", [128, 64], u16),
    "PS": ("psum", [128, 4096], f32),
}
INSIDE = {"TT": ("TC", 0), "CB": ("TC", 1024), "L1": ("EB", 0), "L2": ("EB", 768), "L3": ("EB", 1152), "DD": ("XG", 3072),
          "M0": ("MG", 0), "M1": ("MG", 144), "I1": ("MG", 288), "I2": ("MG", 432), "I3": ("MG", 560), "I4": ("MG", 624),
          "M2": ("MG", 752), "M3": ("MG", 880), "M4": ("MG", 1008)}
SEMAPHORES = ["sv", "ss", "sp", "sg", "ldc", "lde", "ldl", "ldk", "ldx", "ldo", "ldt", "so", "cd", "ci", "ce", "cc",
              "ac", "lc", "le", "lf", "ll", "lw", "lx"] + ["a%s%d" % (w, i) for w in "emwfl" for i in range(3)]


def dst_id(topo, c):
    rid, pid, _ = topo.addr(c)
    return DstId(rid=rid, pnc=pid)


def common_engines(topo, src, dsts):
    e = [x for x in topo.engines(src, dsts[0]) if all(x in topo.engines(src, d) for d in dsts)]
    n = 1
    while 2 * n <= len(e):
        n *= 2
    return e[:n]


def as_mask(engines):
    return sum(1 << e for e in engines)


def cyclic(p, a, b, width):
    lo, n = (p + a) % width, b - a
    return [(lo, lo + n)] if lo + n <= width else [(lo, width), (0, lo + n - width)]


def pieces(q, t, what):
    name, base, width, p, lsem = {"e": ("EA", ET + q * SO, SO, 0, "le"), "m": ("WM", q * RO, RO, 256 * t, "lw"),
                                  "f": ("EB", ET + q * SO, SO, 0, "lf"), "l": ("LV", q * SO, SO, 0, "ll"),
                                  "w": ("BIG", (W1 if t % 2 else W0) + q * RO, RO, 0, "lx")}[what]
    k = 2 if what == "m" else 1
    n = width // k
    return [(name, [(base + lo, base + hi) for lo, hi in cyclic(p, i * n, i * n + n, width)], "a%s%d" % (what, i), lsem) for i in range(k)]


def rank_program(g, core, T, topo):
    q = T.rank_of(core)
    if q is None:
        return
    others = [T.cores[(q + d) % N] for d in range(1, N)]
    eng = common_engines(topo, core, others)
    NE = len(eng)
    Q = {"v": g.vector, "s": g.scalar, "p": g.tensor, "g": g, "y": g.sync}
    CS = {"v": "sv", "s": "ss", "p": "sp", "g": "sg"}
    total = {n: 0 for n in SEMAPHORES}
    known = {k: {} for k in Q}
    clock = {}
    acc = {n: [] for n in SCRATCH}

    def R(name, lo, hi, step=1):
        if name in INSIDE:
            name, at = INSIDE[name]
            lo, hi = lo + at, hi + at
        ap = T[name][:, lo:hi] if step == 1 else T[name][:, lo:hi:step]
        return (ap, [(name, lo, hi)])

    def G(win, off):
        return (win[0].indirect(off[0]), win[1], off[1])

    def wait(k, sem, n):
        if known[k].get(sem, 0) >= n:
            return
        if sem not in CS.values():
            n = total[sem]
        Q[k].wait_ge(T.sem[sem], n)
        known[k][sem] = n
        for s, m in clock.get((sem, n), {}).items():
            if known[k].get(s, 0) < m:
                known[k][s] = m

    def need(k, sem):
        wait(k, sem, total[sem])

    def order(k, reads, writes, chain=False):
        dep = {}
        for regs, wr in ((reads, False), (writes, True)):
            for name, lo, hi in regs:
                for (a, b, w2, k2, sem, n) in acc[name]:
                    x, y, hit = lo, hi, wr or w2
                    if name == "PS" and k2 != k:
                        x, y, hit = lo // 512 * 512, -(-hi // 512) * 512, True
                    if chain and k2 == k and name == "PS":
                        hit = False
                    if hit and a < y and x < b:
                        dep[sem] = max(dep.get(sem, 0), n)
        for sem in sorted(dep, key=lambda s: s not in CS.values()):
            wait(k, sem, dep[sem])

    def note(k, reads, writes, sem, n):
        for name, lo, hi in writes:
            acc[name][:] = [e for e in acc[name] if not (lo <= e[0] and e[1] <= hi and (name != "PS" or e[3] == k))]
            acc[name].append((lo, hi, True, k, sem, n))
        for name, lo, hi in reads:
            acc[name][:] = [e for e in acc[name] if not (e[3] == k and e[4] == sem and not e[2] and lo <= e[0] and e[1] <= hi)]
            acc[name].append((lo, hi, False, k, sem, n))

    part = [None, -1]

    def skipped(k):
        if part[0] is None:
            return False
        part[1] += k == "v"
        return part[1] != part[0]

    def op(k, out, ins, call, chain=False):
        if skipped(k):
            return
        reads = [r for x in ins for r in x[1]] + [r for x in ins + [out] if len(x) > 2 for r in x[2]]
        order(k, reads, out[1], chain)
        sem = CS[k]
        total[sem] += 1
        call().then_inc(T.sem[sem], 1)
        clock[(sem, total[sem])] = dict(known[k])
        note(k, reads, out[1], sem, total[sem])

    def isap(x):
        return isinstance(x, tuple)

    def tt(out, a, b, o):
        op("v", out, [a, b], lambda: g.vector.tensor_tensor(out[0], a[0], b[0], o))

    def ts(out, a, s1, o1, s2=None, o2=None):
        ins = [a] + [s for s in (s1, s2) if isap(s)]
        x1, x2 = (s1[0] if isap(s1) else s1), (s2[0] if isap(s2) else s2)
        if o2 is None:
            op("v", out, ins, lambda: g.vector.tensor_scalar(out[0], a[0], x1, None, o1))
        else:
            op("v", out, ins, lambda: g.vector.tensor_scalar(out[0], a[0], x1, x2, o1, o2))

    def cp(out, a):
        op("v", out, [a], lambda: g.vector.tensor_copy(out[0], a[0]))

    def fill(out, c):
        op("v", out, [], lambda: g.vector.memset(out[0], c))

    def scan(out, d0, d1, init, o0, o1):
        ins = [d0, d1] + ([init] if isap(init) else [])
        op("v", out, ins, lambda: g.vector.tensor_tensor_scan(out[0], d0[0], d1[0], init[0] if isap(init) else init, o0, o1))

    def act(out, a, scale=1.0):
        op("s", out, [a], lambda: g.scalar.activation(out[0], a[0], F.Copy, scale=scale))

    def mm(out, l, r, start, stop):
        op("p", out, [l, r], lambda: g.tensor.matmul(out[0], l[0], r[0], start, stop), chain=not start)

    def ident(out, srcs):
        for i, s in enumerate(srcs):
            mm(out, R("ID", 0, 128), s, i == 0, i == len(srcs) - 1)

    def move(k, out, a):
        if k == "p":
            ident(out, [a])
        else:
            (cp if k == "v" else act)(out, a)

    def iota(out, pattern, base, cm, small=True):
        if small:
            op("g", out, [], lambda: g.iota(out[0], pattern, base, cm, allow_small_or_imprecise_dtypes=True))
        else:
            op("g", out, [], lambda: g.iota(out[0], pattern, base, cm))

    def dma(k, out, a, sem):
        if skipped(k):
            return
        writes, reads = (out[1] if isap(out) else []), (a[1] if isap(a) else [])
        order(k, reads, writes)
        total[sem] += 16
        Q[k].dma_start(out[0] if isap(out) else out, a[0] if isap(a) else a).then_inc(T.sem[sem], 16)
        note(k, reads, writes, sem, total[sem])

    def send(parts, rsem, lsem):
        if skipped("g"):
            return
        reads = [r for p in parts for r in p[1]]
        order("g", reads, [])
        n = len(parts)
        g.remote_dma_fused([RemoteDMATransfer(dst_ids=[dst_id(topo, c) for c in others], dma_engine_mask=as_mask(eng[i::n]),
                                              remote_sem=T.sem[rsem], src=p[0], dsts=[p[0]] * len(others))
                            for i, p in enumerate(parts)], local_sem=T.sem[lsem])
        total[lsem] += NE
        note("g", reads, [], lsem, total[lsem])

    def send_piece(t, what, i):
        name, cols, rsem, lsem = pieces(q, t, what)[i]
        send([R(name, lo, hi) for lo, hi in cols], rsem, lsem)

    def send_block(t, what):
        for i in range(len(pieces(q, t, what))):
            send_piece(t, what, i)

    def arrive_amounts():
        total["ac"] += (N - 1) * NE
        note("x", [], [("CT", r * SO, (r + 1) * SO) for r in range(N) if r != q], "ac", total["ac"])

    def arrive_block(t, what):
        for i, mine in enumerate(pieces(q, t, what)):
            total[mine[2]] += (N - 1) * NE
            note("x", [], [(mine[0], lo, hi) for r in range(N) if r != q for lo, hi in pieces(r, t, what)[i][1]], mine[2], total[mine[2]])

    def extract(bank, z, src, lo, n):
        for r in range(16):
            mm(R("PS", 512 * bank, 512 * bank + n), R(z, 16 - r, 144 - r), R(src, lo + r, lo + 16 * n, 16), r == 0, False)

    cown = R("CT", q * SO, (q + 1) * SO)
    ctab = R("CT", 0, 2048)
    lvtab = R("LV", 0, 2048)
    mtab = R("WM", 0, 4096)
    delta = float(4096 - RO * q)
    sm = lambda i: R("SM", 32 * i, 32 * i + 32)
    col = lambda i: R("COL", i, i + 1)
    eown = lambda b, lo=0, hi=SO: R(b, ET + q * SO + lo, ET + q * SO + hi)
    etab = lambda b: R(b, ET, ET + 2048)
    rxl = lambda lo, hi: R("L16", lo // 16, hi // 16)
    egat = lambda b, lo, hi: G(etab(b), R("L16", 256 + lo // 16, 256 + hi // 16))
    mgat = lambda lo, hi: G(mtab, rxl(lo, hi))

    def live_count(lo, hi, ahead=False):
        if ahead:
            tt(R("FL", lo, hi), G(R("EB", 0, 6144), R("OE16", lo // 16, hi // 16)), R("TH", lo, hi), A.is_ge)
        else:
            ts(R("FL", lo, hi), eown("EA", lo, hi), 0.125, A.is_ge)
        mm(R("PS", 2048 + 2 * lo, 2048 + lo + hi), R("MX", 0, 128), R("FL", lo, hi), True, True)

    def live_bound(lo, hi):
        out, a = R("LV", q * SO + lo, q * SO + hi), R("PS", 2048 + 2 * lo, 2048 + lo + hi)
        op("s", out, [a, col(8)], lambda: g.scalar.activation(out[0], a[0], F.Sign, bias=col(8)[0]))

    def picks_count(t):
        p = (128 * t) % SO
        scan(R("SCL", p, SO), R("TY", p, SO), R("LV", q * SO + p, (q + 1) * SO), 0.0, A.mult, A.add)
        if p:
            cp(R("CAR", 0, 1), R("SCL", SO - 1, SO))
            scan(R("SCL", 0, p), R("TY", 0, p), R("LV", q * SO, q * SO + p), R("CAR", 0, 1), A.mult, A.add)
        else:
            part[1] += 2
        out, at = R("PS", 3072, 3104), 32 - 8 * (t % 4)
        extract(6, "Z2", "SCL", 0, 32)
        mm(out, R("ONE", 0, 128), R("HB", at, at + 32), False, False)
        mm(out, R("RH", 0, 128), R("ONE", 0, 32), False, True)

    def picks_slots(t):
        y = R("PS", 3072, 3104)
        x0 = 32 - 8 * (t % 4)
        tt(sm(1), R("KT", x0, x0 + 32), y, A.subtract)
        ts(sm(0), y, 192.0 - 2047.0, A.is_ge, 192.0, A.mult)
        ts(sm(3), sm(1), 256.0 - 2047.0, A.is_ge, 512.0, A.mult)
        tt(sm(2), sm(0), y, A.add)
        tt(sm(4), sm(3), sm(1), A.add)
        tt(sm(5), sm(2), sm(4), A.min)
        ts(R("SL16", 0, 32), sm(5), 2047.0, A.add)

    def picks_scatter(t):
        p = (128 * t) % SO
        out, a = G(R("INV", 0, 1216), R("SL16", 0, 32)), R("POS", SO - p, 2 * SO - p)
        op("s", out, [a], lambda: g.scalar.activation(out[0], a[0], F.Silu))

    def picks_extract():
        scan(R("IH", 0, 256), R("PM", 0, 256), R("INV", 0, 256), 0.0, A.max, A.min)

    def picks_inv():
        ts(R("IV16", 0, 16), R("IH", 15, 256, 16), -1024.0, A.add, 511.0, A.min)

    def picks_lists(t, h):
        p = (128 * t) % SO
        cp(R("L16", 256 * h, 256 * h + 256), G(R("LI", 1024 * h + p, 1024 * h + p + 512), R("IV16", 0, 16)))

    def back(i):
        if i == 0:
            ts(sm(6), sm(5), 16.0, A.mult, 2047.0 * 16 + 15, A.add)
            ts(sm(7), sm(5), 256.0 - 2047.0, A.is_lt, 1024.0, A.mult)
        elif i == 1:
            tt(R("SM", 256, 320), R("SM", 192, 256), R("YE", 0, 64), A.min)
        else:
            cp(R("OE16", 0, 64), R("SM", 256, 320))

    def writeback(src, dst, lo, hi):
        tt(eown(dst, lo, hi), G(R(src, 0, 6144), R("OE16", lo // 16, hi // 16)), R("TE", lo, hi), A.max)

    def to_psum(k, name, lo, hi):
        if k == "p":
            for x in range(lo // 512 * 512, hi, 512):
                move(k, R("PS", max(x, lo), min(x + 512, hi)), R(name, max(x, lo), min(x + 512, hi)))
        else:
            move(k, R("PS", lo, hi), R(name, lo, hi))

    def a_round(t):
        wn, wo = (W0, W1) if t % 2 == 0 else (W1, W0)
        last = t == TR - 1
        x0 = 16 * (t % 4)
        win = R("BIG", wo + q * RO, wo + 5120)
        wtab = R("BIG", wn, wn + 4096)
        wown = lambda lo, hi: R("BIG", wn + q * RO + lo, wn + q * RO + hi)
        at = lambda i: R("PS", 2048 + 512 * i, 2080 + 512 * i)
        ps = lambda lo, hi, step=1: R("PS", 1024 + lo, 1024 + hi, step)
        x = lambda e, lo, hi: R("XG", lo + e, hi, 4)
        have = {k: set() for k in "FCDG"}

        def places(a, b):
            for lo, hi in cyclic(256 * t, a, b, RO):
                yield lo, hi, G(win, R("SEL", a // 16, (a + hi - lo) // 16))
                a += hi - lo

        def step(s):
            s, _, only = s.partition(".")
            part[:] = [int(only) if only else None, -1]
            k, arg = s[:2], [int(c, 17) for c in s[2:]]
            lo, hi = ([U * a for a in arg] + [0, 0])[:2]
            units = set(range(lo // U, hi // U))
            if k == "se":
                send_block(t, "e")
            elif k == "AC":
                arrive_amounts()
            elif k == "KP":
                to_psum("p", "KK", lo, hi)
            elif k[0] == "a" and k != "ao":
                if k == "aC":
                    arrive_amounts()
                else:
                    arrive_block(t, k[1].lower())
                if k == "aW" and last:
                    need("y", "aw0")
                    dma("y", T.yw[:], wown(0, RO), "so")
            elif k == "r1":
                for a, b in cyclic(256 * t, lo, hi, RO):
                    tt(R("PS", a, b), R("TT", a, b), R("PS", a, b), A.mult)
            elif k == "r2":
                for a, b in cyclic(256 * t, lo, hi, RO):
                    tt(R("BIG", wo + 4096 + a, wo + 4096 + b), R("CB", a, b), R("PS", a, b), A.mult)
            elif k == "pc":
                picks_count(t)
            elif k == "ps":
                picks_slots(t)
            elif k == "px":
                picks_scatter(t)
            elif k == "pi":
                picks_extract()
            elif k == "pj":
                picks_inv()
            elif k in ("lr", "lo"):
                picks_lists(t, k == "lo")
            elif k[0] == "b":
                back(int(k[1]))
            elif k in ("tv", "ts"):
                move(k[1], R("TE", 0, SO), G(R("TAU", 0, 528), R("OE16", 32, 64)))
            elif k in ("uv", "us"):
                move(k[1], R("TH", 0, SO), G(R("TB", 0, 528), R("OE16", 32, 64)))
            elif k[0] == "L":
                out, src = R("LA", lo, hi), G(lvtab, R("A16", x0 + lo // 16, x0 + hi // 16))
                if k == "Ls":
                    act(out, src, -1.0)
                else:
                    ts(out, src, -1.0, A.mult)
            elif k == "lk":
                tt(R("ACT", lo, hi), G(lvtab, R("B16", x0 + lo // 16, x0 + hi // 16)), R("LA", lo, hi), A.is_ge)
                if hi == 512:
                    extract(4, "Z1", "ACT", 0, 32)
                    mm(at(0), R("ONE", 0, 128), R("JB", x0, x0 + 32), False, True)
            elif k == "ct":
                scan(R("SC", 0, RO), R("ACT", 0, RO), R("CAP", 0, RO), 0.0, A.add, A.min)
                mm(at(1), R("ZM", 0, 128), R("SC", 511, RO - 1, 16), True, False)
                for r in range(16):
                    mm(at(1), R("ZD" if r < 15 else "ZP", 16 - r, 144 - r), R("SC", 512 + r, RO, 16), False, False)
                mm(at(1), R("ONE", 0, 128), R("JB", x0 + 32, x0 + 64), False, True)
            elif k[0] == "o":
                h = int(k[1])
                ts(R("SEL", 32 * h, 32 * h + 32), at(h), col(2), A.add)
            elif k == "mv":
                for a, b, src in places(lo, hi):
                    ts(R("WM", q * RO + a, q * RO + b), src, 1.0, A.min)
            elif k in ("wv", "ws"):
                for a, b, src in places(lo, hi):
                    move(k[1], wown(a, b), src)
            elif k == "q_":
                for a, b, _ in places(lo, hi):
                    ts(R("WM", q * RO + a, q * RO + b), wown(a, b), 1.0, A.min)
            elif k[0] == "M":
                send_piece(t, "m", int(k[1]))
            elif k == "W_":
                send_block(t, "w")
            elif k[0] in "EG":
                move(k[1], R("EG", lo, hi), egat("EA", lo, hi))
                if k[0] == "G":
                    have["G"] |= units
            elif k[0] == "F":
                move(k[1], R("EA", lo, hi), egat("EA", lo, hi))
                have["F"] |= units
            elif k[0] in "CD":
                to_psum(k[1], "EG" if k[0] == "C" else "MG", lo, hi)
                have[k[0]] |= units
            elif k in ("ms", "mg"):
                move("s" if k == "ms" else "v", R("MG", lo, hi), mgat(lo, hi))
            elif k == "P_":
                if units <= have["C"]:
                    tt(R("EG", lo, hi), R("MG", lo, hi), R("PS", lo, hi), A.mult)
                elif units <= have["G"] & have["D"]:
                    tt(R("EG", lo, hi), R("EG", lo, hi), R("PS", lo, hi), A.mult)
                elif units <= have["F"]:
                    tt(R("EG", lo, hi), mgat(lo, hi), R("EA", lo, hi), A.mult)
                else:
                    tt(R("EG", lo, hi), egat("EA", lo, hi), R("MG", lo, hi), A.mult)
            elif k in ("z_", "Z_"):
                scan(R("EA" if k == "z_" else "EB", lo, hi), R("RM", 0, hi - lo), R("EG", lo, hi), 0.0, A.min, A.max)
            elif k == "cd":
                need("y", "lw")
                dma("y", R("INV", 0, 256), R("BV", 0, 256), "cc")
            elif k == "Rs":
                act(R("TC", 0, 2048), G(ctab, R("AB16", 0, 128)))
            elif k in ("Ra", "Rb", "RA", "RB"):
                for a, b in cyclic(256 * (t + k[1].islower()), lo, hi, RO):
                    act(R("TT" if k[1] in "aA" else "CB", a, b), G(ctab, R("A16" if k[1] in "aA" else "B16", a // 16, b // 16)))
            elif k == "r3":
                for a, b in cyclic(256 * t, lo, hi, RO):
                    tt(R("TT", a, b), G(ctab, R("A16", a // 16, b // 16)), R("KK", a, b), A.mult)
            elif k == "r4":
                for a, b in cyclic(256 * t, lo, hi, RO):
                    tt(R("BIG", wo + 4096 + a, wo + 4096 + b), G(ctab, R("B16", a // 16, b // 16)), R("TT", a, b), A.mult)
            elif k == "f1":
                tt(R("TT", lo, hi), G(ctab, R("A16", lo // 16, hi // 16)), R("KK", lo, hi), A.mult)
            elif k == "f2":
                tt(wown(lo, hi), G(ctab, R("B16", lo // 16, hi // 16)), R("TT", lo, hi), A.mult)
            elif k == "f3":
                tt(wown(lo, hi), R("CB", lo, hi), R("PS", lo, hi), A.mult)
            elif k == "w1":
                writeback("EA", "EB", 0, SO)
                send_block(t, "f")
            elif k == "As":
                act(R("XG", lo, hi), G(wtab, rxl(lo, hi)), 0.125)
                y = lambda e: R("XG", lo + e, hi, 8)
                bank = lambda b: R("PS", 512 * b + lo // 8, 512 * b + hi // 8)
                ident(bank(3), [y(4), y(5)])
                if "J2" in OPT["rest"]:
                    mm(bank(2), R("ID", 0, 128), y(0), lo == 0, False)
                    mm(bank(2), R("ID", 0, 128), y(1), False, False)
                else:
                    ident(bank(2), [y(0), y(1)])
            elif k == "S2":
                tt(R("L2", 0, 384), R("L1", 1, 768, 2), ps(512, 896), A.add)
                tt(ps(0, 384), ps(0, 384), R("L1", 0, 768, 2), A.add)
            elif k == "S5":
                tt(R("L3", 0, 192), ps(1, 384, 2), R("L2", 1, 384, 2), A.add)
                tt(ps(512, 704), ps(0, 384, 2), R("L2", 0, 384, 2), A.add)
                tt(R("DD", 0, 192), ps(512, 704), R("L3", 0, 192), A.subtract)
            elif k == "U2":
                tt(R("L2", lo // 8, hi // 8), R("L1", lo // 4 + 1, hi // 4, 2), ps(512 + lo // 8, 512 + hi // 8), A.add)
            elif k == "U3":
                tt(ps(lo // 8, hi // 8), ps(lo // 8, hi // 8), R("L1", lo // 4, hi // 4, 2), A.add)
            elif k == "U4":
                tt(R("L3", lo // 16, hi // 16), ps(lo // 8 + 1, hi // 8, 2), R("L2", lo // 8 + 1, hi // 8, 2), A.add)
            elif k == "U5":
                tt(ps(512 + lo // 16, 512 + hi // 16), ps(lo // 8, hi // 8, 2), R("L2", lo // 8, hi // 8, 2), A.add)
            elif k == "U6":
                tt(R("DD", lo // 16, hi // 16), ps(512 + lo // 16, 512 + hi // 16), R("L3", lo // 16, hi // 16), A.subtract)
            elif k == "U7":
                tt(ps(lo // 16, hi // 16), ps(512 + lo // 16, 512 + hi // 16), R("L3", lo // 16, hi // 16), A.subtract)
            elif k == "U8":
                tt(ps(lo // 16, hi // 16), ps(lo // 16, hi // 16), R("CS", lo // 16, hi // 16), A.add)
            elif k == "U9":
                ts(R("EA", lo + 15, hi, 16), ps(lo // 16, hi // 16), 0.125, A.max, 8.0, A.min)
            elif k in ("Xv", "Xs"):
                move(k[1], R("EA", 3087, 4096, 16), R("CS", 192, 256))
            elif k == "th":
                ts(R("TH", lo, hi), R("TE", lo, hi), 0.125, A.is_lt, 0.125, A.mult)
            elif k == "J2":
                mm(ps(0, 384), R("ID", 0, 128), R("L1", 0, 768, 2), False, True)
            elif k == "J3":
                mm(ps(0, 384, 2), R("ID", 0, 128), R("L2", 0, 384, 2), False, True)
            elif k == "S6":
                tt(ps(512, 704), ps(0, 384, 2), R("L3", 0, 192), A.subtract)
            elif k == "S7":
                tt(ps(0, 192), ps(512, 704), R("L3", 0, 192), A.subtract)
            elif k == "cs":
                p = (128 * t) % SO
                act(R("CS", 0, 256), G(R("CD", p, p + SO), R("IV16", 0, 16)))
            elif k == "ce":
                dma("y", eown("EA"), R("CD", 0, SO), "ce")
            elif k in ("T6", "T7"):
                d = ps(512, 704) if k == "T6" else ps(0, 192)
                tt(d, d, R("CS", 0, 192), A.add)
                cp(R("EA", 3087, 4096, 16), R("CS", 192, 256))
                ts(R("EA", 15, 3072, 16), d, 0.125, A.max, 8.0, A.min)
            elif k in ("cv", "cw"):
                move("v" if k == "cv" else "s", cown, G(R("EA", 0, ET + (q + 1) * SO), R("OE16", 0, 32)))
                if last:
                    dma("y", T.yc[:], cown, "so")
                else:
                    send([cown], "ac", "lc")
                    dma("y", R("CD", 0, SO), cown, "ci")
                    dma("y", R("CD", SO, SO + 384), R("CT", q * SO, q * SO + 384), "ci")
            elif k[0] == "B":
                move(k[1], R("PS", lo // 4, hi // 4), x(3, lo, hi))
            elif k == "T5":
                tt(R("L1", lo // 4, hi // 4), x(2, lo, hi), R("PS", lo // 4, hi // 4), A.add)
            elif k == "ao":
                tt(R("CB", 0, SO), G(R("DD", 0, 1216), R("SL16", 0, 32)), cown, A.add)
                ts(cown, R("CB", 0, SO), 0.125, A.max, 8.0, A.min)
                if last:
                    dma("y", T.yc[:], cown, "so")
                else:
                    send([cown], "ac", "lc")
            elif k == "c1":
                tt(R("CB", lo, hi), G(R("DD", 0, 1216), R("SL16", lo // 16, hi // 16)), R("CT", q * SO + lo, q * SO + hi), A.add)
            elif k == "c2":
                ts(R("CT", q * SO + lo, q * SO + hi), R("CB", lo, hi), 0.125, A.max, 8.0, A.min)
            elif k == "c3":
                if last:
                    dma("y", T.yc[:], cown, "so")
                else:
                    send([cown], "ac", "lc")
            elif k == "es":
                act(R("EG", lo, hi), egat("EB", lo, hi))
            elif k == "Q_":
                if units <= have["D"]:
                    tt(R("EG", lo, hi), R("EG", lo, hi), R("PS", lo, hi), A.mult)
                else:
                    tt(R("EG", lo, hi), egat("EB", lo, hi), R("MG", lo, hi), A.mult)
            elif k[0] == "K":
                to_psum(k[1], "KK", lo, hi)
            elif k == "w2":
                writeback("EB", "EA", lo, hi)
                if last:
                    dma("s" if lo else "y", T.ye[:, lo:hi], eown("EA", lo, hi), "so")
            elif k == "w3":
                writeback("EB", "EA", 0, SO)
            elif k in ("g_", "h_"):
                live_count(lo, hi, k == "h_")
            elif k == "t_":
                live_bound(lo, hi)
                if hi == SO:
                    send_piece(t + 1, "l", 0)
            elif k in ("hh", "tt"):
                p = (128 * (t + 1)) % SO or 256
                a, b = sorted([(0, p), (p, SO)], key=lambda x: x[1] - x[0])[arg[0]]
                bank = R("PS", 2048 + 512 * arg[0], 2048 + 512 * arg[0] + b - a)
                if k == "hh":
                    tt(R("FL", a, b), G(R("EB", 0, 6144), R("OE16", a // 16, b // 16)), R("TH", a, b), A.is_ge)
                    mm(bank, R("MX", 0, 128), R("FL", a, b), True, True)
                else:
                    out, acc_ = R("LV", q * SO + a, q * SO + b), R("CAR", 4 * (a > 0), 4 * (a > 0) + 1)
                    op("s", (out[0], out[1] + acc_[1]), [bank, col(8)],
                       lambda: g.scalar.activation(out[0], bank[0], F.Sign, bias=col(8)[0], accum_out=acc_[0]))
                    if arg[0]:
                        send_piece(t + 1, "l", 0)
            elif k == "pd":
                p = (128 * t) % SO
                scan(R("SCL", p, SO), R("TY", p, SO), R("LV", q * SO + p, (q + 1) * SO), 0.0, A.mult, A.add)
                if p:
                    scan(R("SCL", 0, p), R("TY", 0, p), R("LV", q * SO, q * SO + p), R("CAR", 4, 5), A.mult, A.add)
                else:
                    part[1] += 1
                out, x1 = R("PS", 3072, 3104), 32 - 8 * (t % 4)
                extract(6, "Z2", "SCL", 0, 32)
                mm(out, R("ONE", 0, 128), R("HB", x1, x1 + 32), False, False)
                mm(out, R("RH", 0, 128), R("ONE", 0, 32), False, True)
            elif k == "sa":
                out, a, acc_ = R("LA", 0, 511), R("ACT", 0, 511), R("CAR", 2, 3)
                op("s", (out[0], out[1] + acc_[1]), [a], lambda: g.scalar.activation(out[0], a[0], F.Copy, accum_out=acc_[0]))
            elif k == "cu":
                scan(R("SC", 511, RO), R("ACT", 511, RO), R("CAP", 511, RO), R("CAR", 2, 3), A.add, A.min)
                mm(at(1), R("ZM", 0, 128), R("SC", 511, RO - 1, 16), True, False)
                for r in range(16):
                    mm(at(1), R("ZD" if r < 15 else "ZP", 16 - r, 144 - r), R("SC", 512 + r, RO, 16), False, False)
                mm(at(1), R("ONE", 0, 128), R("JB", x0 + 32, x0 + 64), False, True)
            else:
                raise ValueError(s)

        return step

    def rounds():
        step = [a_round(t) for t in range(TR)]
        for t in range(TR):
            last = t == TR - 1
            skip = "Kp Ks Kv aC Ra Rb Rs cd us uv th hh tt g_ t_ h_ w2 +" if last else ""
            for s in (OPT["head" if t else "first"] + " " + OPT["rest"]).split() + (OPT["end"].split() if last else []):
                OPT["cur"] = (t, s)
                if s[0] == "x":
                    part[:] = [None, -1]
                    once[s]()
                elif s[0] == "+" and not last:
                    step[t + 1](s[1:])
                elif s[:2] not in skip.split() and s[0] != "+":
                    step[t](s.replace("W2", "w2"))

    loads = {"c": (cown, T.cin[:], "ldc"), "e": (eown("EA"), T.ein[:], "lde"), "a": (R("RAI", 0, 64), T.ra[:], "ldl"),
             "b": (R("RBI", 0, 64), T.rb[:], "ldl"), "k": (R("KK", 0, RO), T.kin[:], "ldk"), "o": (R("LI", 1024, 1536), T.ot[:], "ldo"),
             "r": (R("LI", 0, SO), T.rx[:], "ldx"), "t": (R("TAU", 16, 528), T.tau[:], "ldt")}
    loads.update({"R": (R("LI", SO, 896), T.rx[:, 0:384], "cd"), "O": (R("LI", 1536, 1920), T.ot[:, 0:384], "cd")})
    OPT["cur"] = (-1, "start")
    for k in "ceabkort":
        dma("y", *loads[k])
    iota(R("PI", 0, 2), [[112, 2]], 0, 1, small=False)
    iota(R("I2", 0, 128), [[1, 8], [0, 16]], 0, 0)
    iota(R("I1", 0, 144), [[1, 144]], -16, -1)
    iota(R("I4", 0, 128), [[0, 8], [1, 16]], 1, 0)
    iota(R("I3", 0, 64), [[0, 2], [16, 32]], 192 - 2047, 0)
    iota(R("JB", 0, 128), [[0, 2], [16, 64]], 0, 0)
    send([cown], "ac", "lc")
    send_block(0, "e")
    iota(R("POS", 0, 2 * SO), [[0, 2], [1, SO]], 1024, 0)
    iota(R("RM", 0, 1024), [[0, 64], [1, 16]], 0, 0)

    def clear_slots():
        out, a = R("INV", 0, 256), R("BV", 0, 256)
        op("s", out, [a], lambda: g.scalar.activation(out[0], a[0], F.Silu))

    def zeros():
        if "ao" in OPT["rest"] or "c1" in OPT["rest"]:
            act(R("DD", 192, 1216), R("KK", 0, RO), 0.0)
        else:
            dma("y", R("CD", 0, SO), T.cin[:], "ci")
            dma("y", R("CD", SO, SO + 384), T.cin[:, 0:384], "ci")

    def lists_again():
        need("y", "lw")
        for k in "RO":
            dma("y", *loads[k])

    once = {
        "xbv": lambda: fill(R("BV", 0, 256), 4096.0), "xiv": clear_slots,
        "xj0": lambda: ts(R("PJ", 0, 2), R("PI", 0, 2), 4, A.arith_shift_right, 7, A.bitwise_and),
        "xj1": lambda: ts(R("PJ", 2, 3), R("PI", 0, 1), 15, A.bitwise_and),
        "xcc": lambda: cp(R("COL", 0, 3), R("PJ", 0, 3)),
        "xc8": lambda: fill(col(8), -23.5), "xon": lambda: fill(R("ONE", 0, 128), 1.0 / 128), "xta": lambda: fill(R("TAU", 0, 16), 0.0),
        "xm0": lambda: ts(R("M2", 0, 128), R("I2", 0, 128), col(0), A.is_equal, 2.0, A.mult),
        "xm1": lambda: ts(R("M3", 0, 128), R("I2", 0, 128), col(1), A.is_equal),
        "xmx": lambda: tt(R("MX", 0, 128), R("M2", 0, 128), R("M3", 0, 128), A.add),
        "xc4": lambda: ts(col(4), col(2), 0.0, A.is_equal),
        "xc5": lambda: ts(col(5), col(2), 1.0, A.is_equal, -1024.0, A.mult),
        "xc6": lambda: ts(col(6), col(2), 1.0, A.not_equal),
        "xty": lambda: ts(R("TY", 0, SO), R("TY", 0, SO), col(6), A.mult),
        "xtt": lambda: fill(R("TY", 0, SO), 1.0),
        "xn0": lambda: ts(R("M0", 0, 144), R("I1", 0, 144), 0.0, A.is_equal, col(4), A.mult),
        "xn1": lambda: ts(R("M1", 0, 144), R("I1", 0, 144), -1.0, A.is_equal, col(5), A.mult),
        "xn2": lambda: ts(R("M4", 0, 144), R("M0", 0, 144), 0.5, A.mult),
        "xz2": lambda: tt(R("Z2", 0, 144), R("M4", 0, 144), R("M1", 0, 144), A.add),
        "xrh": lambda: ts(R("RH", 0, 128), R("I4", 0, 128), 0.5, A.mult),
        "xhb": lambda: ts(R("HB", 0, 64), R("I3", 0, 64), 2047.0 - 192 - 2048, A.add, 0.5, A.mult),
        "xid": lambda: ts(R("ID", 0, 128), R("I1", 16, 144), 0.0, A.is_equal),
        "xkt": lambda: ts(R("KT", 0, 64), R("I3", 0, 64), col(2), A.add),
        "xcd": lambda: ts(col(13), col(2), 1.0, A.add),
        "xa0": lambda: cp(R("A16", 0, 64), R("RAI", 0, 64)), "xb0": lambda: cp(R("B16", 0, 64), R("RBI", 0, 64)),
        "xa1": lambda: cp(R("A16", 64, 128), R("RAI", 0, 64)), "xb1": lambda: cp(R("B16", 64, 128), R("RBI", 0, 64)),
        "xa2": lambda: cp(R("AB16", 0, 64), R("RAI", 0, 64)), "xb2": lambda: cp(R("AB16", 64, 128), R("RBI", 0, 64)),
        "xp0": lambda: ts(R("PM", 0, 128), R("I4", 0, 128), col(13), A.is_equal, 8192.0, A.mult),
        "xp1": lambda: ts(R("PM", 128, 256), R("I4", 0, 128), col(13), A.is_equal, 8192.0, A.mult),
        "xy0": lambda: ts(R("YE", 0, 32), R("JB", 0, 32), col(2), A.add, float(ET + SO * q), A.add),
        "xy1": lambda: ts(R("YE", 32, 64), R("JB", 0, 32), col(2), A.add, 16.0, A.add),
        "xz1": lambda: ts(R("Z1", 0, 144), R("M0", 0, 144), delta, A.mult),
        "xzp": lambda: ts(R("ZP", 0, 144), R("M0", 0, 144), delta, A.mult),
        "xzm": lambda: ts(R("ZM", 0, 128), R("M0", 16, 144), -delta, A.mult),
        "xzc": lambda: ts(R("ZD", 0, 8), R("M0", 0, 8), delta, A.mult),
        "xzd": lambda: tt(R("ZD", 8, 144), R("ZP", 8, 144), R("ZP", 7, 143), A.subtract),
        "xcp": lambda: fill(R("CAP", 0, RO), 512.0),
        "xtb": lambda: ts(R("TB", 0, 528), R("TAU", 0, 528), 0.125, A.is_lt, 0.125, A.mult),
        "xdd": zeros, "xll": lists_again,
        "xg0": lambda: live_count(0, 256), "xg1": lambda: live_count(256, SO),
        "xt0": lambda: live_bound(0, 256), "xt1": lambda: live_bound(256, SO),
    }
    rounds()

    for sem in SEMAPHORES:
        if total[sem]:
            need("g", sem)
